import numpy as np
import ml_dtypes


def mxq(x, axis, fmt="e4m3"):
    dtype, down = {"e4m3": (ml_dtypes.float8_e4m3fn, 7), "e5m2": (ml_dtypes.float8_e5m2, 14)}[fmt]
    v = np.moveaxis(np.asarray(x, np.float32).astype(ml_dtypes.bfloat16).astype(np.float64), axis, -1)
    blocks = v.reshape(v.shape[:-1] + (-1, 32))
    amax = np.abs(blocks).max(-1, keepdims=True)
    byte = np.maximum(np.where(amax > 0, np.frexp(amax)[1] - 1 + 127, 0) - down, 1)
    scale = np.exp2(byte - 127.0)
    codes = (blocks / scale).astype(np.float32).astype(dtype).astype(np.float64)
    return np.moveaxis((codes * scale).reshape(v.shape), -1, axis)


WIDE = False


def mx_kscale(k):
    if not WIDE:
        return np.ones(k)
    levels = np.array([10, -10, 5, -5, 0])
    if k % 512:
        return np.exp2(np.random.permutation(np.resize(levels, k // 32))).repeat(32)
    a = np.empty((k // 512, 16))
    for p in range(k // 512):
        a[p, :8] = np.random.permutation(np.resize(levels, 8))
        for g in range(8):
            far = levels[np.abs(levels - a[p, g]) >= 10]
            a[p, g + 8] = far[np.random.randint(len(far))]
    return np.exp2(a.ravel()).repeat(32)


def f64(x):
    return np.asarray(x).astype(np.float64)


def striped(idx):
    return np.tile(idx.reshape(-1, 16).T, (8, 1)).astype(np.uint16)


def unstriped(offs):
    return offs[:16].T.reshape(-1).astype(np.int64)


E2M1 = np.array([0.0, 0.5, 1.0, 1.5, 2.0, 3.0, 4.0, 6.0, -0.0, -0.5, -1.0, -1.5, -2.0, -3.0, -4.0, -6.0])


def pack_weight(w, fmt):
    k, n = w.shape
    w = f64(np.asarray(w, np.float32).astype(ml_dtypes.bfloat16)).reshape(k // 32, 32, n)
    amax = np.abs(w).max(1)
    if fmt == "e4m3":
        byte = np.frexp(amax)[1] - 1 + 127 - 7
    else:
        mant, ex = np.frexp(amax / 6.0)
        byte = np.where(mant > 0.5, ex, ex - 1) + 127
    byte = np.clip(np.where(amax > 0, byte, 1), 1, 254)
    scaled = (w * np.exp2(127.0 - byte)[:, None, :]).reshape(k, n).astype(np.float32)
    by_word = np.ascontiguousarray(scaled.reshape(k // 512, 128, 4, n).transpose(0, 1, 3, 2))
    if fmt == "e4m3":
        words = by_word.astype(ml_dtypes.float8_e4m3fn).view(np.uint8)
    else:
        c = by_word.astype(ml_dtypes.float4_e2m1fn).view(np.uint8) & 0xF
        words = (c[..., 0::2] | (c[..., 1::2] << 4)).reshape(k // 512, 128, 2 * n)
    return np.ascontiguousarray(words), np.ascontiguousarray(byte.astype(np.uint8).reshape(k // 512, 16, n))


def unpack_weight(words, scales, fmt):
    g, _, n = scales.shape
    words = np.ascontiguousarray(words).reshape(g, 128, n, -1)
    if fmt == "e4m3":
        vals = words.view(ml_dtypes.float8_e4m3fn).astype(np.float64)
    else:
        nib = np.empty((g, 128, n, 4), np.uint8)
        nib[..., 0::2] = words & 0xF
        nib[..., 1::2] = words >> 4
        vals = E2M1[nib]
    vals = vals * np.repeat(np.exp2(scales.astype(np.float64) - 127.0), 8, axis=1)[..., None]
    return vals.transpose(0, 1, 3, 2).reshape(g * 512, n)


def gelu(v):
    return 0.5 * v * (1.0 + np.tanh(np.sqrt(2.0 / np.pi) * (v + 0.044715 * v**3)))


def often(T, S):
    return np.random.permutation(T)[(T * np.random.uniform(0, 1, S) ** 4).astype(np.int64)]


def bf(x):
    return np.asarray(x, np.float32).astype(ml_dtypes.bfloat16)


def planes(Y):
    n, m = Y.shape
    b = f64(bf(Y)).reshape(n // 32, 32, m)
    amax = np.abs(b).max(1)
    byte = np.clip(np.where(amax > 0, np.frexp(amax)[1] - 1 + 127 - 7, 1), 1, 254)
    codes = (b * np.exp2(127.0 - byte)[:, None, :]).reshape(n, m).astype(np.float32).astype(ml_dtypes.float8_e4m3fn).view(np.uint8)
    words = codes.reshape(n // 512, 128, 4, m).transpose(0, 1, 3, 2)
    return np.ascontiguousarray(words), np.ascontiguousarray(byte.astype(np.uint8).reshape(n // 512, 16, m))


K, T, S, K2, T2, P, H, N = 512, 2048, 1024, 1024, 2048, 512, 1536, 512

def setup_inputs():
    n = np.random.standard_normal
    s, s2 = mx_kscale(K)[:, None], mx_kscale(K2)[:, None]
    u = mx_kscale(H)[:, None]
    tab_words, tab_scales = pack_weight(n((K, T)) * s, "e4m3")
    tab2_words, tab2_scales = pack_weight(n((K2, T2)) * s2, "e4m3")
    w1_words, w1_scales = pack_weight(n((K, H)) / np.sqrt(K) / s * u.T, "e2m1")
    w4_words, w4_scales = pack_weight(n((K2, N)) / np.sqrt(K2) / s2, "e4m3")
    return {
        "tab_words": tab_words, "tab_scales": tab_scales,
        "offs": striped(np.random.permutation(T)[:S]),
        "pos1": striped(often(S, P)),
        "tab2_words": tab2_words, "tab2_scales": tab2_scales,
        "offs2": striped(np.random.permutation(T2)[:P]),
        "w1_words": w1_words, "w1_scales": w1_scales,
        "b1": (0.5 * n(H) * u[:, 0]).astype(np.float32),
        "w2": (n((K2, H)) / np.sqrt(K2) / s2).astype(np.float32),
        "w3": (n((H, N)) / np.sqrt(H) / u).astype(np.float32),
        "w4_words": w4_words, "w4_scales": w4_scales,
        "by": (0.5 * n(N)).astype(np.float32),
        "gy": (0.7 * np.exp(0.8 * n(N))).astype(np.float32),
    }

def reference(tab_words, tab_scales, offs, pos1, tab2_words, tab2_scales, offs2, w1_words, w1_scales,
              b1, w2, w3, w4_words, w4_scales, by, gy):
    v = unpack_weight(tab_words, tab_scales, "e4m3")[:, unstriped(offs)]
    v2 = unpack_weight(tab2_words, tab2_scales, "e4m3")[:, unstriped(offs2)]
    W1 = unpack_weight(w1_words, w1_scales, "e2m1")
    W4 = unpack_weight(w4_words, w4_scales, "e4m3")
    h = (W1.T @ v) + f64(b1)[:, None]
    a = h[:, unstriped(pos1)]
    b = mxq(f64(w2), 0, "e4m3").T @ v2
    z = mxq(a * b, 0, "e4m3")
    o = mxq(f64(w3), 0, "e4m3").T @ z + W4.T @ v2
    y = f64(gy)[:, None] * (o + f64(by)[:, None])
    words, scales = planes(y)
    return y, words, scales

@@ -1,0 +1,300 @@
+from contextlib import ExitStack
+
+import concourse.mybir as mybir
+
+K, T, S, K2, T2, M, H, N = 512, 2048, 1024, 1024, 2048, 512, 1536, 512
+FLOPS = 2 * (K * H * S + K2 * H * M + H * N * M + K2 * N * M)
+
+F32 = mybir.dt.float32
+BF16 = mybir.dt.bfloat16
+I32 = mybir.dt.int32
+U32 = mybir.dt.uint32
+U16 = mybir.dt.uint16
+U8 = mybir.dt.uint8
+FP8X4 = mybir.dt.float8_e4m3fn_x4
+FP4X4 = mybir.dt.float4_e2m1fn_x4
+IDENT = mybir.ActivationFunctionType.Identity
+MULT = mybir.AluOpType.mult
+ADD = mybir.AluOpType.add
+
+P = 128
+G = H // 512
+A = K2 // 512
+Q = M // P
+
+
+def tile_list_inlining_adviser_kernel(
+    tc, tab_words, tab_scales, offs, pos1, tab2_words, tab2_scales, offs2, w1_words, w1_scales,
+    b1, w2, w3, w4_words, w4_scales, by, gy, out_0, out_1, out_2,
+):
+    nc = tc.nc
+    with ExitStack() as ctx:
+        keep = ctx.enter_context(tc.tile_pool(name="keep", bufs=1))
+        stream = ctx.enter_context(tc.tile_pool(name="stream", bufs=5))
+        bf_pool = ctx.enter_context(tc.tile_pool(name="bf", bufs=3))
+        work = ctx.enter_context(tc.tile_pool(name="work", bufs=2))
+        acc_pool = ctx.enter_context(tc.psum_pool(name="acc", bufs=4))
+        b_pool = ctx.enter_context(tc.psum_pool(name="bps", bufs=4))
+
+        def held(shape, dtype, name):
+            return keep.tile(shape, dtype, name=name, align_bytes=64)
+
+        def staged(shape, dtype, name):
+            return stream.tile(shape, dtype, name=name, tag="stream", align_bytes=64)
+
+        def load_scale_rows(queue, plane, scales):
+            passes = scales.shape[0]
+            for quad in range(4):
+                queue.dma_start(
+                    out=plane[32 * quad : 32 * quad + 4 * passes, :].bitcast(I32),
+                    in_=scales[:, 4 * quad : 4 * quad + 4, :].bitcast(I32),
+                )
+
+        def words_view(words_pass):
+            return words_pass.rearrange("p t i -> p (t i)").bitcast(I32)
+
+        offs_sb = held([P, S // 16], U16, "offs_sb")
+        offs2_sb = held([P, M // 16], U16, "offs2_sb")
+        pos_sb = held([P, M // 16], U16, "pos_sb")
+        w1_s = staged([P, H], U8, "w1_s")
+        tab_s = staged([P, T], U8, "tab_s")
+        tab2_s = staged([P, T2], U8, "tab2_s")
+        w1_w = staged([P, H // 2], I32, "w1_w")
+        tab_w = staged([P, T], I32, "tab_w")
+        tab2_w = [staged([P, T2], I32, "tab2_w%d" % a) for a in range(A)]
+        w1_sd = held([P, H], U8, "w1_sd")
+        nc.gpsimd.memset(tab_s[:].bitcast(I32), 0)
+        for plane in (w1_sd, tab2_s):
+            nc.vector.memset(plane[:].bitcast(I32), 0)
+
+        bias1 = held([P, G, 16], F32, "bias1")
+        by_sb = held([P, 4], F32, "by_sb")
+        gy_sb = held([P, 4], F32, "gy_sb")
+        gby = held([P, 4], F32, "gby")
+
+        nc.sync.dma_start(offs_sb[:], offs)
+        load_scale_rows(nc.sync, w1_s, w1_scales)
+        load_scale_rows(nc.sync, tab_s, tab_scales)
+        nc.sync.dma_start(out=tab_w[:], in_=words_view(tab_words[0]))
+        nc.sync.dma_start(out=w1_w[:], in_=w1_words[0].bitcast(I32))
+        nc.sync.dma_start(offs2_sb[:], offs2)
+        b1_view = b1.rearrange("(g u k) -> u g k", g=G, k=16)
+        for s in range(4):
+            nc.gpsimd.dma_start(out=bias1[s:P:4, :, 0:13], in_=b1_view[:, :, s : s + 13])
+        nc.sync.dma_start(out=tab2_w[0][:], in_=words_view(tab2_words[0]))
+        nc.sync.dma_start(out=tab2_w[1][:], in_=words_view(tab2_words[1]))
+        load_scale_rows(nc.sync, tab2_s, tab2_scales)
+        nc.sync.dma_start(pos_sb[:], pos1)
+        nc.gpsimd.dma_start(out=by_sb[:], in_=by.rearrange("(p t) -> p t", t=4))
+        nc.gpsimd.dma_start(out=gy_sb[:], in_=gy.rearrange("(p t) -> p t", t=4))
+        nc.gpsimd.tensor_tensor(gby[:], gy_sb[:], by_sb[:], MULT)
+
+        def load_w2(g, a):
+            raw = staged([P, 4, 512], F32, "raw")
+            rows = w2[512 * a : 512 * (a + 1), 512 * g : 512 * (g + 1)]
+            nc.sync.dma_start(out=raw[:], in_=rows.rearrange("(p j) c -> p j c", j=4))
+            return raw
+
+        def load_w3(g):
+            raw = staged([P, 4, 512], F32, "raw")
+            rows = w3[512 * g : 512 * (g + 1), :].rearrange("(u j s) n -> s u j n", j=4, s=4)
+            for s in range(4):
+                nc.sync.dma_start(out=raw[s:P:4, :, :], in_=rows[s])
+            return raw
+
+        def round_w2(raw):
+            bf = bf_pool.tile([P, 2048], BF16, name="bf", align_bytes=64)
+            nc.scalar.copy(
+                out=bf[:].rearrange("p (t u s j) -> p t u j s", t=4, s=4, j=4),
+                in_=raw[:].rearrange("p j (u t s) -> p t u j s", t=4, s=4),
+            )
+            return bf
+
+        def round_w3(raw):
+            bf = bf_pool.tile([P, 2048], BF16, name="bf3", align_bytes=64)
+            dealt = bf[:].rearrange("p (t m j) -> p m t j", t=4, j=4)
+            source = raw[:].rearrange("p j (m t) -> p m t j", t=4)
+            for c in range(4):
+                nc.gpsimd.tensor_scalar(
+                    dealt[:, 32 * c : 32 * (c + 1)], source[:, 32 * c : 32 * (c + 1)],
+                    1.0, 0.0, MULT, ADD,
+                )
+            return bf
+
+        def quantise(bf, name):
+            codes = held([P, 512], U32, name + "_c")
+            scales = held([P, 512], U8, name + "_s")
+            nc.vector.quantize_mx(out=codes[:].bitcast(FP8X4), scales=scales[:], in_=bf[:])
+            return codes, scales
+
+        v_s = [held([P, 512], U8, "v_s%d" % c) for c in range(2)]
+        v_w = [held([P, 512], U32, "v_w%d" % c) for c in range(2)]
+        w1_wd = held([P, H // 2], I32, "w1_wd")
+        nc.vector.tensor_copy(v_w[0][:], tab_w[:].bitcast(U32).indirect(offs_sb[:, 0:32]))
+        nc.vector.tensor_copy(v_s[0][:], tab_s[:].indirect(offs_sb[:, 0:32]))
+        nc.vector.tensor_copy(
+            out=w1_wd[:].rearrange("p (g t u h) -> p g t u h", g=G, t=4, h=2),
+            in_=w1_w[:].rearrange("p (g u t h) -> p g t u h", g=G, t=4, h=2),
+        )
+        for quad in range(4):
+            rows = slice(32 * quad, 32 * quad + 4)
+            nc.vector.tensor_copy(
+                out=w1_sd[rows, :].bitcast(I32).rearrange("p (g t u i) -> p g u t i", g=G, t=4, i=4),
+                in_=w1_s[rows, :].bitcast(I32).rearrange("p (g u i t) -> p g u t i", g=G, t=4, i=4),
+            )
+        nc.vector.tensor_copy(v_w[1][:], tab_w[:].bitcast(U32).indirect(offs_sb[:, 32:64]))
+        nc.vector.tensor_copy(v_s[1][:], tab_s[:].indirect(offs_sb[:, 32:64]))
+
+        v2_s = held([P, M], U8, "v2_s")
+        v2_w = [held([P, M], U32, "v2_w%d" % a) for a in range(A)]
+        nc.vector.tensor_copy(v2_s[:], tab2_s[:].indirect(offs2_sb[:]))
+        for a in range(A):
+            nc.vector.tensor_copy(v2_w[a][:], tab2_w[a][:].bitcast(U32).indirect(offs2_sb[:]))
+
+        h = [held([P, S], F32, "h%d" % i) for i in range(G * 4)]
+
+        def scope_results(g):
+            for t in range(4):
+                i = 4 * g + t
+                for c in range(2):
+                    bank = acc_pool.tile([P, 512], F32, name="acc")
+                    nc.tensor.matmul_mx(
+                        out=bank[:],
+                        lhsT=w1_wd[:, 64 * i : 64 * (i + 1)].bitcast(U8).bitcast(FP4X4),
+                        lhsT_scale=w1_sd[:, P * i : P * (i + 1)],
+                        rhs=v_w[c][:].bitcast(FP8X4),
+                        rhs_scale=v_s[c][:],
+                        start=True,
+                        stop=True,
+                    )
+                    nc.scalar.activation(
+                        h[i][:, 512 * c : 512 * (c + 1)], bank[:], IDENT, bias=bias1[:, g, 4 * t : 4 * t + 1]
+                    )
+
+        def pick_scopes(g):
+            picked = held([P, 4, M], F32, "picked%d" % g)
+            for t in range(4):
+                nc.vector.tensor_copy(picked[:, t, :], h[4 * g + t][:].indirect(pos_sb[:]))
+            return picked
+
+        def call_projection(w2q, q):
+            bank = b_pool.tile([P, 4, P], F32, name="bbank")
+            cols = slice(P * q, P * (q + 1))
+            for t in range(4):
+                for a in range(A):
+                    codes, scales = w2q[a]
+                    nc.tensor.matmul_mx(
+                        out=bank[:, t, :],
+                        lhsT=codes[:, P * t : P * (t + 1)].bitcast(FP8X4),
+                        lhsT_scale=scales[:, P * t : P * (t + 1)],
+                        rhs=v2_w[a][:, cols].bitcast(FP8X4),
+                        rhs_scale=v2_s[4 * a : P, cols],
+                        start=(a == 0),
+                        stop=(a == A - 1),
+                    )
+            return bank
+
+        def multiply(zb, picked, bank):
+            nc.vector.tensor_tensor(
+                zb.rearrange("p (m i t) -> p m t i", i=2, t=4),
+                picked.rearrange("p t (m i) -> p m t i", i=2),
+                bank[:].rearrange("p t (m i) -> p m t i", i=2),
+                MULT,
+            )
+
+        z_c = [held([P, M], U32, "z_c%d" % g) for g in range(G)]
+        z_s = [held([P, M], U8, "z_s%d" % g) for g in range(G)]
+
+        def product(g, w2q, picked):
+            zb = work.tile([P, 4 * M], BF16, name="zb", align_bytes=64)
+            for q in range(Q):
+                bank = call_projection(w2q, q)
+                multiply(zb[:, 512 * q : 512 * (q + 1)], picked[:, :, P * q : P * (q + 1)], bank)
+            nc.vector.quantize_mx(out=z_c[g][:].bitcast(FP8X4), scales=z_s[g][:], in_=zb[:])
+
+        def prepare_w2(g):
+            raws = [load_w2(g, a) for a in range(A)]
+            return [quantise(round_w2(raws[a]), "w2_%d%d" % (g, a)) for a in range(A)]
+
+        picked = []
+        for g in range(G):
+            scope_results(g)
+            picked.append(pick_scopes(g))
+        w3q = [quantise(round_w3(load_w3(g)), "w3_%d" % g) for g in range(G)]
+        w2q = [prepare_w2(0)]
+
+        w4_w = staged([P, A, N], I32, "w4_w")
+        w4_s = staged([P, N], U8, "w4_s")
+        nc.gpsimd.memset(w4_s[:].bitcast(I32), 0)
+        nc.sync.dma_start(out=w4_w[:], in_=w4_words.rearrange("a p c i -> p a (c i)").bitcast(I32))
+        load_scale_rows(nc.sync, w4_s, w4_scales)
+        w4_wd = held([P, A, N], I32, "w4_wd")
+        w4_sd = held([P, N], U8, "w4_sd")
+        nc.vector.tensor_copy(
+            out=w4_wd[:].rearrange("p a (t m i) -> p a m t i", t=4, i=4),
+            in_=w4_w[:].rearrange("p a (m i t) -> p a m t i", t=4, i=4),
+        )
+        nc.vector.tensor_copy(
+            out=w4_sd[:].rearrange("p (t m i) -> p m t i", t=4, i=16),
+            in_=w4_s[:].rearrange("p (m i t) -> p m t i", t=4, i=16),
+        )
+        for g in range(G - 1):
+            product(g, w2q[g], picked[g])
+            w2q.append(prepare_w2(g + 1))
+
+        banks = [acc_pool.tile([P, 4, P], F32, name="acc") for q in range(Q)]
+
+        def out_passes(q, codes, scales, row, z_codes, z_scales, first, last):
+            cols = slice(P * q, P * (q + 1))
+            for t in range(4):
+                nc.tensor.matmul_mx(
+                    out=banks[q][:, t, :],
+                    lhsT=codes[:, P * t : P * (t + 1)].bitcast(FP8X4),
+                    lhsT_scale=scales[row:P, P * t : P * (t + 1)],
+                    rhs=z_codes[:, cols].bitcast(FP8X4),
+                    rhs_scale=z_scales[row:P, cols],
+                    start=(first and t == 0),
+                    stop=(last and t == 3),
+                )
+
+        for q in range(Q):
+            for a in range(A):
+                out_passes(q, w4_wd[:, a, :], w4_sd, 4 * a, v2_w[a], v2_s, a == 0, False)
+        for g in range(G - 1):
+            for q in range(Q):
+                out_passes(q, w3q[g][0], w3q[g][1], 0, z_c[g], z_s[g], False, False)
+
+        y_c = held([P, M], U32, "y_c")
+        y_s = held([P, M], U8, "y_s")
+        y_rows = out_0.rearrange("(p t) m -> p t m", t=4)
+        last = G - 1
+        for q in range(Q):
+            cols = slice(P * q, P * (q + 1))
+            bank = call_projection(w2q[last], q)
+            zb = work.tile([P, 512], BF16, name="zb", align_bytes=64)
+            multiply(zb[:], picked[last][:, :, cols], bank)
+            nc.vector.quantize_mx(
+                out=z_c[last][:, cols].bitcast(FP8X4), scales=z_s[last][:, cols], in_=zb[:]
+            )
+            out_passes(q, w3q[last][0], w3q[last][1], 0, z_c[last], z_s[last], False, True)
+            y = held([P, 4, P], F32, "y%d" % q)
+            for t in range(4):
+                nc.scalar.activation(
+                    y[:, t, :], banks[q][:, t, :], IDENT,
+                    bias=gby[:, t : t + 1], scale=gy_sb[:, t : t + 1],
+                )
+            nc.sync.dma_start(out=y_rows[:, :, cols], in_=y[:])
+            yb = work.tile([P, 512], BF16, name="yb", align_bytes=64)
+            nc.scalar.copy(
+                out=yb[:].rearrange("p (m i t) -> p m t i", i=2, t=4),
+                in_=y[:].rearrange("p t (m i) -> p m t i", i=2),
+            )
+            nc.vector.quantize_mx(out=y_c[:, cols].bitcast(FP8X4), scales=y_s[:, cols], in_=yb[:])
+            nc.sync.dma_start(
+                out=words_view(out_1[0])[:, cols], in_=y_c[:, cols].bitcast(I32)
+            )
+        for quad in range(4):
+            nc.sync.dma_start(
+                out=out_2[0, 4 * quad : 4 * quad + 4, :].bitcast(I32),
+                in_=y_s[32 * quad : 32 * quad + 4, :].bitcast(I32),
+            )

@@ -15,7 +15,6 @@ FP8X4 = mybir.dt.float8_e4m3fn_x4
 FP4X4 = mybir.dt.float4_e2m1fn_x4
 IDENT = mybir.ActivationFunctionType.Identity
 MULT = mybir.AluOpType.mult
-ADD = mybir.AluOpType.add
 
 P = 128
 G = H // 512
@@ -31,10 +30,13 @@ def tile_list_inlining_adviser_kernel(
     with ExitStack() as ctx:
         keep = ctx.enter_context(tc.tile_pool(name="keep", bufs=1))
         stream = ctx.enter_context(tc.tile_pool(name="stream", bufs=5))
-        bf_pool = ctx.enter_context(tc.tile_pool(name="bf", bufs=3))
+        bf_pool = ctx.enter_context(tc.tile_pool(name="bf", bufs=4))
+        late = ctx.enter_context(tc.tile_pool(name="late", bufs=4))
         work = ctx.enter_context(tc.tile_pool(name="work", bufs=2))
-        acc_pool = ctx.enter_context(tc.psum_pool(name="acc", bufs=4))
-        b_pool = ctx.enter_context(tc.psum_pool(name="bps", bufs=4))
+        psum = ctx.enter_context(tc.psum_pool(name="psum", bufs=1))
+
+        def psum_bank(shape, index):
+            return psum.tile(shape, F32, name="bank%d" % index)
 
         def held(shape, dtype, name):
             return keep.tile(shape, dtype, name=name, align_bytes=64)
@@ -56,15 +58,14 @@ def tile_list_inlining_adviser_kernel(
         offs_sb = held([P, S // 16], U16, "offs_sb")
         offs2_sb = held([P, M // 16], U16, "offs2_sb")
         pos_sb = held([P, M // 16], U16, "pos_sb")
+        w1_w = staged([P, H // 2], I32, "w1_w")
         w1_s = staged([P, H], U8, "w1_s")
+        tab_w = staged([P, T], I32, "tab_w")
         tab_s = staged([P, T], U8, "tab_s")
         tab2_s = staged([P, T2], U8, "tab2_s")
-        w1_w = staged([P, H // 2], I32, "w1_w")
-        tab_w = staged([P, T], I32, "tab_w")
         tab2_w = [staged([P, T2], I32, "tab2_w%d" % a) for a in range(A)]
-        w1_sd = held([P, H], U8, "w1_sd")
         nc.gpsimd.memset(tab_s[:].bitcast(I32), 0)
-        for plane in (w1_sd, tab2_s):
+        for plane in (w1_s, tab2_s):
             nc.vector.memset(plane[:].bitcast(I32), 0)
 
         bias1 = held([P, G, 16], F32, "bias1")
@@ -73,24 +74,27 @@ def tile_list_inlining_adviser_kernel(
         gby = held([P, 4], F32, "gby")
 
         nc.sync.dma_start(offs_sb[:], offs)
-        load_scale_rows(nc.sync, w1_s, w1_scales)
         load_scale_rows(nc.sync, tab_s, tab_scales)
         nc.sync.dma_start(out=tab_w[:], in_=words_view(tab_words[0]))
         nc.sync.dma_start(out=w1_w[:], in_=w1_words[0].bitcast(I32))
         nc.sync.dma_start(offs2_sb[:], offs2)
+        load_scale_rows(nc.sync, w1_s, w1_scales)
+        nc.gpsimd.dma_start(out=by_sb[:], in_=by.rearrange("(p t) -> p t", t=4))
+        nc.gpsimd.dma_start(out=gy_sb[:], in_=gy.rearrange("(p t) -> p t", t=4))
         b1_view = b1.rearrange("(g u k) -> u g k", g=G, k=16)
         for s in range(4):
             nc.gpsimd.dma_start(out=bias1[s:P:4, :, 0:13], in_=b1_view[:, :, s : s + 13])
-        nc.sync.dma_start(out=tab2_w[0][:], in_=words_view(tab2_words[0]))
-        nc.sync.dma_start(out=tab2_w[1][:], in_=words_view(tab2_words[1]))
+        for a in range(A):
+            nc.sync.dma_start(out=tab2_w[a][:], in_=words_view(tab2_words[a]))
         load_scale_rows(nc.sync, tab2_s, tab2_scales)
         nc.sync.dma_start(pos_sb[:], pos1)
-        nc.gpsimd.dma_start(out=by_sb[:], in_=by.rearrange("(p t) -> p t", t=4))
-        nc.gpsimd.dma_start(out=gy_sb[:], in_=gy.rearrange("(p t) -> p t", t=4))
-        nc.gpsimd.tensor_tensor(gby[:], gy_sb[:], by_sb[:], MULT)
+        for t in range(4):
+            nc.scalar.activation(
+                gby[:, t : t + 1], by_sb[:, t : t + 1], IDENT, scale=gy_sb[:, t : t + 1]
+            )
 
         def load_w2(g, a):
-            raw = staged([P, 4, 512], F32, "raw")
+            raw = late.tile([P, 4, 512], F32, name="raw2")
             rows = w2[512 * a : 512 * (a + 1), 512 * g : 512 * (g + 1)]
             nc.sync.dma_start(out=raw[:], in_=rows.rearrange("(p j) c -> p j c", j=4))
             return raw
@@ -110,15 +114,12 @@ def tile_list_inlining_adviser_kernel(
             )
             return bf
 
-        def round_w3(raw):
-            bf = bf_pool.tile([P, 2048], BF16, name="bf3", align_bytes=64)
-            dealt = bf[:].rearrange("p (t m j) -> p m t j", t=4, j=4)
-            source = raw[:].rearrange("p j (m t) -> p m t j", t=4)
-            for c in range(4):
-                nc.gpsimd.tensor_scalar(
-                    dealt[:, 32 * c : 32 * (c + 1)], source[:, 32 * c : 32 * (c + 1)],
-                    1.0, 0.0, MULT, ADD,
-                )
+        def round_w3(raw, copy):
+            bf = bf_pool.tile([P, 2048], BF16, name="bf", align_bytes=64)
+            copy(
+                out=bf[:].rearrange("p (t m j) -> p m t j", t=4, j=4),
+                in_=raw[:].rearrange("p j (m t) -> p m t j", t=4),
+            )
             return bf
 
         def quantise(bf, name):
@@ -130,20 +131,23 @@ def tile_list_inlining_adviser_kernel(
         v_s = [held([P, 512], U8, "v_s%d" % c) for c in range(2)]
         v_w = [held([P, 512], U32, "v_w%d" % c) for c in range(2)]
         w1_wd = held([P, H // 2], I32, "w1_wd")
-        nc.vector.tensor_copy(v_w[0][:], tab_w[:].bitcast(U32).indirect(offs_sb[:, 0:32]))
-        nc.vector.tensor_copy(v_s[0][:], tab_s[:].indirect(offs_sb[:, 0:32]))
+        w1_sd = held([P, H], U8, "w1_sd")
+
+        def pick_scope_columns(c):
+            entries = offs_sb[:, 32 * c : 32 * (c + 1)]
+            nc.vector.tensor_copy(v_w[c][:], tab_w[:].bitcast(U32).indirect(entries))
+            nc.vector.tensor_copy(v_s[c][:], tab_s[:].indirect(entries))
+
+        pick_scope_columns(0)
         nc.vector.tensor_copy(
             out=w1_wd[:].rearrange("p (g t u h) -> p g t u h", g=G, t=4, h=2),
             in_=w1_w[:].rearrange("p (g u t h) -> p g t u h", g=G, t=4, h=2),
         )
-        for quad in range(4):
-            rows = slice(32 * quad, 32 * quad + 4)
-            nc.vector.tensor_copy(
-                out=w1_sd[rows, :].bitcast(I32).rearrange("p (g t u i) -> p g u t i", g=G, t=4, i=4),
-                in_=w1_s[rows, :].bitcast(I32).rearrange("p (g u i t) -> p g u t i", g=G, t=4, i=4),
-            )
-        nc.vector.tensor_copy(v_w[1][:], tab_w[:].bitcast(U32).indirect(offs_sb[:, 32:64]))
-        nc.vector.tensor_copy(v_s[1][:], tab_s[:].indirect(offs_sb[:, 32:64]))
+        nc.vector.tensor_copy(
+            out=w1_sd[:].bitcast(I32).rearrange("p (g t u i) -> p g u t i", g=G, t=4, i=4),
+            in_=w1_s[:].bitcast(I32).rearrange("p (g u i t) -> p g u t i", g=G, t=4, i=4),
+        )
+        pick_scope_columns(1)
 
         v2_s = held([P, M], U8, "v2_s")
         v2_w = [held([P, M], U32, "v2_w%d" % a) for a in range(A)]
@@ -157,7 +161,7 @@ def tile_list_inlining_adviser_kernel(
             for t in range(4):
                 i = 4 * g + t
                 for c in range(2):
-                    bank = acc_pool.tile([P, 512], F32, name="acc")
+                    bank = psum_bank([P, 512], (2 * i + c) % 8)
                     nc.tensor.matmul_mx(
                         out=bank[:],
                         lhsT=w1_wd[:, 64 * i : 64 * (i + 1)].bitcast(U8).bitcast(FP4X4),
@@ -177,8 +181,8 @@ def tile_list_inlining_adviser_kernel(
                 nc.vector.tensor_copy(picked[:, t, :], h[4 * g + t][:].indirect(pos_sb[:]))
             return picked
 
-        def call_projection(w2q, q):
-            bank = b_pool.tile([P, 4, P], F32, name="bbank")
+        def call_projection(w2q, q, index):
+            bank = psum_bank([P, 4, P], index)
             cols = slice(P * q, P * (q + 1))
             for t in range(4):
                 for a in range(A):
@@ -202,16 +206,6 @@ def tile_list_inlining_adviser_kernel(
                 MULT,
             )
 
-        z_c = [held([P, M], U32, "z_c%d" % g) for g in range(G)]
-        z_s = [held([P, M], U8, "z_s%d" % g) for g in range(G)]
-
-        def product(g, w2q, picked):
-            zb = work.tile([P, 4 * M], BF16, name="zb", align_bytes=64)
-            for q in range(Q):
-                bank = call_projection(w2q, q)
-                multiply(zb[:, 512 * q : 512 * (q + 1)], picked[:, :, P * q : P * (q + 1)], bank)
-            nc.vector.quantize_mx(out=z_c[g][:].bitcast(FP8X4), scales=z_s[g][:], in_=zb[:])
-
         def prepare_w2(g):
             raws = [load_w2(g, a) for a in range(A)]
             return [quantise(round_w2(raws[a]), "w2_%d%d" % (g, a)) for a in range(A)]
@@ -220,12 +214,9 @@ def tile_list_inlining_adviser_kernel(
         for g in range(G):
             scope_results(g)
             picked.append(pick_scopes(g))
-        w3q = [quantise(round_w3(load_w3(g)), "w3_%d" % g) for g in range(G)]
-        w2q = [prepare_w2(0)]
-
         w4_w = staged([P, A, N], I32, "w4_w")
-        w4_s = staged([P, N], U8, "w4_s")
-        nc.gpsimd.memset(w4_s[:].bitcast(I32), 0)
+        w4_s = held([P, N], U8, "w4_s")
+        nc.vector.memset(w4_s[:].bitcast(I32), 0)
         nc.sync.dma_start(out=w4_w[:], in_=w4_words.rearrange("a p c i -> p a (c i)").bitcast(I32))
         load_scale_rows(nc.sync, w4_s, w4_scales)
         w4_wd = held([P, A, N], I32, "w4_wd")
@@ -238,45 +229,59 @@ def tile_list_inlining_adviser_kernel(
             out=w4_sd[:].rearrange("p (t m i) -> p m t i", t=4, i=16),
             in_=w4_s[:].rearrange("p (m i t) -> p m t i", t=4, i=16),
         )
-        for g in range(G - 1):
-            product(g, w2q[g], picked[g])
-            w2q.append(prepare_w2(g + 1))
+        w3q = [
+            quantise(round_w3(load_w3(g), nc.vector.tensor_copy), "w3_%d" % g) for g in range(G - 1)
+        ]
 
-        banks = [acc_pool.tile([P, 4, P], F32, name="acc") for q in range(Q)]
+        z_c = [held([P, M], U32, "z_c%d" % g) for g in range(G)]
+        z_s = [held([P, M], U8, "z_s%d" % g) for g in range(G)]
+        last = G - 1
+        for g in range(last):
+            w2q = prepare_w2(g)
+            zb = work.tile([P, 4 * M], BF16, name="zb", align_bytes=64)
+            for q in range(Q):
+                bank = call_projection(w2q, q, q)
+                multiply(zb[:, 512 * q : 512 * (q + 1)], picked[g][:, :, P * q : P * (q + 1)], bank)
+            nc.vector.quantize_mx(out=z_c[g][:].bitcast(FP8X4), scales=z_s[g][:], in_=zb[:])
+        w2q = prepare_w2(last)
+        w3q.append(quantise(round_w3(load_w3(last), nc.scalar.copy), "w3_%d" % last))
+        b_banks = [call_projection(w2q, q, q) for q in range(Q)]
 
-        def out_passes(q, codes, scales, row, z_codes, z_scales, first, last):
+        banks = [psum_bank([P, 4, P], Q + q) for q in range(Q)]
+
+        def out_passes(q, codes, scales, row, moving, moving_scales, first, final):
             cols = slice(P * q, P * (q + 1))
             for t in range(4):
                 nc.tensor.matmul_mx(
                     out=banks[q][:, t, :],
                     lhsT=codes[:, P * t : P * (t + 1)].bitcast(FP8X4),
                     lhsT_scale=scales[row:P, P * t : P * (t + 1)],
-                    rhs=z_codes[:, cols].bitcast(FP8X4),
-                    rhs_scale=z_scales[row:P, cols],
+                    rhs=moving[:, cols].bitcast(FP8X4),
+                    rhs_scale=moving_scales[row:P, cols],
                     start=(first and t == 0),
-                    stop=(last and t == 3),
+                    stop=(final and t == 3),
                 )
 
         for q in range(Q):
             for a in range(A):
                 out_passes(q, w4_wd[:, a, :], w4_sd, 4 * a, v2_w[a], v2_s, a == 0, False)
-        for g in range(G - 1):
+        for g in range(last):
             for q in range(Q):
                 out_passes(q, w3q[g][0], w3q[g][1], 0, z_c[g], z_s[g], False, False)
 
         y_c = held([P, M], U32, "y_c")
         y_s = held([P, M], U8, "y_s")
         y_rows = out_0.rearrange("(p t) m -> p t m", t=4)
-        last = G - 1
         for q in range(Q):
             cols = slice(P * q, P * (q + 1))
-            bank = call_projection(w2q[last], q)
-            zb = work.tile([P, 512], BF16, name="zb", align_bytes=64)
-            multiply(zb[:], picked[last][:, :, cols], bank)
+            zq = work.tile([P, 512], BF16, name="zq", align_bytes=64)
+            multiply(zq[:], picked[last][:, :, cols], b_banks[q])
             nc.vector.quantize_mx(
-                out=z_c[last][:, cols].bitcast(FP8X4), scales=z_s[last][:, cols], in_=zb[:]
+                out=z_c[last][:, cols].bitcast(FP8X4), scales=z_s[last][:, cols], in_=zq[:]
             )
             out_passes(q, w3q[last][0], w3q[last][1], 0, z_c[last], z_s[last], False, True)
+        for q in range(Q):
+            cols = slice(P * q, P * (q + 1))
             y = held([P, 4, P], F32, "y%d" % q)
             for t in range(4):
                 nc.scalar.activation(
@@ -285,14 +290,12 @@ def tile_list_inlining_adviser_kernel(
                 )
             nc.sync.dma_start(out=y_rows[:, :, cols], in_=y[:])
             yb = work.tile([P, 512], BF16, name="yb", align_bytes=64)
-            nc.scalar.copy(
+            nc.vector.tensor_copy(
                 out=yb[:].rearrange("p (m i t) -> p m t i", i=2, t=4),
                 in_=y[:].rearrange("p t (m i) -> p m t i", i=2),
             )
             nc.vector.quantize_mx(out=y_c[:, cols].bitcast(FP8X4), scales=y_s[:, cols], in_=yb[:])
-            nc.sync.dma_start(
-                out=words_view(out_1[0])[:, cols], in_=y_c[:, cols].bitcast(I32)
-            )
+            nc.sync.dma_start(out=words_view(out_1[0])[:, cols], in_=y_c[:, cols].bitcast(I32))
         for quad in range(4):
             nc.sync.dma_start(
                 out=out_2[0, 4 * quad : 4 * quad + 4, :].bitcast(I32),

@@ -15,6 +15,7 @@ FP8X4 = mybir.dt.float8_e4m3fn_x4
 FP4X4 = mybir.dt.float4_e2m1fn_x4
 IDENT = mybir.ActivationFunctionType.Identity
 MULT = mybir.AluOpType.mult
+ADD = mybir.AluOpType.add
 
 P = 128
 G = H // 512
@@ -29,9 +30,9 @@ def tile_list_inlining_adviser_kernel(
     nc = tc.nc
     with ExitStack() as ctx:
         keep = ctx.enter_context(tc.tile_pool(name="keep", bufs=1))
-        stream = ctx.enter_context(tc.tile_pool(name="stream", bufs=5))
+        stream = ctx.enter_context(tc.tile_pool(name="stream", bufs=1))
         bf_pool = ctx.enter_context(tc.tile_pool(name="bf", bufs=4))
-        late = ctx.enter_context(tc.tile_pool(name="late", bufs=4))
+        side = ctx.enter_context(tc.tile_pool(name="side", bufs=5))
         work = ctx.enter_context(tc.tile_pool(name="work", bufs=2))
         psum = ctx.enter_context(tc.psum_pool(name="psum", bufs=1))
 
@@ -41,8 +42,8 @@ def tile_list_inlining_adviser_kernel(
         def held(shape, dtype, name):
             return keep.tile(shape, dtype, name=name, align_bytes=64)
 
-        def staged(shape, dtype, name):
-            return stream.tile(shape, dtype, name=name, tag="stream", align_bytes=64)
+        def staged(shape, dtype, name, slot):
+            return stream.tile(shape, dtype, name=name, tag="slot%d" % slot, align_bytes=64)
 
         def load_scale_rows(queue, plane, scales):
             passes = scales.shape[0]
@@ -58,12 +59,12 @@ def tile_list_inlining_adviser_kernel(
         offs_sb = held([P, S // 16], U16, "offs_sb")
         offs2_sb = held([P, M // 16], U16, "offs2_sb")
         pos_sb = held([P, M // 16], U16, "pos_sb")
-        w1_w = staged([P, H // 2], I32, "w1_w")
-        w1_s = staged([P, H], U8, "w1_s")
-        tab_w = staged([P, T], I32, "tab_w")
-        tab_s = staged([P, T], U8, "tab_s")
-        tab2_s = staged([P, T2], U8, "tab2_s")
-        tab2_w = [staged([P, T2], I32, "tab2_w%d" % a) for a in range(A)]
+        w1_w = staged([P, H // 2], I32, "w1_w", 1)
+        w1_s = staged([P, H], U8, "w1_s", 2)
+        tab_w = staged([P, T], I32, "tab_w", 3)
+        tab_s = staged([P, T], U8, "tab_s", 0)
+        tab2_s = staged([P, T2], U8, "tab2_s", 4)
+        tab2_w = [staged([P, T2], I32, "tab2_w%d" % a, 5 + a) for a in range(A)]
         nc.gpsimd.memset(tab_s[:].bitcast(I32), 0)
         for plane in (w1_s, tab2_s):
             nc.vector.memset(plane[:].bitcast(I32), 0)
@@ -74,33 +75,36 @@ def tile_list_inlining_adviser_kernel(
         gby = held([P, 4], F32, "gby")
 
         nc.sync.dma_start(offs_sb[:], offs)
+        nc.sync.dma_start(offs2_sb[:], offs2)
+        nc.sync.dma_start(pos_sb[:], pos1)
         load_scale_rows(nc.sync, tab_s, tab_scales)
         nc.sync.dma_start(out=tab_w[:], in_=words_view(tab_words[0]))
         nc.sync.dma_start(out=w1_w[:], in_=w1_words[0].bitcast(I32))
-        nc.sync.dma_start(offs2_sb[:], offs2)
         load_scale_rows(nc.sync, w1_s, w1_scales)
         nc.gpsimd.dma_start(out=by_sb[:], in_=by.rearrange("(p t) -> p t", t=4))
         nc.gpsimd.dma_start(out=gy_sb[:], in_=gy.rearrange("(p t) -> p t", t=4))
         b1_view = b1.rearrange("(g u k) -> u g k", g=G, k=16)
         for s in range(4):
             nc.gpsimd.dma_start(out=bias1[s:P:4, :, 0:13], in_=b1_view[:, :, s : s + 13])
-        for a in range(A):
-            nc.sync.dma_start(out=tab2_w[a][:], in_=words_view(tab2_words[a]))
+        nc.sync.dma_start(out=tab2_w[0][:], in_=words_view(tab2_words[0]))
         load_scale_rows(nc.sync, tab2_s, tab2_scales)
-        nc.sync.dma_start(pos_sb[:], pos1)
+        nc.sync.dma_start(out=tab2_w[1][:], in_=words_view(tab2_words[1]))
         for t in range(4):
             nc.scalar.activation(
                 gby[:, t : t + 1], by_sb[:, t : t + 1], IDENT, scale=gy_sb[:, t : t + 1]
             )
 
+        w2_slot = [[0, 1], [5, 6], [0, 1]]
+        w3_slot = [2, 3, 4]
+
         def load_w2(g, a):
-            raw = late.tile([P, 4, 512], F32, name="raw2")
+            raw = staged([P, 4, 512], F32, "raw", w2_slot[g][a])
             rows = w2[512 * a : 512 * (a + 1), 512 * g : 512 * (g + 1)]
             nc.sync.dma_start(out=raw[:], in_=rows.rearrange("(p j) c -> p j c", j=4))
             return raw
 
         def load_w3(g):
-            raw = staged([P, 4, 512], F32, "raw")
+            raw = staged([P, 4, 512], F32, "raw", w3_slot[g])
             rows = w3[512 * g : 512 * (g + 1), :].rearrange("(u j s) n -> s u j n", j=4, s=4)
             for s in range(4):
                 nc.sync.dma_start(out=raw[s:P:4, :, :], in_=rows[s])
@@ -114,12 +118,23 @@ def tile_list_inlining_adviser_kernel(
             )
             return bf
 
-        def round_w3(raw, copy):
-            bf = bf_pool.tile([P, 2048], BF16, name="bf", align_bytes=64)
-            copy(
-                out=bf[:].rearrange("p (t m j) -> p m t j", t=4, j=4),
-                in_=raw[:].rearrange("p j (m t) -> p m t j", t=4),
-            )
+        def round_w2_gpsimd(raw):
+            bf = side.tile([P, 2048], BF16, name="side_bf", tag="side", align_bytes=64)
+            dealt = bf[:].rearrange("p (t u s j) -> p t u s j", t=4, s=4, j=4)
+            source = raw[:].rearrange("p j (u t s) -> p t u s j", t=4, s=4)
+            for t in range(4):
+                nc.gpsimd.tensor_scalar(dealt[:, t], source[:, t], 1.0, 0.0, MULT, ADD)
+            return bf
+
+        def round_w3(raw):
+            bf = side.tile([P, 2048], BF16, name="side_bf", tag="side", align_bytes=64)
+            dealt = bf[:].rearrange("p (t m j) -> p m t j", t=4, j=4)
+            source = raw[:].rearrange("p j (m t) -> p m t j", t=4)
+            for c in range(4):
+                nc.gpsimd.tensor_scalar(
+                    dealt[:, 32 * c : 32 * (c + 1)], source[:, 32 * c : 32 * (c + 1)],
+                    1.0, 0.0, MULT, ADD,
+                )
             return bf
 
         def quantise(bf, name):
@@ -128,17 +143,12 @@ def tile_list_inlining_adviser_kernel(
             nc.vector.quantize_mx(out=codes[:].bitcast(FP8X4), scales=scales[:], in_=bf[:])
             return codes, scales
 
-        v_s = [held([P, 512], U8, "v_s%d" % c) for c in range(2)]
+        v_s = held([P, S], U8, "v_s")
         v_w = [held([P, 512], U32, "v_w%d" % c) for c in range(2)]
         w1_wd = held([P, H // 2], I32, "w1_wd")
         w1_sd = held([P, H], U8, "w1_sd")
-
-        def pick_scope_columns(c):
-            entries = offs_sb[:, 32 * c : 32 * (c + 1)]
-            nc.vector.tensor_copy(v_w[c][:], tab_w[:].bitcast(U32).indirect(entries))
-            nc.vector.tensor_copy(v_s[c][:], tab_s[:].indirect(entries))
-
-        pick_scope_columns(0)
+        nc.vector.tensor_copy(v_s[:], tab_s[:].indirect(offs_sb[:]))
+        nc.vector.tensor_copy(v_w[0][:], tab_w[:].bitcast(U32).indirect(offs_sb[:, 0:32]))
         nc.vector.tensor_copy(
             out=w1_wd[:].rearrange("p (g t u h) -> p g t u h", g=G, t=4, h=2),
             in_=w1_w[:].rearrange("p (g u t h) -> p g t u h", g=G, t=4, h=2),
@@ -147,7 +157,7 @@ def tile_list_inlining_adviser_kernel(
             out=w1_sd[:].bitcast(I32).rearrange("p (g t u i) -> p g u t i", g=G, t=4, i=4),
             in_=w1_s[:].bitcast(I32).rearrange("p (g u i t) -> p g u t i", g=G, t=4, i=4),
         )
-        pick_scope_columns(1)
+        nc.vector.tensor_copy(v_w[1][:], tab_w[:].bitcast(U32).indirect(offs_sb[:, 32:64]))
 
         v2_s = held([P, M], U8, "v2_s")
         v2_w = [held([P, M], U32, "v2_w%d" % a) for a in range(A)]
@@ -167,7 +177,7 @@ def tile_list_inlining_adviser_kernel(
                         lhsT=w1_wd[:, 64 * i : 64 * (i + 1)].bitcast(U8).bitcast(FP4X4),
                         lhsT_scale=w1_sd[:, P * i : P * (i + 1)],
                         rhs=v_w[c][:].bitcast(FP8X4),
-                        rhs_scale=v_s[c][:],
+                        rhs_scale=v_s[:, 512 * c : 512 * (c + 1)],
                         start=True,
                         stop=True,
                     )
@@ -181,8 +191,8 @@ def tile_list_inlining_adviser_kernel(
                 nc.vector.tensor_copy(picked[:, t, :], h[4 * g + t][:].indirect(pos_sb[:]))
             return picked
 
-        def call_projection(w2q, q, index):
-            bank = psum_bank([P, 4, P], index)
+        def call_projection(w2q, q):
+            bank = psum_bank([P, 4, P], q)
             cols = slice(P * q, P * (q + 1))
             for t in range(4):
                 for a in range(A):
@@ -206,15 +216,16 @@ def tile_list_inlining_adviser_kernel(
                 MULT,
             )
 
-        def prepare_w2(g):
+        def prepare_w2(g, rounding):
             raws = [load_w2(g, a) for a in range(A)]
-            return [quantise(round_w2(raws[a]), "w2_%d%d" % (g, a)) for a in range(A)]
+            return [quantise(rounding(raws[a]), "w2_%d%d" % (g, a)) for a in range(A)]
 
         picked = []
         for g in range(G):
             scope_results(g)
             picked.append(pick_scopes(g))
-        w4_w = staged([P, A, N], I32, "w4_w")
+        w2q = [prepare_w2(0, round_w2_gpsimd)]
+        w4_w = held([P, A, N], I32, "w4_w")
         w4_s = held([P, N], U8, "w4_s")
         nc.vector.memset(w4_s[:].bitcast(I32), 0)
         nc.sync.dma_start(out=w4_w[:], in_=w4_words.rearrange("a p c i -> p a (c i)").bitcast(I32))
@@ -229,23 +240,19 @@ def tile_list_inlining_adviser_kernel(
             out=w4_sd[:].rearrange("p (t m i) -> p m t i", t=4, i=16),
             in_=w4_s[:].rearrange("p (m i t) -> p m t i", t=4, i=16),
         )
-        w3q = [
-            quantise(round_w3(load_w3(g), nc.vector.tensor_copy), "w3_%d" % g) for g in range(G - 1)
-        ]
+        w3q = [quantise(round_w3(load_w3(g)), "w3_%d" % g) for g in range(G)]
 
         z_c = [held([P, M], U32, "z_c%d" % g) for g in range(G)]
         z_s = [held([P, M], U8, "z_s%d" % g) for g in range(G)]
         last = G - 1
         for g in range(last):
-            w2q = prepare_w2(g)
             zb = work.tile([P, 4 * M], BF16, name="zb", align_bytes=64)
             for q in range(Q):
-                bank = call_projection(w2q, q, q)
+                bank = call_projection(w2q[g], q)
                 multiply(zb[:, 512 * q : 512 * (q + 1)], picked[g][:, :, P * q : P * (q + 1)], bank)
             nc.vector.quantize_mx(out=z_c[g][:].bitcast(FP8X4), scales=z_s[g][:], in_=zb[:])
-        w2q = prepare_w2(last)
-        w3q.append(quantise(round_w3(load_w3(last), nc.scalar.copy), "w3_%d" % last))
-        b_banks = [call_projection(w2q, q, q) for q in range(Q)]
+            w2q.append(prepare_w2(g + 1, round_w2))
+        b_banks = [call_projection(w2q[last], q) for q in range(Q)]
 
         banks = [psum_bank([P, 4, P], Q + q) for q in range(Q)]
 
@@ -282,7 +289,7 @@ def tile_list_inlining_adviser_kernel(
             out_passes(q, w3q[last][0], w3q[last][1], 0, z_c[last], z_s[last], False, True)
         for q in range(Q):
             cols = slice(P * q, P * (q + 1))
-            y = held([P, 4, P], F32, "y%d" % q)
+            y = keep.tile([P, 4, P], F32, name="y", tag="h%d" % q, align_bytes=64)
             for t in range(4):
                 nc.scalar.activation(
                     y[:, t, :], banks[q][:, t, :], IDENT,

@@ -18,9 +18,12 @@ MULT = mybir.AluOpType.mult
 ADD = mybir.AluOpType.add
 
 P = 128
-G = H // 512
-A = K2 // 512
+PASS = 512
+G = H // PASS
+A = K2 // PASS
 Q = M // P
+BANKS = 8
+SLOTS = 7
 
 
 def tile_list_inlining_adviser_kernel(
@@ -31,8 +34,8 @@ def tile_list_inlining_adviser_kernel(
     with ExitStack() as ctx:
         keep = ctx.enter_context(tc.tile_pool(name="keep", bufs=1))
         stream = ctx.enter_context(tc.tile_pool(name="stream", bufs=1))
-        bf_pool = ctx.enter_context(tc.tile_pool(name="bf", bufs=4))
-        side = ctx.enter_context(tc.tile_pool(name="side", bufs=5))
+        w2_rounded = ctx.enter_context(tc.tile_pool(name="w2_rounded", bufs=1))
+        w3_rounded = ctx.enter_context(tc.tile_pool(name="w3_rounded", bufs=G))
         work = ctx.enter_context(tc.tile_pool(name="work", bufs=2))
         psum = ctx.enter_context(tc.psum_pool(name="psum", bufs=1))
 
@@ -45,11 +48,11 @@ def tile_list_inlining_adviser_kernel(
         def staged(shape, dtype, name, slot):
             return stream.tile(shape, dtype, name=name, tag="slot%d" % slot, align_bytes=64)
 
-        def load_scale_rows(queue, plane, scales):
+        def load_scale_rows(scale_tile, scales):
             passes = scales.shape[0]
             for quad in range(4):
-                queue.dma_start(
-                    out=plane[32 * quad : 32 * quad + 4 * passes, :].bitcast(I32),
+                nc.sync.dma_start(
+                    out=scale_tile[32 * quad : 32 * quad + 4 * passes, :].bitcast(I32),
                     in_=scales[:, 4 * quad : 4 * quad + 4, :].bitcast(I32),
                 )
 
@@ -66,8 +69,8 @@ def tile_list_inlining_adviser_kernel(
         tab2_s = staged([P, T2], U8, "tab2_s", 4)
         tab2_w = [staged([P, T2], I32, "tab2_w%d" % a, 5 + a) for a in range(A)]
         nc.gpsimd.memset(tab_s[:].bitcast(I32), 0)
-        for plane in (w1_s, tab2_s):
-            nc.vector.memset(plane[:].bitcast(I32), 0)
+        for scale_tile in (w1_s, tab2_s):
+            nc.vector.memset(scale_tile[:].bitcast(I32), 0)
 
         bias1 = held([P, G, 16], F32, "bias1")
         by_sb = held([P, 4], F32, "by_sb")
@@ -77,85 +80,72 @@ def tile_list_inlining_adviser_kernel(
         nc.sync.dma_start(offs_sb[:], offs)
         nc.sync.dma_start(offs2_sb[:], offs2)
         nc.sync.dma_start(pos_sb[:], pos1)
-        load_scale_rows(nc.sync, tab_s, tab_scales)
+        load_scale_rows(tab_s, tab_scales)
         nc.sync.dma_start(out=tab_w[:], in_=words_view(tab_words[0]))
         nc.sync.dma_start(out=w1_w[:], in_=w1_words[0].bitcast(I32))
-        load_scale_rows(nc.sync, w1_s, w1_scales)
-        nc.gpsimd.dma_start(out=by_sb[:], in_=by.rearrange("(p t) -> p t", t=4))
-        nc.gpsimd.dma_start(out=gy_sb[:], in_=gy.rearrange("(p t) -> p t", t=4))
+        load_scale_rows(w1_s, w1_scales)
+        nc.sync.dma_start(out=tab2_w[0][:], in_=words_view(tab2_words[0]))
         b1_view = b1.rearrange("(g u k) -> u g k", g=G, k=16)
         for s in range(4):
-            nc.gpsimd.dma_start(out=bias1[s:P:4, :, 0:13], in_=b1_view[:, :, s : s + 13])
-        nc.sync.dma_start(out=tab2_w[0][:], in_=words_view(tab2_words[0]))
-        load_scale_rows(nc.sync, tab2_s, tab2_scales)
+            nc.sync.dma_start(out=bias1[s:P:4, :, 0:13], in_=b1_view[:, :, s : s + 13])
+        load_scale_rows(tab2_s, tab2_scales)
         nc.sync.dma_start(out=tab2_w[1][:], in_=words_view(tab2_words[1]))
-        for t in range(4):
-            nc.scalar.activation(
-                gby[:, t : t + 1], by_sb[:, t : t + 1], IDENT, scale=gy_sb[:, t : t + 1]
-            )
-
-        w2_slot = [[0, 1], [5, 6], [0, 1]]
-        w3_slot = [2, 3, 4]
-
-        def load_w2(g, a):
-            raw = staged([P, 4, 512], F32, "raw", w2_slot[g][a])
-            rows = w2[512 * a : 512 * (a + 1), 512 * g : 512 * (g + 1)]
-            nc.sync.dma_start(out=raw[:], in_=rows.rearrange("(p j) c -> p j c", j=4))
-            return raw
 
         def load_w3(g):
-            raw = staged([P, 4, 512], F32, "raw", w3_slot[g])
-            rows = w3[512 * g : 512 * (g + 1), :].rearrange("(u j s) n -> s u j n", j=4, s=4)
+            raw = staged([P, 4, N], F32, "raw", g)
+            rows = w3[PASS * g : PASS * (g + 1), :].rearrange("(u j s) n -> s u j n", j=4, s=4)
             for s in range(4):
                 nc.sync.dma_start(out=raw[s:P:4, :, :], in_=rows[s])
             return raw
 
-        def round_w2(raw):
-            bf = bf_pool.tile([P, 2048], BF16, name="bf", align_bytes=64)
-            nc.scalar.copy(
-                out=bf[:].rearrange("p (t u s j) -> p t u j s", t=4, s=4, j=4),
-                in_=raw[:].rearrange("p j (u t s) -> p t u j s", t=4, s=4),
-            )
-            return bf
-
-        def round_w2_gpsimd(raw):
-            bf = side.tile([P, 2048], BF16, name="side_bf", tag="side", align_bytes=64)
-            dealt = bf[:].rearrange("p (t u s j) -> p t u s j", t=4, s=4, j=4)
-            source = raw[:].rearrange("p j (u t s) -> p t u s j", t=4, s=4)
-            for t in range(4):
-                nc.gpsimd.tensor_scalar(dealt[:, t], source[:, t], 1.0, 0.0, MULT, ADD)
-            return bf
+        def load_w2(g, a):
+            raw = staged([P, 4, PASS], F32, "raw", (G + A * g + a) % SLOTS)
+            rows = w2[PASS * a : PASS * (a + 1), PASS * g : PASS * (g + 1)]
+            nc.sync.dma_start(out=raw[:], in_=rows.rearrange("(p j) c -> p j c", j=4))
+            return raw
 
         def round_w3(raw):
-            bf = side.tile([P, 2048], BF16, name="side_bf", tag="side", align_bytes=64)
-            dealt = bf[:].rearrange("p (t m j) -> p m t j", t=4, j=4)
+            rounded = w3_rounded.tile([P, 4 * N], BF16, name="w3_bf", align_bytes=64)
+            dealt = rounded[:].rearrange("p (t m j) -> p m t j", t=4, j=4)
             source = raw[:].rearrange("p j (m t) -> p m t j", t=4)
             for c in range(4):
-                nc.gpsimd.tensor_scalar(
-                    dealt[:, 32 * c : 32 * (c + 1)], source[:, 32 * c : 32 * (c + 1)],
-                    1.0, 0.0, MULT, ADD,
-                )
-            return bf
+                part = slice(32 * c, 32 * (c + 1))
+                nc.gpsimd.tensor_scalar(dealt[:, part], source[:, part], 1.0, 0.0, MULT, ADD)
+            return rounded
 
-        def quantise(bf, name):
-            codes = held([P, 512], U32, name + "_c")
-            scales = held([P, 512], U8, name + "_s")
-            nc.vector.quantize_mx(out=codes[:].bitcast(FP8X4), scales=scales[:], in_=bf[:])
+        def round_w2(raw, g, a):
+            rounded = w2_rounded.tile(
+                [P, 4 * PASS], BF16, name="w2_bf", tag="w2_bf%d%d" % (g, a), align_bytes=64
+            )
+            nc.scalar.copy(
+                out=rounded[:].rearrange("p (t u s j) -> p t u j s", t=4, s=4, j=4),
+                in_=raw[:].rearrange("p j (u t s) -> p t u j s", t=4, s=4),
+            )
+            return rounded
+
+        def quantise(rounded, name):
+            codes = held([P, PASS], U32, name + "_c")
+            scales = held([P, PASS], U8, name + "_s")
+            nc.vector.quantize_mx(out=codes[:].bitcast(FP8X4), scales=scales[:], in_=rounded[:])
             return codes, scales
 
+        def prepare_w2(g):
+            raws = [load_w2(g, a) for a in range(A)]
+            return [quantise(round_w2(raws[a], g, a), "w2_%d%d" % (g, a)) for a in range(A)]
+
         v_s = held([P, S], U8, "v_s")
-        v_w = [held([P, 512], U32, "v_w%d" % c) for c in range(2)]
+        v_w = [held([P, PASS], U32, "v_w%d" % c) for c in range(2)]
         w1_wd = held([P, H // 2], I32, "w1_wd")
         w1_sd = held([P, H], U8, "w1_sd")
         nc.vector.tensor_copy(v_s[:], tab_s[:].indirect(offs_sb[:]))
         nc.vector.tensor_copy(v_w[0][:], tab_w[:].bitcast(U32).indirect(offs_sb[:, 0:32]))
         nc.vector.tensor_copy(
-            out=w1_wd[:].rearrange("p (g t u h) -> p g t u h", g=G, t=4, h=2),
-            in_=w1_w[:].rearrange("p (g u t h) -> p g t u h", g=G, t=4, h=2),
+            out=w1_wd[:].rearrange("p (g t u i) -> p g t u i", g=G, t=4, i=2),
+            in_=w1_w[:].rearrange("p (g u t i) -> p g t u i", g=G, t=4, i=2),
         )
         nc.vector.tensor_copy(
-            out=w1_sd[:].bitcast(I32).rearrange("p (g t u i) -> p g u t i", g=G, t=4, i=4),
-            in_=w1_s[:].bitcast(I32).rearrange("p (g u i t) -> p g u t i", g=G, t=4, i=4),
+            out=w1_sd[:].bitcast(I32).rearrange("p (g t c i) -> p g c t i", g=G, t=4, i=4),
+            in_=w1_s[:].bitcast(I32).rearrange("p (g c i t) -> p g c t i", g=G, t=4, i=4),
         )
         nc.vector.tensor_copy(v_w[1][:], tab_w[:].bitcast(U32).indirect(offs_sb[:, 32:64]))
 
@@ -171,32 +161,58 @@ def tile_list_inlining_adviser_kernel(
             for t in range(4):
                 i = 4 * g + t
                 for c in range(2):
-                    bank = psum_bank([P, 512], (2 * i + c) % 8)
+                    half = slice(PASS * c, PASS * (c + 1))
+                    bank = psum_bank([P, PASS], (2 * i + c) % BANKS)
                     nc.tensor.matmul_mx(
                         out=bank[:],
                         lhsT=w1_wd[:, 64 * i : 64 * (i + 1)].bitcast(U8).bitcast(FP4X4),
                         lhsT_scale=w1_sd[:, P * i : P * (i + 1)],
                         rhs=v_w[c][:].bitcast(FP8X4),
-                        rhs_scale=v_s[:, 512 * c : 512 * (c + 1)],
+                        rhs_scale=v_s[:, half],
                         start=True,
                         stop=True,
                     )
                     nc.scalar.activation(
-                        h[i][:, 512 * c : 512 * (c + 1)], bank[:], IDENT, bias=bias1[:, g, 4 * t : 4 * t + 1]
+                        h[i][:, half], bank[:], IDENT, bias=bias1[:, g, 4 * t : 4 * t + 1]
                     )
 
         def pick_scopes(g):
-            picked = held([P, 4, M], F32, "picked%d" % g)
+            scopes = held([P, 4, M], F32, "picked%d" % g)
             for t in range(4):
-                nc.vector.tensor_copy(picked[:, t, :], h[4 * g + t][:].indirect(pos_sb[:]))
-            return picked
+                nc.vector.tensor_copy(scopes[:, t, :], h[4 * g + t][:].indirect(pos_sb[:]))
+            return scopes
 
-        def call_projection(w2q, q):
+        picked = []
+        for g in range(G):
+            scope_results(g)
+            picked.append(pick_scopes(g))
+
+        w3q = [quantise(round_w3(load_w3(g)), "w3_%d" % g) for g in range(G)]
+        w4_w = held([P, A, N], I32, "w4_w")
+        w4_s = held([P, N], U8, "w4_s")
+        nc.vector.memset(w4_s[:].bitcast(I32), 0)
+        nc.sync.dma_start(out=w4_w[:], in_=w4_words.rearrange("a p c i -> p a (c i)").bitcast(I32))
+        load_scale_rows(w4_s, w4_scales)
+        w4_wd = held([P, A, N], I32, "w4_wd")
+        w4_sd = held([P, N], U8, "w4_sd")
+        nc.vector.tensor_copy(
+            out=w4_wd[:].rearrange("p a (t c i) -> p a c t i", t=4, i=4),
+            in_=w4_w[:].rearrange("p a (c i t) -> p a c t i", t=4, i=4),
+        )
+        nc.vector.tensor_copy(
+            out=w4_sd[:].rearrange("p (t c i) -> p c t i", t=4, i=16),
+            in_=w4_s[:].rearrange("p (c i t) -> p c t i", t=4, i=16),
+        )
+        nc.sync.dma_start(out=by_sb[:], in_=by.rearrange("(p t) -> p t", t=4))
+        nc.sync.dma_start(out=gy_sb[:], in_=gy.rearrange("(p t) -> p t", t=4))
+        nc.gpsimd.tensor_tensor(gby[:], gy_sb[:], by_sb[:], MULT)
+
+        def call_projection(w2_pass, q):
             bank = psum_bank([P, 4, P], q)
             cols = slice(P * q, P * (q + 1))
             for t in range(4):
                 for a in range(A):
-                    codes, scales = w2q[a]
+                    codes, scales = w2_pass[a]
                     nc.tensor.matmul_mx(
                         out=bank[:, t, :],
                         lhsT=codes[:, P * t : P * (t + 1)].bitcast(FP8X4),
@@ -208,50 +224,29 @@ def tile_list_inlining_adviser_kernel(
                     )
             return bank
 
-        def multiply(zb, picked, bank):
+        def multiply(z_rounded, scopes, bank):
             nc.vector.tensor_tensor(
-                zb.rearrange("p (m i t) -> p m t i", i=2, t=4),
-                picked.rearrange("p t (m i) -> p m t i", i=2),
-                bank[:].rearrange("p t (m i) -> p m t i", i=2),
+                z_rounded.rearrange("p (c i t) -> p c t i", i=2, t=4),
+                scopes.rearrange("p t (c i) -> p c t i", i=2),
+                bank[:].rearrange("p t (c i) -> p c t i", i=2),
                 MULT,
             )
 
-        def prepare_w2(g, rounding):
-            raws = [load_w2(g, a) for a in range(A)]
-            return [quantise(rounding(raws[a]), "w2_%d%d" % (g, a)) for a in range(A)]
-
-        picked = []
-        for g in range(G):
-            scope_results(g)
-            picked.append(pick_scopes(g))
-        w2q = [prepare_w2(0, round_w2_gpsimd)]
-        w4_w = held([P, A, N], I32, "w4_w")
-        w4_s = held([P, N], U8, "w4_s")
-        nc.vector.memset(w4_s[:].bitcast(I32), 0)
-        nc.sync.dma_start(out=w4_w[:], in_=w4_words.rearrange("a p c i -> p a (c i)").bitcast(I32))
-        load_scale_rows(nc.sync, w4_s, w4_scales)
-        w4_wd = held([P, A, N], I32, "w4_wd")
-        w4_sd = held([P, N], U8, "w4_sd")
-        nc.vector.tensor_copy(
-            out=w4_wd[:].rearrange("p a (t m i) -> p a m t i", t=4, i=4),
-            in_=w4_w[:].rearrange("p a (m i t) -> p a m t i", t=4, i=4),
-        )
-        nc.vector.tensor_copy(
-            out=w4_sd[:].rearrange("p (t m i) -> p m t i", t=4, i=16),
-            in_=w4_s[:].rearrange("p (m i t) -> p m t i", t=4, i=16),
-        )
-        w3q = [quantise(round_w3(load_w3(g)), "w3_%d" % g) for g in range(G)]
-
+        last = G - 1
+        w2q = [prepare_w2(0), prepare_w2(1)]
         z_c = [held([P, M], U32, "z_c%d" % g) for g in range(G)]
         z_s = [held([P, M], U8, "z_s%d" % g) for g in range(G)]
-        last = G - 1
-        for g in range(last):
-            zb = work.tile([P, 4 * M], BF16, name="zb", align_bytes=64)
+
+        def whole_z(g, tag):
+            zb = w2_rounded.tile([P, 4 * M], BF16, name="zb", tag=tag, align_bytes=64)
             for q in range(Q):
                 bank = call_projection(w2q[g], q)
-                multiply(zb[:, 512 * q : 512 * (q + 1)], picked[g][:, :, P * q : P * (q + 1)], bank)
+                multiply(zb[:, PASS * q : PASS * (q + 1)], picked[g][:, :, P * q : P * (q + 1)], bank)
             nc.vector.quantize_mx(out=z_c[g][:].bitcast(FP8X4), scales=z_s[g][:], in_=zb[:])
-            w2q.append(prepare_w2(g + 1, round_w2))
+
+        whole_z(0, "w2_bf11")
+        w2q.append(prepare_w2(last))
+        whole_z(1, "w2_bf20")
         b_banks = [call_projection(w2q[last], q) for q in range(Q)]
 
         banks = [psum_bank([P, 4, P], Q + q) for q in range(Q)]
@@ -281,12 +276,13 @@ def tile_list_inlining_adviser_kernel(
         y_rows = out_0.rearrange("(p t) m -> p t m", t=4)
         for q in range(Q):
             cols = slice(P * q, P * (q + 1))
-            zq = work.tile([P, 512], BF16, name="zq", align_bytes=64)
+            zq = work.tile([P, PASS], BF16, name="zq", align_bytes=64)
             multiply(zq[:], picked[last][:, :, cols], b_banks[q])
             nc.vector.quantize_mx(
                 out=z_c[last][:, cols].bitcast(FP8X4), scales=z_s[last][:, cols], in_=zq[:]
             )
             out_passes(q, w3q[last][0], w3q[last][1], 0, z_c[last], z_s[last], False, True)
+
         for q in range(Q):
             cols = slice(P * q, P * (q + 1))
             y = keep.tile([P, 4, P], F32, name="y", tag="h%d" % q, align_bytes=64)
@@ -296,10 +292,11 @@ def tile_list_inlining_adviser_kernel(
                     bias=gby[:, t : t + 1], scale=gy_sb[:, t : t + 1],
                 )
             nc.sync.dma_start(out=y_rows[:, :, cols], in_=y[:])
-            yb = work.tile([P, 512], BF16, name="yb", align_bytes=64)
-            nc.vector.tensor_copy(
-                out=yb[:].rearrange("p (m i t) -> p m t i", i=2, t=4),
-                in_=y[:].rearrange("p t (m i) -> p m t i", i=2),
+            yb = work.tile([P, PASS], BF16, name="yb", align_bytes=64)
+            copy = nc.scalar.copy if q < Q // 2 else nc.vector.tensor_copy
+            copy(
+                out=yb[:].rearrange("p (c i t) -> p c t i", i=2, t=4),
+                in_=y[:].rearrange("p t (c i) -> p c t i", i=2),
             )
             nc.vector.quantize_mx(out=y_c[:, cols].bitcast(FP8X4), scales=y_s[:, cols], in_=yb[:])
             nc.sync.dma_start(out=words_view(out_1[0])[:, cols], in_=y_c[:, cols].bitcast(I32))

@@ -22,8 +22,6 @@ PASS = 512
 G = H // PASS
 A = K2 // PASS
 Q = M // P
-BANKS = 8
-SLOTS = 7
 
 
 def tile_list_inlining_adviser_kernel(
@@ -33,20 +31,13 @@ def tile_list_inlining_adviser_kernel(
     nc = tc.nc
     with ExitStack() as ctx:
         keep = ctx.enter_context(tc.tile_pool(name="keep", bufs=1))
-        stream = ctx.enter_context(tc.tile_pool(name="stream", bufs=1))
-        w2_rounded = ctx.enter_context(tc.tile_pool(name="w2_rounded", bufs=1))
-        w3_rounded = ctx.enter_context(tc.tile_pool(name="w3_rounded", bufs=G))
-        work = ctx.enter_context(tc.tile_pool(name="work", bufs=2))
         psum = ctx.enter_context(tc.psum_pool(name="psum", bufs=1))
 
         def psum_bank(shape, index):
             return psum.tile(shape, F32, name="bank%d" % index)
 
-        def held(shape, dtype, name):
-            return keep.tile(shape, dtype, name=name, align_bytes=64)
-
-        def staged(shape, dtype, name, slot):
-            return stream.tile(shape, dtype, name=name, tag="slot%d" % slot, align_bytes=64)
+        def held(shape, dtype, name, on=None):
+            return keep.tile(shape, dtype, name=name, tag=on or name, align_bytes=64)
 
         def load_scale_rows(scale_tile, scales):
             passes = scales.shape[0]
@@ -62,15 +53,16 @@ def tile_list_inlining_adviser_kernel(
         offs_sb = held([P, S // 16], U16, "offs_sb")
         offs2_sb = held([P, M // 16], U16, "offs2_sb")
         pos_sb = held([P, M // 16], U16, "pos_sb")
-        w1_w = staged([P, H // 2], I32, "w1_w", 1)
-        w1_s = staged([P, H], U8, "w1_s", 2)
-        tab_w = staged([P, T], I32, "tab_w", 3)
-        tab_s = staged([P, T], U8, "tab_s", 0)
-        tab2_s = staged([P, T2], U8, "tab2_s", 4)
-        tab2_w = [staged([P, T2], I32, "tab2_w%d" % a, 5 + a) for a in range(A)]
-        nc.gpsimd.memset(tab_s[:].bitcast(I32), 0)
-        for scale_tile in (w1_s, tab2_s):
-            nc.vector.memset(scale_tile[:].bitcast(I32), 0)
+        w1_w = held([P, H // 2], I32, "w1_w")
+        w1_s = held([P, H], U8, "w1_s")
+        tab_w = held([P, T], I32, "tab_w")
+        tab_s = held([P, T], U8, "tab_s")
+        tab2_s = held([P, T2], U8, "tab2_s")
+        tab2_w = [held([P, T2], I32, "tab2_w%d" % a) for a in range(A)]
+        w4_w = held([P, A, N], I32, "w4_w")
+        w4_s = held([P, N], U8, "w4_s")
+        for scale_tile in (tab_s, w1_s, tab2_s, w4_s):
+            nc.gpsimd.memset(scale_tile[:].bitcast(I32), 0)
 
         bias1 = held([P, G, 16], F32, "bias1")
         by_sb = held([P, 4], F32, "by_sb")
@@ -78,76 +70,63 @@ def tile_list_inlining_adviser_kernel(
         gby = held([P, 4], F32, "gby")
 
         nc.sync.dma_start(offs_sb[:], offs)
-        nc.sync.dma_start(offs2_sb[:], offs2)
-        nc.sync.dma_start(pos_sb[:], pos1)
+        nc.sync.dma_start(out=gy_sb[:], in_=gy.rearrange("(p t) -> p t", t=4))
+        nc.sync.dma_start(out=by_sb[:], in_=by.rearrange("(p t) -> p t", t=4))
         load_scale_rows(tab_s, tab_scales)
         nc.sync.dma_start(out=tab_w[:], in_=words_view(tab_words[0]))
         nc.sync.dma_start(out=w1_w[:], in_=w1_words[0].bitcast(I32))
         load_scale_rows(w1_s, w1_scales)
-        nc.sync.dma_start(out=tab2_w[0][:], in_=words_view(tab2_words[0]))
         b1_view = b1.rearrange("(g u k) -> u g k", g=G, k=16)
         for s in range(4):
             nc.sync.dma_start(out=bias1[s:P:4, :, 0:13], in_=b1_view[:, :, s : s + 13])
+        nc.sync.dma_start(out=tab2_w[0][:], in_=words_view(tab2_words[0]))
+        nc.sync.dma_start(offs2_sb[:], offs2)
         load_scale_rows(tab2_s, tab2_scales)
+        nc.sync.dma_start(pos_sb[:], pos1)
         nc.sync.dma_start(out=tab2_w[1][:], in_=words_view(tab2_words[1]))
 
-        def load_w3(g):
-            raw = staged([P, 4, N], F32, "raw", g)
-            rows = w3[PASS * g : PASS * (g + 1), :].rearrange("(u j s) n -> s u j n", j=4, s=4)
-            for s in range(4):
-                nc.sync.dma_start(out=raw[s:P:4, :, :], in_=rows[s])
-            return raw
-
         def load_w2(g, a):
-            raw = staged([P, 4, PASS], F32, "raw", (G + A * g + a) % SLOTS)
+            raw = held([P, 4, PASS], F32, "w2_raw%d%d" % (g, a))
             rows = w2[PASS * a : PASS * (a + 1), PASS * g : PASS * (g + 1)]
             nc.sync.dma_start(out=raw[:], in_=rows.rearrange("(p j) c -> p j c", j=4))
             return raw
 
-        def round_w3(raw):
-            rounded = w3_rounded.tile([P, 4 * N], BF16, name="w3_bf", align_bytes=64)
-            dealt = rounded[:].rearrange("p (t m j) -> p m t j", t=4, j=4)
-            source = raw[:].rearrange("p j (m t) -> p m t j", t=4)
-            for c in range(4):
-                part = slice(32 * c, 32 * (c + 1))
-                nc.gpsimd.tensor_scalar(dealt[:, part], source[:, part], 1.0, 0.0, MULT, ADD)
-            return rounded
+        def load_w3(g, on):
+            raw = held([P, 4, N], F32, "w3_raw%d" % g, on)
+            rows = w3[PASS * g : PASS * (g + 1), :].rearrange("(u j s) n -> j u s n", j=4, s=4)
+            for j in range(4):
+                nc.sync.dma_start(out=raw[:, j, :], in_=rows[j])
+            return raw
 
-        def round_w2(raw, g, a):
-            rounded = w2_rounded.tile(
-                [P, 4 * PASS], BF16, name="w2_bf", tag="w2_bf%d%d" % (g, a), align_bytes=64
+        w2_raw = [[load_w2(0, a) for a in range(A)]]
+        load_scale_rows(w4_s, w4_scales)
+        nc.sync.dma_start(out=w4_w[:], in_=w4_words.rearrange("a p c i -> p a (c i)").bitcast(I32))
+        for g in range(1, G):
+            w2_raw.append([load_w2(g, a) for a in range(A)])
+
+        for t in range(4):
+            nc.scalar.activation(
+                gby[:, t : t + 1], by_sb[:, t : t + 1], IDENT, scale=gy_sb[:, t : t + 1]
             )
-            nc.scalar.copy(
-                out=rounded[:].rearrange("p (t u s j) -> p t u j s", t=4, s=4, j=4),
-                in_=raw[:].rearrange("p j (u t s) -> p t u j s", t=4, s=4),
-            )
-            return rounded
 
-        def quantise(rounded, name):
-            codes = held([P, PASS], U32, name + "_c")
-            scales = held([P, PASS], U8, name + "_s")
-            nc.vector.quantize_mx(out=codes[:].bitcast(FP8X4), scales=scales[:], in_=rounded[:])
-            return codes, scales
-
-        def prepare_w2(g):
-            raws = [load_w2(g, a) for a in range(A)]
-            return [quantise(round_w2(raws[a], g, a), "w2_%d%d" % (g, a)) for a in range(A)]
-
-        v_s = held([P, S], U8, "v_s")
-        v_w = [held([P, PASS], U32, "v_w%d" % c) for c in range(2)]
         w1_wd = held([P, H // 2], I32, "w1_wd")
         w1_sd = held([P, H], U8, "w1_sd")
-        nc.vector.tensor_copy(v_s[:], tab_s[:].indirect(offs_sb[:]))
+        v_s = [held([P, PASS], U8, "v_s0")]
+        v_w = [held([P, PASS], U32, "v_w0")]
+        nc.vector.tensor_copy(v_s[0][:], tab_s[:].indirect(offs_sb[:, 0:32]))
         nc.vector.tensor_copy(v_w[0][:], tab_w[:].bitcast(U32).indirect(offs_sb[:, 0:32]))
         nc.vector.tensor_copy(
-            out=w1_wd[:].rearrange("p (g t u i) -> p g t u i", g=G, t=4, i=2),
-            in_=w1_w[:].rearrange("p (g u t i) -> p g t u i", g=G, t=4, i=2),
+            out=w1_wd[:].rearrange("p (g t u i) -> p t g u i", g=G, t=4, i=2),
+            in_=w1_w[:].rearrange("p (g u t i) -> p t g u i", g=G, t=4, i=2),
         )
         nc.vector.tensor_copy(
-            out=w1_sd[:].bitcast(I32).rearrange("p (g t c i) -> p g c t i", g=G, t=4, i=4),
-            in_=w1_s[:].bitcast(I32).rearrange("p (g c i t) -> p g c t i", g=G, t=4, i=4),
+            out=w1_sd[:].bitcast(I32).rearrange("p (g t c i) -> p c g t i", g=G, t=4, i=4),
+            in_=w1_s[:].bitcast(I32).rearrange("p (g c i t) -> p c g t i", g=G, t=4, i=4),
         )
+        v_w.append(held([P, PASS], U32, "v_w1", "w1_w"))
+        v_s.append(held([P, PASS], U8, "v_s1", "w1_s"))
         nc.vector.tensor_copy(v_w[1][:], tab_w[:].bitcast(U32).indirect(offs_sb[:, 32:64]))
+        nc.vector.tensor_copy(v_s[1][:], tab_s[:].indirect(offs_sb[:, 32:64]))
 
         v2_s = held([P, M], U8, "v2_s")
         v2_w = [held([P, M], U32, "v2_w%d" % a) for a in range(A)]
@@ -155,44 +134,41 @@ def tile_list_inlining_adviser_kernel(
         for a in range(A):
             nc.vector.tensor_copy(v2_w[a][:], tab2_w[a][:].bitcast(U32).indirect(offs2_sb[:]))
 
+        w3_raw = [load_w3(g, on) for g, on in enumerate(("tab2_w0", "tab2_w1", "tab_w"))]
+
         h = [held([P, S], F32, "h%d" % i) for i in range(G * 4)]
 
-        def scope_results(g):
+        def scope_half(g, t, c, bank_index):
+            i = 4 * g + t
+            bank = psum_bank([P, PASS], bank_index)
+            nc.tensor.matmul_mx(
+                out=bank[:],
+                lhsT=w1_wd[:, 64 * i : 64 * (i + 1)].bitcast(U8).bitcast(FP4X4),
+                lhsT_scale=w1_sd[:, P * i : P * (i + 1)],
+                rhs=v_w[c][:].bitcast(FP8X4),
+                rhs_scale=v_s[c][:],
+                start=True,
+                stop=True,
+            )
+            nc.scalar.activation(
+                h[i][:, PASS * c : PASS * (c + 1)], bank[:], IDENT,
+                bias=bias1[:, g, 4 * t : 4 * t + 1],
+            )
+
+        def pick_scope(scopes, g, t):
+            nc.vector.tensor_copy(scopes[:, t, :], h[4 * g + t][:].indirect(pos_sb[:]))
+
+        picked = [held([P, 4, M], F32, "picked%d" % g) for g in range(G)]
+        for c in range(2):
             for t in range(4):
-                i = 4 * g + t
-                for c in range(2):
-                    half = slice(PASS * c, PASS * (c + 1))
-                    bank = psum_bank([P, PASS], (2 * i + c) % BANKS)
-                    nc.tensor.matmul_mx(
-                        out=bank[:],
-                        lhsT=w1_wd[:, 64 * i : 64 * (i + 1)].bitcast(U8).bitcast(FP4X4),
-                        lhsT_scale=w1_sd[:, P * i : P * (i + 1)],
-                        rhs=v_w[c][:].bitcast(FP8X4),
-                        rhs_scale=v_s[:, half],
-                        start=True,
-                        stop=True,
-                    )
-                    nc.scalar.activation(
-                        h[i][:, half], bank[:], IDENT, bias=bias1[:, g, 4 * t : 4 * t + 1]
-                    )
+                scope_half(0, t, c, 4 * c + t)
+        for t in range(4):
+            pick_scope(picked[0], 0, t)
+        for t in range(4):
+            for c in range(2):
+                scope_half(1, t, c, 2 * t + c)
+            pick_scope(picked[1], 1, t)
 
-        def pick_scopes(g):
-            scopes = held([P, 4, M], F32, "picked%d" % g)
-            for t in range(4):
-                nc.vector.tensor_copy(scopes[:, t, :], h[4 * g + t][:].indirect(pos_sb[:]))
-            return scopes
-
-        picked = []
-        for g in range(G):
-            scope_results(g)
-            picked.append(pick_scopes(g))
-
-        w3q = [quantise(round_w3(load_w3(g)), "w3_%d" % g) for g in range(G)]
-        w4_w = held([P, A, N], I32, "w4_w")
-        w4_s = held([P, N], U8, "w4_s")
-        nc.vector.memset(w4_s[:].bitcast(I32), 0)
-        nc.sync.dma_start(out=w4_w[:], in_=w4_words.rearrange("a p c i -> p a (c i)").bitcast(I32))
-        load_scale_rows(w4_s, w4_scales)
         w4_wd = held([P, A, N], I32, "w4_wd")
         w4_sd = held([P, N], U8, "w4_sd")
         nc.vector.tensor_copy(
@@ -203,9 +179,34 @@ def tile_list_inlining_adviser_kernel(
             out=w4_sd[:].rearrange("p (t c i) -> p c t i", t=4, i=16),
             in_=w4_s[:].rearrange("p (c i t) -> p c t i", t=4, i=16),
         )
-        nc.sync.dma_start(out=by_sb[:], in_=by.rearrange("(p t) -> p t", t=4))
-        nc.sync.dma_start(out=gy_sb[:], in_=gy.rearrange("(p t) -> p t", t=4))
-        nc.gpsimd.tensor_tensor(gby[:], gy_sb[:], by_sb[:], MULT)
+
+        def prepare_w2(g, a):
+            rounded = held([P, 4 * PASS], BF16, "w2_bf%d%d" % (g, a), "h%d" % (A * g + a))
+            nc.scalar.copy(
+                out=rounded[:].rearrange("p (t u s j) -> p t u j s", t=4, s=4, j=4),
+                in_=w2_raw[g][a][:].rearrange("p j (u t s) -> p t u j s", t=4, s=4),
+            )
+            codes = held([P, PASS], U32, "w2_c%d%d" % (g, a))
+            scales = held([P, PASS], U8, "w2_s%d%d" % (g, a))
+            nc.vector.quantize_mx(out=codes[:].bitcast(FP8X4), scales=scales[:], in_=rounded[:])
+            return codes, scales
+
+        def prepare_w3(g):
+            rounded = held([P, 4 * N], BF16, "w3_bf%d" % g, "h%d" % (A * G + g))
+            codes = held([P, N], U32, "w3_c%d" % g)
+            scales = held([P, N], U8, "w3_s%d" % g)
+            source = w3_raw[g][:].rearrange("p j (m t) -> p m j t", t=4)
+            for half in range(2):
+                part = rounded[:, 2 * N * half : 2 * N * (half + 1)]
+                cols = slice(2 * P * half, 2 * P * (half + 1))
+                nc.scalar.copy(
+                    out=part.rearrange("p (t m j) -> p m j t", t=2, j=4),
+                    in_=source[:, :, :, 2 * half : 2 * half + 2],
+                )
+                nc.vector.quantize_mx(
+                    out=codes[:, cols].bitcast(FP8X4), scales=scales[:, cols], in_=part
+                )
+            return codes, scales
 
         def call_projection(w2_pass, q):
             bank = psum_bank([P, 4, P], q)
@@ -224,81 +225,85 @@ def tile_list_inlining_adviser_kernel(
                     )
             return bank
 
-        def multiply(z_rounded, scopes, bank):
-            nc.vector.tensor_tensor(
-                z_rounded.rearrange("p (c i t) -> p c t i", i=2, t=4),
-                scopes.rearrange("p t (c i) -> p c t i", i=2),
-                bank[:].rearrange("p t (c i) -> p c t i", i=2),
-                MULT,
+        def products(g, w2_pass):
+            zb = held([P, 4 * M], BF16, "zb%d" % g, "h%d" % (A * G + G + g))
+            for q in range(Q):
+                bank = call_projection(w2_pass, q)
+                nc.vector.tensor_tensor(
+                    zb[:, PASS * q : PASS * (q + 1)].rearrange("p (c i t) -> p c t i", i=2, t=4),
+                    picked[g][:, :, P * q : P * (q + 1)].rearrange("p t (c i) -> p c t i", i=2),
+                    bank[:].rearrange("p t (c i) -> p c t i", i=2),
+                    MULT,
+                )
+            return zb
+
+        def quantise_z(g, zb, on):
+            codes = held([P, M], U32, "z_c%d" % g, on)
+            scales = held([P, M], U8, "z_s%d" % g)
+            nc.vector.quantize_mx(out=codes[:].bitcast(FP8X4), scales=scales[:], in_=zb[:])
+            return codes, scales
+
+        w2q = [prepare_w2(0, a) for a in range(A)]
+        for t in range(4):
+            for c in range(2):
+                scope_half(2, t, c, 4 + (2 * t + c) % 4)
+            pick_scope(picked[2], 2, t)
+        zq = []
+        zb = products(0, w2q)
+        for g in range(1, G):
+            w2q = [prepare_w2(g, a) for a in range(A)]
+            zq.append(quantise_z(g - 1, zb, "h%d" % (A * g + 1)))
+            zb = products(g, w2q)
+        zq.append(quantise_z(G - 1, zb, None))
+
+        banks = [psum_bank([P, M], 4 + t) for t in range(4)]
+
+        def out_pass(t, codes, scales, row, moving, moving_scales, first, final):
+            nc.tensor.matmul_mx(
+                out=banks[t][:],
+                lhsT=codes[:, P * t : P * (t + 1)].bitcast(FP8X4),
+                lhsT_scale=scales[row:P, P * t : P * (t + 1)],
+                rhs=moving[:].bitcast(FP8X4),
+                rhs_scale=moving_scales[row:P, :],
+                start=first,
+                stop=final,
             )
 
-        last = G - 1
-        w2q = [prepare_w2(0), prepare_w2(1)]
-        z_c = [held([P, M], U32, "z_c%d" % g) for g in range(G)]
-        z_s = [held([P, M], U8, "z_s%d" % g) for g in range(G)]
-
-        def whole_z(g, tag):
-            zb = w2_rounded.tile([P, 4 * M], BF16, name="zb", tag=tag, align_bytes=64)
-            for q in range(Q):
-                bank = call_projection(w2q[g], q)
-                multiply(zb[:, PASS * q : PASS * (q + 1)], picked[g][:, :, P * q : P * (q + 1)], bank)
-            nc.vector.quantize_mx(out=z_c[g][:].bitcast(FP8X4), scales=z_s[g][:], in_=zb[:])
-
-        whole_z(0, "w2_bf11")
-        w2q.append(prepare_w2(last))
-        whole_z(1, "w2_bf20")
-        b_banks = [call_projection(w2q[last], q) for q in range(Q)]
-
-        banks = [psum_bank([P, 4, P], Q + q) for q in range(Q)]
-
-        def out_passes(q, codes, scales, row, moving, moving_scales, first, final):
-            cols = slice(P * q, P * (q + 1))
-            for t in range(4):
-                nc.tensor.matmul_mx(
-                    out=banks[q][:, t, :],
-                    lhsT=codes[:, P * t : P * (t + 1)].bitcast(FP8X4),
-                    lhsT_scale=scales[row:P, P * t : P * (t + 1)],
-                    rhs=moving[:, cols].bitcast(FP8X4),
-                    rhs_scale=moving_scales[row:P, cols],
-                    start=(first and t == 0),
-                    stop=(final and t == 3),
-                )
-
-        for q in range(Q):
+        for t in range(4):
             for a in range(A):
-                out_passes(q, w4_wd[:, a, :], w4_sd, 4 * a, v2_w[a], v2_s, a == 0, False)
-        for g in range(last):
-            for q in range(Q):
-                out_passes(q, w3q[g][0], w3q[g][1], 0, z_c[g], z_s[g], False, False)
+                out_pass(t, w4_wd[:, a, :], w4_sd, 4 * a, v2_w[a], v2_s, a == 0, False)
+        for g in range(G):
+            codes, scales = prepare_w3(g)
+            for t in range(4):
+                out_pass(t, codes, scales, 0, zq[g][0], zq[g][1], False, g == G - 1)
 
+        y = held([P, 4, M], F32, "y", "w2_raw00")
+        yb = held([P, 4 * M], BF16, "yb", "w2_raw01")
         y_c = held([P, M], U32, "y_c")
         y_s = held([P, M], U8, "y_s")
         y_rows = out_0.rearrange("(p t) m -> p t m", t=4)
-        for q in range(Q):
-            cols = slice(P * q, P * (q + 1))
-            zq = work.tile([P, PASS], BF16, name="zq", align_bytes=64)
-            multiply(zq[:], picked[last][:, :, cols], b_banks[q])
-            nc.vector.quantize_mx(
-                out=z_c[last][:, cols].bitcast(FP8X4), scales=z_s[last][:, cols], in_=zq[:]
-            )
-            out_passes(q, w3q[last][0], w3q[last][1], 0, z_c[last], z_s[last], False, True)
-
-        for q in range(Q):
-            cols = slice(P * q, P * (q + 1))
-            y = keep.tile([P, 4, P], F32, name="y", tag="h%d" % q, align_bytes=64)
-            for t in range(4):
+        for t in range(4):
+            if t == 2:
                 nc.scalar.activation(
-                    y[:, t, :], banks[q][:, t, :], IDENT,
+                    y[:, t, :], banks[t][:], IDENT,
                     bias=gby[:, t : t + 1], scale=gy_sb[:, t : t + 1],
                 )
-            nc.sync.dma_start(out=y_rows[:, :, cols], in_=y[:])
-            yb = work.tile([P, PASS], BF16, name="yb", align_bytes=64)
-            copy = nc.scalar.copy if q < Q // 2 else nc.vector.tensor_copy
+            else:
+                nc.vector.tensor_scalar(
+                    y[:, t, :], banks[t][:], gy_sb[:, t : t + 1], gby[:, t : t + 1], MULT, ADD
+                )
+            nc.sync.dma_start(out=y_rows[:, t, :], in_=y[:, t, :])
+        for q in range(Q):
+            cols = slice(P * q, P * (q + 1))
+            copy = nc.scalar.copy if q == Q - 1 else nc.vector.tensor_copy
             copy(
-                out=yb[:].rearrange("p (c i t) -> p c t i", i=2, t=4),
-                in_=y[:].rearrange("p t (c i) -> p c t i", i=2),
+                out=yb[:, PASS * q : PASS * (q + 1)].rearrange("p (c i t) -> p c t i", i=2, t=4),
+                in_=y[:, :, cols].rearrange("p t (c i) -> p c t i", i=2),
             )
-            nc.vector.quantize_mx(out=y_c[:, cols].bitcast(FP8X4), scales=y_s[:, cols], in_=yb[:])
+        for half in range(2):
+            cols = slice(M // 2 * half, M // 2 * (half + 1))
+            part = yb[:, 2 * M * half : 2 * M * (half + 1)]
+            nc.vector.quantize_mx(out=y_c[:, cols].bitcast(FP8X4), scales=y_s[:, cols], in_=part)
             nc.sync.dma_start(out=words_view(out_1[0])[:, cols], in_=y_c[:, cols].bitcast(I32))
         for quad in range(4):
             nc.sync.dma_start(

@@ -69,16 +69,19 @@ def tile_list_inlining_adviser_kernel(
         gy_sb = held([P, 4], F32, "gy_sb")
         gby = held([P, 4], F32, "gby")
 
+        b1_view = b1.rearrange("(g u k) -> u g k", g=G, k=16)
+
+        def load_bias1(s):
+            nc.sync.dma_start(out=bias1[s:P:4, :, 0:13], in_=b1_view[:, :, s : s + 13])
+
         nc.sync.dma_start(offs_sb[:], offs)
-        nc.sync.dma_start(out=gy_sb[:], in_=gy.rearrange("(p t) -> p t", t=4))
-        nc.sync.dma_start(out=by_sb[:], in_=by.rearrange("(p t) -> p t", t=4))
+        nc.sync.dma_start(out=w1_w[:], in_=w1_words[0].bitcast(I32))
+        load_bias1(0)
         load_scale_rows(tab_s, tab_scales)
         nc.sync.dma_start(out=tab_w[:], in_=words_view(tab_words[0]))
-        nc.sync.dma_start(out=w1_w[:], in_=w1_words[0].bitcast(I32))
         load_scale_rows(w1_s, w1_scales)
-        b1_view = b1.rearrange("(g u k) -> u g k", g=G, k=16)
-        for s in range(4):
-            nc.sync.dma_start(out=bias1[s:P:4, :, 0:13], in_=b1_view[:, :, s : s + 13])
+        for s in range(1, 4):
+            load_bias1(s)
         nc.sync.dma_start(out=tab2_w[0][:], in_=words_view(tab2_words[0]))
         nc.sync.dma_start(offs2_sb[:], offs2)
         load_scale_rows(tab2_s, tab2_scales)
@@ -99,34 +102,29 @@ def tile_list_inlining_adviser_kernel(
             return raw
 
         w2_raw = [[load_w2(0, a) for a in range(A)]]
+        w2_raw.append([load_w2(1, a) for a in range(A)])
         load_scale_rows(w4_s, w4_scales)
         nc.sync.dma_start(out=w4_w[:], in_=w4_words.rearrange("a p c i -> p a (c i)").bitcast(I32))
-        for g in range(1, G):
-            w2_raw.append([load_w2(g, a) for a in range(A)])
-
-        for t in range(4):
-            nc.scalar.activation(
-                gby[:, t : t + 1], by_sb[:, t : t + 1], IDENT, scale=gy_sb[:, t : t + 1]
-            )
+        nc.sync.dma_start(out=gy_sb[:], in_=gy.rearrange("(p t) -> p t", t=4))
+        nc.sync.dma_start(out=by_sb[:], in_=by.rearrange("(p t) -> p t", t=4))
+        w3_raw = [load_w3(0, None), load_w3(1, None)]
 
         w1_wd = held([P, H // 2], I32, "w1_wd")
         w1_sd = held([P, H], U8, "w1_sd")
-        v_s = [held([P, PASS], U8, "v_s0")]
-        v_w = [held([P, PASS], U32, "v_w0")]
-        nc.vector.tensor_copy(v_s[0][:], tab_s[:].indirect(offs_sb[:, 0:32]))
-        nc.vector.tensor_copy(v_w[0][:], tab_w[:].bitcast(U32).indirect(offs_sb[:, 0:32]))
         nc.vector.tensor_copy(
             out=w1_wd[:].rearrange("p (g t u i) -> p t g u i", g=G, t=4, i=2),
             in_=w1_w[:].rearrange("p (g u t i) -> p t g u i", g=G, t=4, i=2),
         )
+        v_s = held([P, S], U8, "v_s")
+        v_w = [held([P, PASS], U32, "v_w0")]
+        nc.vector.tensor_copy(v_s[:], tab_s[:].indirect(offs_sb[:]))
+        nc.vector.tensor_copy(v_w[0][:], tab_w[:].bitcast(U32).indirect(offs_sb[:, 0:32]))
         nc.vector.tensor_copy(
             out=w1_sd[:].bitcast(I32).rearrange("p (g t c i) -> p c g t i", g=G, t=4, i=4),
             in_=w1_s[:].bitcast(I32).rearrange("p (g c i t) -> p c g t i", g=G, t=4, i=4),
         )
-        v_w.append(held([P, PASS], U32, "v_w1", "w1_w"))
-        v_s.append(held([P, PASS], U8, "v_s1", "w1_s"))
+        v_w.append(held([P, PASS], U32, "v_w1", "w1_s"))
         nc.vector.tensor_copy(v_w[1][:], tab_w[:].bitcast(U32).indirect(offs_sb[:, 32:64]))
-        nc.vector.tensor_copy(v_s[1][:], tab_s[:].indirect(offs_sb[:, 32:64]))
 
         v2_s = held([P, M], U8, "v2_s")
         v2_w = [held([P, M], U32, "v2_w%d" % a) for a in range(A)]
@@ -134,19 +132,23 @@ def tile_list_inlining_adviser_kernel(
         for a in range(A):
             nc.vector.tensor_copy(v2_w[a][:], tab2_w[a][:].bitcast(U32).indirect(offs2_sb[:]))
 
-        w3_raw = [load_w3(g, on) for g, on in enumerate(("tab2_w0", "tab2_w1", "tab_w"))]
+        w3_raw.append(load_w3(G - 1, "tab2_w0"))
+        w2_raw.append([load_w2(2, a) for a in range(A)])
 
-        h = [held([P, S], F32, "h%d" % i) for i in range(G * 4)]
+        h = {}
 
         def scope_half(g, t, c, bank_index):
             i = 4 * g + t
+            if i not in h:
+                on = {6: "w2_raw00", 7: "w2_raw01"}.get(i)
+                h.setdefault(i, held([P, S], F32, "h%d" % i, on))
             bank = psum_bank([P, PASS], bank_index)
             nc.tensor.matmul_mx(
                 out=bank[:],
                 lhsT=w1_wd[:, 64 * i : 64 * (i + 1)].bitcast(U8).bitcast(FP4X4),
                 lhsT_scale=w1_sd[:, P * i : P * (i + 1)],
                 rhs=v_w[c][:].bitcast(FP8X4),
-                rhs_scale=v_s[c][:],
+                rhs_scale=v_s[:, PASS * c : PASS * (c + 1)],
                 start=True,
                 stop=True,
             )
@@ -160,52 +162,64 @@ def tile_list_inlining_adviser_kernel(
 
         picked = [held([P, 4, M], F32, "picked%d" % g) for g in range(G)]
         for c in range(2):
-            for t in range(4):
-                scope_half(0, t, c, 4 * c + t)
+            for t in range(2):
+                scope_half(0, t, c, 2 * t + c)
         for t in range(4):
+            if t >= 2:
+                for c in range(2):
+                    scope_half(0, t, c, 2 * t + c)
             pick_scope(picked[0], 0, t)
-        for t in range(4):
+        for t in range(2):
             for c in range(2):
                 scope_half(1, t, c, 2 * t + c)
             pick_scope(picked[1], 1, t)
 
-        w4_wd = held([P, A, N], I32, "w4_wd")
-        w4_sd = held([P, N], U8, "w4_sd")
-        nc.vector.tensor_copy(
-            out=w4_wd[:].rearrange("p a (t c i) -> p a c t i", t=4, i=4),
-            in_=w4_w[:].rearrange("p a (c i t) -> p a c t i", t=4, i=4),
-        )
-        nc.vector.tensor_copy(
-            out=w4_sd[:].rearrange("p (t c i) -> p c t i", t=4, i=16),
-            in_=w4_s[:].rearrange("p (c i t) -> p c t i", t=4, i=16),
-        )
-
-        def prepare_w2(g, a):
-            rounded = held([P, 4 * PASS], BF16, "w2_bf%d%d" % (g, a), "h%d" % (A * g + a))
+        def round_w2(g, a, on):
+            rounded = held([P, 4 * PASS], BF16, "w2_bf%d%d" % (g, a), on)
+            if g == 1:
+                dealt = rounded[:].rearrange("p (t u s j) -> p t u s j", t=4, s=4, j=4)
+                source = w2_raw[g][a][:].rearrange("p j (u t s) -> p t u s j", t=4, s=4)
+                for t in range(4):
+                    for c in range(2):
+                        part = slice(16 * c, 16 * (c + 1))
+                        nc.gpsimd.tensor_scalar(
+                            dealt[:, t, part], source[:, t, part], 1.0, 0.0, MULT, ADD
+                        )
+                return rounded
             nc.scalar.copy(
                 out=rounded[:].rearrange("p (t u s j) -> p t u j s", t=4, s=4, j=4),
                 in_=w2_raw[g][a][:].rearrange("p j (u t s) -> p t u j s", t=4, s=4),
             )
+            return rounded
+
+        def quantise_w2(g, a, rounded):
             codes = held([P, PASS], U32, "w2_c%d%d" % (g, a))
             scales = held([P, PASS], U8, "w2_s%d%d" % (g, a))
             nc.vector.quantize_mx(out=codes[:].bitcast(FP8X4), scales=scales[:], in_=rounded[:])
             return codes, scales
 
-        def prepare_w3(g):
-            rounded = held([P, 4 * N], BF16, "w3_bf%d" % g, "h%d" % (A * G + g))
-            codes = held([P, N], U32, "w3_c%d" % g)
-            scales = held([P, N], U8, "w3_s%d" % g)
+        def round_w3(g, on):
+            rounded = held([P, 4 * N], BF16, "w3_bf%d" % g, on)
+            if g == 0:
+                dealt = rounded[:].rearrange("p (t m j) -> p m t j", t=4, j=4)
+                source = w3_raw[g][:].rearrange("p j (m t) -> p m t j", t=4)
+                for c in range(8):
+                    part = slice(16 * c, 16 * (c + 1))
+                    nc.gpsimd.tensor_scalar(dealt[:, part], source[:, part], 1.0, 0.0, MULT, ADD)
+                return rounded
             source = w3_raw[g][:].rearrange("p j (m t) -> p m j t", t=4)
             for half in range(2):
                 part = rounded[:, 2 * N * half : 2 * N * (half + 1)]
-                cols = slice(2 * P * half, 2 * P * (half + 1))
                 nc.scalar.copy(
                     out=part.rearrange("p (t m j) -> p m j t", t=2, j=4),
                     in_=source[:, :, :, 2 * half : 2 * half + 2],
                 )
-                nc.vector.quantize_mx(
-                    out=codes[:, cols].bitcast(FP8X4), scales=scales[:, cols], in_=part
-                )
+            return rounded
+
+        def quantise_w3(g, rounded, on):
+            codes = held([P, N], U32, "w3_c%d" % g, on)
+            scales = held([P, N], U8, "w3_s%d" % g)
+            nc.vector.quantize_mx(out=codes[:].bitcast(FP8X4), scales=scales[:], in_=rounded[:])
             return codes, scales
 
         def call_projection(w2_pass, q):
@@ -225,16 +239,18 @@ def tile_list_inlining_adviser_kernel(
                     )
             return bank
 
+        def multiply(z_rounded, g, q, bank, engine=nc.vector):
+            engine.tensor_tensor(
+                z_rounded.rearrange("p (c i t) -> p c t i", i=2, t=4),
+                picked[g][:, :, P * q : P * (q + 1)].rearrange("p t (c i) -> p c t i", i=2),
+                bank.rearrange("p t (c i) -> p c t i", i=2),
+                MULT,
+            )
+
         def products(g, w2_pass):
-            zb = held([P, 4 * M], BF16, "zb%d" % g, "h%d" % (A * G + G + g))
+            zb = held([P, 4 * M], BF16, "zb%d" % g, ("tab2_w1", "h3")[g])
             for q in range(Q):
-                bank = call_projection(w2_pass, q)
-                nc.vector.tensor_tensor(
-                    zb[:, PASS * q : PASS * (q + 1)].rearrange("p (c i t) -> p c t i", i=2, t=4),
-                    picked[g][:, :, P * q : P * (q + 1)].rearrange("p t (c i) -> p c t i", i=2),
-                    bank[:].rearrange("p t (c i) -> p c t i", i=2),
-                    MULT,
-                )
+                multiply(zb[:, PASS * q : PASS * (q + 1)], g, q, call_projection(w2_pass, q)[:])
             return zb
 
         def quantise_z(g, zb, on):
@@ -243,67 +259,92 @@ def tile_list_inlining_adviser_kernel(
             nc.vector.quantize_mx(out=codes[:].bitcast(FP8X4), scales=scales[:], in_=zb[:])
             return codes, scales
 
-        w2q = [prepare_w2(0, a) for a in range(A)]
+        last = G - 1
+        w2_bf1 = [round_w2(1, a, None) for a in range(A)]
+        w4_wd = held([P, A, N], I32, "w4_wd")
+        w4_sd = held([P, N], U8, "w4_sd")
+        nc.gpsimd.tensor_copy(
+            out=w4_wd[:].rearrange("p a (t c i) -> p a c t i", t=4, i=4),
+            in_=w4_w[:].rearrange("p a (c i t) -> p a c t i", t=4, i=4),
+        )
+        nc.gpsimd.tensor_copy(
+            out=w4_sd[:].rearrange("p (t c i) -> p c t i", t=4, i=16),
+            in_=w4_s[:].rearrange("p (c i t) -> p c t i", t=4, i=16),
+        )
+
+        nc.gpsimd.tensor_tensor(gby[:], gy_sb[:], by_sb[:], MULT)
+
+        w2q = [quantise_w2(0, a, round_w2(0, a, "h%d" % a)) for a in range(A)]
+        for t in range(2, 4):
+            for c in range(2):
+                scope_half(1, t, c, 2 * t + c)
+            pick_scope(picked[1], 1, t)
+        w3_bf = [round_w3(0, "h0")]
         for t in range(4):
             for c in range(2):
-                scope_half(2, t, c, 4 + (2 * t + c) % 4)
+                scope_half(2, t, c, 2 * t + c)
             pick_scope(picked[2], 2, t)
-        zq = []
-        zb = products(0, w2q)
-        for g in range(1, G):
-            w2q = [prepare_w2(g, a) for a in range(A)]
-            zq.append(quantise_z(g - 1, zb, "h%d" % (A * g + 1)))
-            zb = products(g, w2q)
-        zq.append(quantise_z(G - 1, zb, None))
+        zb0 = products(0, w2q)
+        w2q = [quantise_w2(1, a, w2_bf1[a]) for a in range(A)]
+        zq = [quantise_z(0, zb0, "w2_bf11")]
+        zb1 = products(1, w2q)
+        w3_bf.extend([round_w3(g, "h%d" % g) for g in range(1, G)])
+        w3q = [quantise_w3(g, w3_bf[g], None) for g in range(last)]
+        w2q = [quantise_w2(2, a, round_w2(2, a, "h%d" % (4 + a))) for a in range(A)]
+        zq.append(quantise_z(1, zb1, "h5"))
+        w3q.append(quantise_w3(last, w3_bf[last], "w2_raw21"))
+        b_banks = [call_projection(w2q, q) for q in range(Q)]
 
-        banks = [psum_bank([P, M], 4 + t) for t in range(4)]
+        banks = [psum_bank([P, 4, P], Q + q) for q in range(Q)]
 
-        def out_pass(t, codes, scales, row, moving, moving_scales, first, final):
-            nc.tensor.matmul_mx(
-                out=banks[t][:],
-                lhsT=codes[:, P * t : P * (t + 1)].bitcast(FP8X4),
-                lhsT_scale=scales[row:P, P * t : P * (t + 1)],
-                rhs=moving[:].bitcast(FP8X4),
-                rhs_scale=moving_scales[row:P, :],
-                start=first,
-                stop=final,
-            )
-
-        for t in range(4):
-            for a in range(A):
-                out_pass(t, w4_wd[:, a, :], w4_sd, 4 * a, v2_w[a], v2_s, a == 0, False)
-        for g in range(G):
-            codes, scales = prepare_w3(g)
+        def out_passes(q, codes, scales, row, moving, moving_scales, first, final):
+            cols = slice(P * q, P * (q + 1))
             for t in range(4):
-                out_pass(t, codes, scales, 0, zq[g][0], zq[g][1], False, g == G - 1)
+                nc.tensor.matmul_mx(
+                    out=banks[q][:, t, :],
+                    lhsT=codes[:, P * t : P * (t + 1)].bitcast(FP8X4),
+                    lhsT_scale=scales[row:P, P * t : P * (t + 1)],
+                    rhs=moving[:, cols].bitcast(FP8X4),
+                    rhs_scale=moving_scales[row:P, cols],
+                    start=(first and t == 0),
+                    stop=(final and t == 3),
+                )
 
-        y = held([P, 4, M], F32, "y", "w2_raw00")
-        yb = held([P, 4 * M], BF16, "yb", "w2_raw01")
+        for q in range(Q):
+            for a in range(A):
+                out_passes(q, w4_wd[:, a, :], w4_sd, 4 * a, v2_w[a], v2_s, a == 0, False)
+        for g in range(last):
+            for q in range(Q):
+                out_passes(q, w3q[g][0], w3q[g][1], 0, zq[g][0], zq[g][1], False, False)
+
+        z_c = held([P, M], U32, "z_c2")
+        z_s = held([P, M], U8, "z_s2")
+        for q in range(Q):
+            cols = slice(P * q, P * (q + 1))
+            zb = held([P, PASS], BF16, "zb2%d" % q)
+            multiply(zb[:], last, q, b_banks[q][:])
+            nc.vector.quantize_mx(out=z_c[:, cols].bitcast(FP8X4), scales=z_s[:, cols], in_=zb[:])
+            out_passes(q, w3q[last][0], w3q[last][1], 0, z_c, z_s, False, True)
+
         y_c = held([P, M], U32, "y_c")
         y_s = held([P, M], U8, "y_s")
         y_rows = out_0.rearrange("(p t) m -> p t m", t=4)
-        for t in range(4):
-            if t == 2:
-                nc.scalar.activation(
-                    y[:, t, :], banks[t][:], IDENT,
-                    bias=gby[:, t : t + 1], scale=gy_sb[:, t : t + 1],
-                )
-            else:
-                nc.vector.tensor_scalar(
-                    y[:, t, :], banks[t][:], gy_sb[:, t : t + 1], gby[:, t : t + 1], MULT, ADD
-                )
-            nc.sync.dma_start(out=y_rows[:, t, :], in_=y[:, t, :])
         for q in range(Q):
             cols = slice(P * q, P * (q + 1))
-            copy = nc.scalar.copy if q == Q - 1 else nc.vector.tensor_copy
+            y = held([P, 4, P], F32, "y%d" % q, "h%d" % (8 + q))
+            for t in range(4):
+                nc.scalar.activation(
+                    y[:, t, :], banks[q][:, t, :], IDENT,
+                    bias=gby[:, t : t + 1], scale=gy_sb[:, t : t + 1],
+                )
+            nc.sync.dma_start(out=y_rows[:, :, cols], in_=y[:])
+            yb = held([P, PASS], BF16, "yb%d" % q)
+            copy = nc.scalar.copy if q < Q // 2 else nc.vector.tensor_copy
             copy(
-                out=yb[:, PASS * q : PASS * (q + 1)].rearrange("p (c i t) -> p c t i", i=2, t=4),
-                in_=y[:, :, cols].rearrange("p t (c i) -> p c t i", i=2),
+                out=yb[:].rearrange("p (c i t) -> p c t i", i=2, t=4),
+                in_=y[:].rearrange("p t (c i) -> p c t i", i=2),
             )
-        for half in range(2):
-            cols = slice(M // 2 * half, M // 2 * (half + 1))
-            part = yb[:, 2 * M * half : 2 * M * (half + 1)]
-            nc.vector.quantize_mx(out=y_c[:, cols].bitcast(FP8X4), scales=y_s[:, cols], in_=part)
+            nc.vector.quantize_mx(out=y_c[:, cols].bitcast(FP8X4), scales=y_s[:, cols], in_=yb[:])
             nc.sync.dma_start(out=words_view(out_1[0])[:, cols], in_=y_c[:, cols].bitcast(I32))
         for quad in range(4):
             nc.sync.dma_start(

@@ -102,12 +102,13 @@ def tile_list_inlining_adviser_kernel(
             return raw
 
         w2_raw = [[load_w2(0, a) for a in range(A)]]
-        w2_raw.append([load_w2(1, a) for a in range(A)])
         load_scale_rows(w4_s, w4_scales)
         nc.sync.dma_start(out=w4_w[:], in_=w4_words.rearrange("a p c i -> p a (c i)").bitcast(I32))
         nc.sync.dma_start(out=gy_sb[:], in_=gy.rearrange("(p t) -> p t", t=4))
         nc.sync.dma_start(out=by_sb[:], in_=by.rearrange("(p t) -> p t", t=4))
-        w3_raw = [load_w3(0, None), load_w3(1, None)]
+        w2_raw.append([load_w2(1, a) for a in range(A)])
+        w3_raw = [load_w3(0, None)]
+        w2_raw.append([load_w2(2, a) for a in range(A)])
 
         w1_wd = held([P, H // 2], I32, "w1_wd")
         w1_sd = held([P, H], U8, "w1_sd")
@@ -132,8 +133,7 @@ def tile_list_inlining_adviser_kernel(
         for a in range(A):
             nc.vector.tensor_copy(v2_w[a][:], tab2_w[a][:].bitcast(U32).indirect(offs2_sb[:]))
 
-        w3_raw.append(load_w3(G - 1, "tab2_w0"))
-        w2_raw.append([load_w2(2, a) for a in range(A)])
+        w3_raw.extend([load_w3(1 + a, "tab2_w%d" % a) for a in range(A)])
 
         h = {}
 
@@ -176,16 +176,6 @@ def tile_list_inlining_adviser_kernel(
 
         def round_w2(g, a, on):
             rounded = held([P, 4 * PASS], BF16, "w2_bf%d%d" % (g, a), on)
-            if g == 1:
-                dealt = rounded[:].rearrange("p (t u s j) -> p t u s j", t=4, s=4, j=4)
-                source = w2_raw[g][a][:].rearrange("p j (u t s) -> p t u s j", t=4, s=4)
-                for t in range(4):
-                    for c in range(2):
-                        part = slice(16 * c, 16 * (c + 1))
-                        nc.gpsimd.tensor_scalar(
-                            dealt[:, t, part], source[:, t, part], 1.0, 0.0, MULT, ADD
-                        )
-                return rounded
             nc.scalar.copy(
                 out=rounded[:].rearrange("p (t u s j) -> p t u j s", t=4, s=4, j=4),
                 in_=w2_raw[g][a][:].rearrange("p j (u t s) -> p t u j s", t=4, s=4),
@@ -200,11 +190,11 @@ def tile_list_inlining_adviser_kernel(
 
         def round_w3(g, on):
             rounded = held([P, 4 * N], BF16, "w3_bf%d" % g, on)
-            if g == 0:
+            if g < G - 1:
                 dealt = rounded[:].rearrange("p (t m j) -> p m t j", t=4, j=4)
                 source = w3_raw[g][:].rearrange("p j (m t) -> p m t j", t=4)
-                for c in range(8):
-                    part = slice(16 * c, 16 * (c + 1))
+                for c in range(4):
+                    part = slice(32 * c, 32 * (c + 1))
                     nc.gpsimd.tensor_scalar(dealt[:, part], source[:, part], 1.0, 0.0, MULT, ADD)
                 return rounded
             source = w3_raw[g][:].rearrange("p j (m t) -> p m j t", t=4)
@@ -247,8 +237,8 @@ def tile_list_inlining_adviser_kernel(
                 MULT,
             )
 
-        def products(g, w2_pass):
-            zb = held([P, 4 * M], BF16, "zb%d" % g, ("tab2_w1", "h3")[g])
+        def products(g, w2_pass, on):
+            zb = held([P, 4 * M], BF16, "zb%d" % g, on)
             for q in range(Q):
                 multiply(zb[:, PASS * q : PASS * (q + 1)], g, q, call_projection(w2_pass, q)[:])
             return zb
@@ -260,14 +250,13 @@ def tile_list_inlining_adviser_kernel(
             return codes, scales
 
         last = G - 1
-        w2_bf1 = [round_w2(1, a, None) for a in range(A)]
         w4_wd = held([P, A, N], I32, "w4_wd")
         w4_sd = held([P, N], U8, "w4_sd")
-        nc.gpsimd.tensor_copy(
+        nc.vector.tensor_copy(
             out=w4_wd[:].rearrange("p a (t c i) -> p a c t i", t=4, i=4),
             in_=w4_w[:].rearrange("p a (c i t) -> p a c t i", t=4, i=4),
         )
-        nc.gpsimd.tensor_copy(
+        nc.vector.tensor_copy(
             out=w4_sd[:].rearrange("p (t c i) -> p c t i", t=4, i=16),
             in_=w4_s[:].rearrange("p (c i t) -> p c t i", t=4, i=16),
         )
@@ -279,20 +268,37 @@ def tile_list_inlining_adviser_kernel(
             for c in range(2):
                 scope_half(1, t, c, 2 * t + c)
             pick_scope(picked[1], 1, t)
-        w3_bf = [round_w3(0, "h0")]
         for t in range(4):
             for c in range(2):
                 scope_half(2, t, c, 2 * t + c)
             pick_scope(picked[2], 2, t)
-        zb0 = products(0, w2q)
-        w2q = [quantise_w2(1, a, w2_bf1[a]) for a in range(A)]
-        zq = [quantise_z(0, zb0, "w2_bf11")]
-        zb1 = products(1, w2q)
-        w3_bf.extend([round_w3(g, "h%d" % g) for g in range(1, G)])
-        w3q = [quantise_w3(g, w3_bf[g], None) for g in range(last)]
-        w2q = [quantise_w2(2, a, round_w2(2, a, "h%d" % (4 + a))) for a in range(A)]
-        zq.append(quantise_z(1, zb1, "h5"))
-        w3q.append(quantise_w3(last, w3_bf[last], "w2_raw21"))
+        w3_bf0 = round_w3(0, "h10")
+        zb0 = products(0, w2q, "h11")
+        w2q = [quantise_w2(1, a, round_w2(1, a, "h%d" % (2 + a))) for a in range(A)]
+        w3q = [quantise_w3(0, w3_bf0, "w2_raw11")]
+        w2q_next = []
+        zb1 = []
+        for a in range(A):
+            w2q_next.append(quantise_w2(2, a, round_w2(2, a, "h%d" % (4 + a))))
+            if a == 0:
+                zq = [quantise_z(0, zb0, "w2_raw20")]
+                w3_bf1 = round_w3(1, "h11")
+            half = held([P, 2 * M], BF16, "zb1%d" % a, "h%d" % (4 + a))
+            for i in range(2):
+                q = 2 * a + i
+                multiply(half[:, PASS * i : PASS * (i + 1)], 1, q, call_projection(w2q, q)[:])
+            zb1.append(half)
+        w2q = w2q_next
+        z1_c = held([P, M], U32, "z_c1")
+        z1_s = held([P, M], U8, "z_s1")
+        w3q.append(quantise_w3(1, w3_bf1, None))
+        for a in range(A):
+            cols = slice(M // 2 * a, M // 2 * (a + 1))
+            nc.vector.quantize_mx(
+                out=z1_c[:, cols].bitcast(FP8X4), scales=z1_s[:, cols], in_=zb1[a][:]
+            )
+        zq.append((z1_c, z1_s))
+        w3q.append(quantise_w3(2, round_w3(2, "h1"), None))
         b_banks = [call_projection(w2q, q) for q in range(Q)]
 
         banks = [psum_bank([P, 4, P], Q + q) for q in range(Q)]
@@ -313,9 +319,8 @@ def tile_list_inlining_adviser_kernel(
         for q in range(Q):
             for a in range(A):
                 out_passes(q, w4_wd[:, a, :], w4_sd, 4 * a, v2_w[a], v2_s, a == 0, False)
-        for g in range(last):
-            for q in range(Q):
-                out_passes(q, w3q[g][0], w3q[g][1], 0, zq[g][0], zq[g][1], False, False)
+        for q in range(Q):
+            out_passes(q, w3q[0][0], w3q[0][1], 0, zq[0][0], zq[0][1], False, False)
 
         z_c = held([P, M], U32, "z_c2")
         z_s = held([P, M], U8, "z_s2")
@@ -324,6 +329,7 @@ def tile_list_inlining_adviser_kernel(
             zb = held([P, PASS], BF16, "zb2%d" % q)
             multiply(zb[:], last, q, b_banks[q][:])
             nc.vector.quantize_mx(out=z_c[:, cols].bitcast(FP8X4), scales=z_s[:, cols], in_=zb[:])
+            out_passes(q, w3q[1][0], w3q[1][1], 0, zq[1][0], zq[1][1], False, False)
             out_passes(q, w3q[last][0], w3q[last][1], 0, z_c, z_s, False, True)
 
         y_c = held([P, M], U32, "y_c")
@@ -331,7 +337,7 @@ def tile_list_inlining_adviser_kernel(
         y_rows = out_0.rearrange("(p t) m -> p t m", t=4)
         for q in range(Q):
             cols = slice(P * q, P * (q + 1))
-            y = held([P, 4, P], F32, "y%d" % q, "h%d" % (8 + q))
+            y = held([P, 4, P], F32, "y%d" % q)
             for t in range(4):
                 nc.scalar.activation(
                     y[:, t, :], banks[q][:, t, :], IDENT,
@@ -339,8 +345,7 @@ def tile_list_inlining_adviser_kernel(
                 )
             nc.sync.dma_start(out=y_rows[:, :, cols], in_=y[:])
             yb = held([P, PASS], BF16, "yb%d" % q)
-            copy = nc.scalar.copy if q < Q // 2 else nc.vector.tensor_copy
-            copy(
+            nc.vector.tensor_copy(
                 out=yb[:].rearrange("p (c i t) -> p c t i", i=2, t=4),
                 in_=y[:].rearrange("p t (c i) -> p c t i", i=2),
             )

@@ -190,13 +190,6 @@ def tile_list_inlining_adviser_kernel(
 
         def round_w3(g, on):
             rounded = held([P, 4 * N], BF16, "w3_bf%d" % g, on)
-            if g < G - 1:
-                dealt = rounded[:].rearrange("p (t m j) -> p m t j", t=4, j=4)
-                source = w3_raw[g][:].rearrange("p j (m t) -> p m t j", t=4)
-                for c in range(4):
-                    part = slice(32 * c, 32 * (c + 1))
-                    nc.gpsimd.tensor_scalar(dealt[:, part], source[:, part], 1.0, 0.0, MULT, ADD)
-                return rounded
             source = w3_raw[g][:].rearrange("p j (m t) -> p m j t", t=4)
             for half in range(2):
                 part = rounded[:, 2 * N * half : 2 * N * (half + 1)]
@@ -272,17 +265,14 @@ def tile_list_inlining_adviser_kernel(
             for c in range(2):
                 scope_half(2, t, c, 2 * t + c)
             pick_scope(picked[2], 2, t)
-        w3_bf0 = round_w3(0, "h10")
         zb0 = products(0, w2q, "h11")
         w2q = [quantise_w2(1, a, round_w2(1, a, "h%d" % (2 + a))) for a in range(A)]
-        w3q = [quantise_w3(0, w3_bf0, "w2_raw11")]
         w2q_next = []
         zb1 = []
         for a in range(A):
             w2q_next.append(quantise_w2(2, a, round_w2(2, a, "h%d" % (4 + a))))
             if a == 0:
                 zq = [quantise_z(0, zb0, "w2_raw20")]
-                w3_bf1 = round_w3(1, "h11")
             half = held([P, 2 * M], BF16, "zb1%d" % a, "h%d" % (4 + a))
             for i in range(2):
                 q = 2 * a + i
@@ -291,7 +281,21 @@ def tile_list_inlining_adviser_kernel(
         w2q = w2q_next
         z1_c = held([P, M], U32, "z_c1")
         z1_s = held([P, M], U8, "z_s1")
-        w3q.append(quantise_w3(1, w3_bf1, None))
+        w3_c0 = held([P, N], U32, "w3_c0")
+        w3_s0 = held([P, N], U8, "w3_s0")
+        source = w3_raw[0][:].rearrange("p j (m t) -> p m j t", t=4)
+        for half, copy, on in ((1, nc.vector.tensor_copy, "h3"), (0, nc.scalar.copy, "w2_raw21")):
+            part = held([P, 2 * N], BF16, "w3_bf0%d" % half, on)
+            cols = slice(2 * P * half, 2 * P * (half + 1))
+            copy(
+                out=part[:].rearrange("p (t m j) -> p m j t", t=2, j=4),
+                in_=source[:, :, :, 2 * half : 2 * half + 2],
+            )
+            nc.vector.quantize_mx(
+                out=w3_c0[:, cols].bitcast(FP8X4), scales=w3_s0[:, cols], in_=part[:]
+            )
+        w3q = [(w3_c0, w3_s0)]
+        w3q.append(quantise_w3(1, round_w3(1, "h0"), None))
         for a in range(A):
             cols = slice(M // 2 * a, M // 2 * (a + 1))
             nc.vector.quantize_mx(

@@ -82,9 +82,9 @@ def tile_list_inlining_adviser_kernel(
         load_scale_rows(w1_s, w1_scales)
         for s in range(1, 4):
             load_bias1(s)
-        nc.sync.dma_start(out=tab2_w[0][:], in_=words_view(tab2_words[0]))
         nc.sync.dma_start(offs2_sb[:], offs2)
         load_scale_rows(tab2_s, tab2_scales)
+        nc.sync.dma_start(out=tab2_w[0][:], in_=words_view(tab2_words[0]))
         nc.sync.dma_start(pos_sb[:], pos1)
         nc.sync.dma_start(out=tab2_w[1][:], in_=words_view(tab2_words[1]))
 
@@ -284,7 +284,7 @@ def tile_list_inlining_adviser_kernel(
         w3_c0 = held([P, N], U32, "w3_c0")
         w3_s0 = held([P, N], U8, "w3_s0")
         source = w3_raw[0][:].rearrange("p j (m t) -> p m j t", t=4)
-        for half, copy, on in ((1, nc.vector.tensor_copy, "h3"), (0, nc.scalar.copy, "w2_raw21")):
+        for half, copy, on in ((1, nc.vector.tensor_copy, "h3"), (0, nc.vector.tensor_copy, "w2_raw21")):
             part = held([P, 2 * N], BF16, "w3_bf0%d" % half, on)
             cols = slice(2 * P * half, 2 * P * (half + 1))
             copy(
@@ -328,11 +328,12 @@ def tile_list_inlining_adviser_kernel(
 
         z_c = held([P, M], U32, "z_c2")
         z_s = held([P, M], U8, "z_s2")
+        zb2 = [held([P, 2 * M], BF16, "zb2%d" % i, "h%d" % i) for i in range(2)]
         for q in range(Q):
             cols = slice(P * q, P * (q + 1))
-            zb = held([P, PASS], BF16, "zb2%d" % q)
-            multiply(zb[:], last, q, b_banks[q][:])
-            nc.vector.quantize_mx(out=z_c[:, cols].bitcast(FP8X4), scales=z_s[:, cols], in_=zb[:])
+            zb = zb2[q // 2][:, PASS * (q % 2) : PASS * (q % 2 + 1)]
+            multiply(zb, last, q, b_banks[q][:])
+            nc.vector.quantize_mx(out=z_c[:, cols].bitcast(FP8X4), scales=z_s[:, cols], in_=zb)
             out_passes(q, w3q[1][0], w3q[1][1], 0, zq[1][0], zq[1][1], False, False)
             out_passes(q, w3q[last][0], w3q[last][1], 0, z_c, z_s, False, True)
 
@@ -356,7 +357,8 @@ def tile_list_inlining_adviser_kernel(
             nc.vector.quantize_mx(out=y_c[:, cols].bitcast(FP8X4), scales=y_s[:, cols], in_=yb[:])
             nc.sync.dma_start(out=words_view(out_1[0])[:, cols], in_=y_c[:, cols].bitcast(I32))
         for quad in range(4):
-            nc.sync.dma_start(
+            queue = nc.scalar if quad % 2 else nc.sync
+            queue.dma_start(
                 out=out_2[0, 4 * quad : 4 * quad + 4, :].bitcast(I32),
                 in_=y_s[32 * quad : 32 * quad + 4, :].bitcast(I32),
             )

@@ -15,7 +15,6 @@ FP8X4 = mybir.dt.float8_e4m3fn_x4
 FP4X4 = mybir.dt.float4_e2m1fn_x4
 IDENT = mybir.ActivationFunctionType.Identity
 MULT = mybir.AluOpType.mult
-ADD = mybir.AluOpType.add
 
 P = 128
 PASS = 512
@@ -128,21 +127,15 @@ def tile_list_inlining_adviser_kernel(
         nc.vector.tensor_copy(v_w[1][:], tab_w[:].bitcast(U32).indirect(offs_sb[:, 32:64]))
 
         v2_s = held([P, M], U8, "v2_s")
-        v2_w = [held([P, M], U32, "v2_w%d" % a) for a in range(A)]
         nc.vector.tensor_copy(v2_s[:], tab2_s[:].indirect(offs2_sb[:]))
-        for a in range(A):
-            nc.vector.tensor_copy(v2_w[a][:], tab2_w[a][:].bitcast(U32).indirect(offs2_sb[:]))
 
-        w3_raw.extend([load_w3(1 + a, "tab2_w%d" % a) for a in range(A)])
 
-        h = {}
+        def scope_tile(g, t, on=None):
+            return held([P, S], F32, "h%d" % (4 * g + t), on)
 
-        def scope_half(g, t, c, bank_index):
+        def scope_half(h, g, t, c):
             i = 4 * g + t
-            if i not in h:
-                on = {6: "w2_raw00", 7: "w2_raw01"}.get(i)
-                h.setdefault(i, held([P, S], F32, "h%d" % i, on))
-            bank = psum_bank([P, PASS], bank_index)
+            bank = psum_bank([P, PASS], 2 * t + c)
             nc.tensor.matmul_mx(
                 out=bank[:],
                 lhsT=w1_wd[:, 64 * i : 64 * (i + 1)].bitcast(U8).bitcast(FP4X4),
@@ -153,57 +146,77 @@ def tile_list_inlining_adviser_kernel(
                 stop=True,
             )
             nc.scalar.activation(
-                h[i][:, PASS * c : PASS * (c + 1)], bank[:], IDENT,
+                h[:, PASS * c : PASS * (c + 1)], bank[:], IDENT,
                 bias=bias1[:, g, 4 * t : 4 * t + 1],
             )
 
-        def pick_scope(scopes, g, t):
-            nc.vector.tensor_copy(scopes[:, t, :], h[4 * g + t][:].indirect(pos_sb[:]))
-
         picked = [held([P, 4, M], F32, "picked%d" % g) for g in range(G)]
+
+        def pick_scope(h, g, t):
+            nc.vector.tensor_copy(picked[g][:, t, :], h[:].indirect(pos_sb[:]))
+
+        def scope_slice(g, t, on=None):
+            h = scope_tile(g, t, on)
+            for c in range(2):
+                scope_half(h, g, t, c)
+            pick_scope(h, g, t)
+
+        def gather_calls(a, on):
+            words = held([P, M], U32, "v2_w%d" % a, on)
+            nc.vector.tensor_copy(words[:], tab2_w[a][:].bitcast(U32).indirect(offs2_sb[:]))
+            return words
+
+        first_two = [scope_tile(0, t) for t in range(2)]
         for c in range(2):
             for t in range(2):
-                scope_half(0, t, c, 2 * t + c)
+                scope_half(first_two[t], 0, t, c)
+        pick_scope(first_two[0], 0, 0)
+        v2_w = [gather_calls(0, "h0")]
+        pick_scope(first_two[1], 0, 1)
+        scope_slice(0, 2)
+        v2_w.append(gather_calls(1, "h2"))
+        scope_slice(0, 3)
+        w3_raw.extend([load_w3(1 + a, "tab2_w%d" % a) for a in range(A)])
         for t in range(4):
-            if t >= 2:
-                for c in range(2):
-                    scope_half(0, t, c, 2 * t + c)
-            pick_scope(picked[0], 0, t)
-        for t in range(2):
-            for c in range(2):
-                scope_half(1, t, c, 2 * t + c)
-            pick_scope(picked[1], 1, t)
+            scope_slice(1, t)
 
-        def round_w2(g, a, on):
+        def mx_tiles(name, on=None):
+            return held([P, PASS], U32, name + "_c", on), held([P, PASS], U8, name + "_s")
+
+        def quantise(operand, cols, rounded):
+            codes, scales = operand
+            nc.vector.quantize_mx(
+                out=codes[:, cols].bitcast(FP8X4), scales=scales[:, cols], in_=rounded
+            )
+
+        def quantised(name, rounded, on=None):
+            operand = mx_tiles(name, on)
+            quantise(operand, slice(0, PASS), rounded[:])
+            return operand
+
+        def prepare_w2(g, a, on):
             rounded = held([P, 4 * PASS], BF16, "w2_bf%d%d" % (g, a), on)
             nc.scalar.copy(
                 out=rounded[:].rearrange("p (t u s j) -> p t u j s", t=4, s=4, j=4),
                 in_=w2_raw[g][a][:].rearrange("p j (u t s) -> p t u j s", t=4, s=4),
             )
-            return rounded
+            return quantised("w2_%d%d" % (g, a), rounded)
 
-        def quantise_w2(g, a, rounded):
-            codes = held([P, PASS], U32, "w2_c%d%d" % (g, a))
-            scales = held([P, PASS], U8, "w2_s%d%d" % (g, a))
-            nc.vector.quantize_mx(out=codes[:].bitcast(FP8X4), scales=scales[:], in_=rounded[:])
-            return codes, scales
-
-        def round_w3(g, on):
-            rounded = held([P, 4 * N], BF16, "w3_bf%d" % g, on)
+        def round_w3_half(copy, g, half, rounded):
             source = w3_raw[g][:].rearrange("p j (m t) -> p m j t", t=4)
-            for half in range(2):
-                part = rounded[:, 2 * N * half : 2 * N * (half + 1)]
-                nc.scalar.copy(
-                    out=part.rearrange("p (t m j) -> p m j t", t=2, j=4),
-                    in_=source[:, :, :, 2 * half : 2 * half + 2],
-                )
-            return rounded
+            copy(
+                out=rounded.rearrange("p (t m j) -> p m j t", t=2, j=4),
+                in_=source[:, :, :, 2 * half : 2 * half + 2],
+            )
 
-        def quantise_w3(g, rounded, on):
-            codes = held([P, N], U32, "w3_c%d" % g, on)
-            scales = held([P, N], U8, "w3_s%d" % g)
-            nc.vector.quantize_mx(out=codes[:].bitcast(FP8X4), scales=scales[:], in_=rounded[:])
-            return codes, scales
+        def prepare_w3(g, on):
+            rounded = held([P, 4 * N], BF16, "w3_bf%d" % g, on)
+            for half in range(2):
+                round_w3_half(nc.scalar.copy, g, half, rounded[:, 2 * N * half : 2 * N * (half + 1)])
+            return quantised("w3_%d" % g, rounded)
+
+        def half_columns(half):
+            return slice(PASS // 2 * half, PASS // 2 * (half + 1))
 
         def call_projection(w2_pass, q):
             bank = psum_bank([P, 4, P], q)
@@ -222,27 +235,14 @@ def tile_list_inlining_adviser_kernel(
                     )
             return bank
 
-        def multiply(z_rounded, g, q, bank, engine=nc.vector):
-            engine.tensor_tensor(
+        def multiply(z_rounded, g, q, bank):
+            nc.vector.tensor_tensor(
                 z_rounded.rearrange("p (c i t) -> p c t i", i=2, t=4),
                 picked[g][:, :, P * q : P * (q + 1)].rearrange("p t (c i) -> p c t i", i=2),
-                bank.rearrange("p t (c i) -> p c t i", i=2),
+                bank[:].rearrange("p t (c i) -> p c t i", i=2),
                 MULT,
             )
 
-        def products(g, w2_pass, on):
-            zb = held([P, 4 * M], BF16, "zb%d" % g, on)
-            for q in range(Q):
-                multiply(zb[:, PASS * q : PASS * (q + 1)], g, q, call_projection(w2_pass, q)[:])
-            return zb
-
-        def quantise_z(g, zb, on):
-            codes = held([P, M], U32, "z_c%d" % g, on)
-            scales = held([P, M], U8, "z_s%d" % g)
-            nc.vector.quantize_mx(out=codes[:].bitcast(FP8X4), scales=scales[:], in_=zb[:])
-            return codes, scales
-
-        last = G - 1
         w4_wd = held([P, A, N], I32, "w4_wd")
         w4_sd = held([P, N], U8, "w4_sd")
         nc.vector.tensor_copy(
@@ -254,88 +254,73 @@ def tile_list_inlining_adviser_kernel(
             in_=w4_s[:].rearrange("p (c i t) -> p c t i", t=4, i=16),
         )
 
-        nc.gpsimd.tensor_tensor(gby[:], gy_sb[:], by_sb[:], MULT)
+        nc.vector.tensor_tensor(gby[:], gy_sb[:], by_sb[:], MULT)
 
-        w2q = [quantise_w2(0, a, round_w2(0, a, "h%d" % a)) for a in range(A)]
-        for t in range(2, 4):
-            for c in range(2):
-                scope_half(1, t, c, 2 * t + c)
-            pick_scope(picked[1], 1, t)
-        for t in range(4):
-            for c in range(2):
-                scope_half(2, t, c, 2 * t + c)
-            pick_scope(picked[2], 2, t)
-        zb0 = products(0, w2q, "h11")
-        w2q = [quantise_w2(1, a, round_w2(1, a, "h%d" % (2 + a))) for a in range(A)]
-        w2q_next = []
-        zb1 = []
-        for a in range(A):
-            w2q_next.append(quantise_w2(2, a, round_w2(2, a, "h%d" % (4 + a))))
-            if a == 0:
-                zq = [quantise_z(0, zb0, "w2_raw20")]
-            half = held([P, 2 * M], BF16, "zb1%d" % a, "h%d" % (4 + a))
+        w2q = [prepare_w2(0, 0, "tab_w"), prepare_w2(0, 1, "h1")]
+        scope_slice(2, 0, "w2_raw00")
+        scope_slice(2, 1, "w2_raw01")
+        scope_slice(2, 2)
+        scope_slice(2, 3)
+        zb0 = held([P, 4 * M], BF16, "zb0", "h11")
+        for q in range(Q):
+            multiply(zb0[:, PASS * q : PASS * (q + 1)], 0, q, call_projection(w2q, q))
+
+        w2q = [prepare_w2(1, 0, "h7"), prepare_w2(1, 1, "h3")]
+        w2q_last = [prepare_w2(2, 0, "h4")]
+        z0 = quantised("z0", zb0, "w2_raw20")
+
+        def half_products_1(half, on):
+            zb = held([P, 2 * M], BF16, "zb1%d" % half, on)
             for i in range(2):
-                q = 2 * a + i
-                multiply(half[:, PASS * i : PASS * (i + 1)], 1, q, call_projection(w2q, q)[:])
-            zb1.append(half)
-        w2q = w2q_next
-        z1_c = held([P, M], U32, "z_c1")
-        z1_s = held([P, M], U8, "z_s1")
-        w3_c0 = held([P, N], U32, "w3_c0")
-        w3_s0 = held([P, N], U8, "w3_s0")
-        source = w3_raw[0][:].rearrange("p j (m t) -> p m j t", t=4)
-        for half, copy, on in ((1, nc.vector.tensor_copy, "h3"), (0, nc.vector.tensor_copy, "w2_raw21")):
-            part = held([P, 2 * N], BF16, "w3_bf0%d" % half, on)
-            cols = slice(2 * P * half, 2 * P * (half + 1))
-            copy(
-                out=part[:].rearrange("p (t m j) -> p m j t", t=2, j=4),
-                in_=source[:, :, :, 2 * half : 2 * half + 2],
-            )
-            nc.vector.quantize_mx(
-                out=w3_c0[:, cols].bitcast(FP8X4), scales=w3_s0[:, cols], in_=part[:]
-            )
-        w3q = [(w3_c0, w3_s0)]
-        w3q.append(quantise_w3(1, round_w3(1, "h0"), None))
-        for a in range(A):
-            cols = slice(M // 2 * a, M // 2 * (a + 1))
-            nc.vector.quantize_mx(
-                out=z1_c[:, cols].bitcast(FP8X4), scales=z1_s[:, cols], in_=zb1[a][:]
-            )
-        zq.append((z1_c, z1_s))
-        w3q.append(quantise_w3(2, round_w3(2, "h1"), None))
-        b_banks = [call_projection(w2q, q) for q in range(Q)]
+                q = 2 * half + i
+                multiply(zb[:, PASS * i : PASS * (i + 1)], 1, q, call_projection(w2q, q))
+            return zb
+
+        zb1 = [half_products_1(0, "h4")]
+        w2q_last.append(prepare_w2(2, 1, "h5"))
+        zb1.append(half_products_1(1, "h5"))
+
+        z1 = mx_tiles("z1")
+        w3q = [mx_tiles("w3_0")]
+        for half, copy, on in ((1, nc.vector.tensor_copy, "h3"), (0, nc.scalar.copy, "w2_raw21")):
+            rounded = held([P, 2 * N], BF16, "w3_bf0%d" % half, on)
+            round_w3_half(copy, 0, half, rounded[:])
+            quantise(w3q[0], half_columns(half), rounded[:])
+        w3q.append(prepare_w3(1, "tab_w"))
+        for half in range(2):
+            quantise(z1, half_columns(half), zb1[half][:])
+        w3q.append(prepare_w3(2, "h1"))
+        b_banks = [call_projection(w2q_last, q) for q in range(Q)]
 
         banks = [psum_bank([P, 4, P], Q + q) for q in range(Q)]
 
-        def out_passes(q, codes, scales, row, moving, moving_scales, first, final):
+        def out_passes(q, weight, moving, row=0, first=False, final=False):
             cols = slice(P * q, P * (q + 1))
             for t in range(4):
                 nc.tensor.matmul_mx(
                     out=banks[q][:, t, :],
-                    lhsT=codes[:, P * t : P * (t + 1)].bitcast(FP8X4),
-                    lhsT_scale=scales[row:P, P * t : P * (t + 1)],
-                    rhs=moving[:, cols].bitcast(FP8X4),
-                    rhs_scale=moving_scales[row:P, cols],
+                    lhsT=weight[0][:, P * t : P * (t + 1)].bitcast(FP8X4),
+                    lhsT_scale=weight[1][row:P, P * t : P * (t + 1)],
+                    rhs=moving[0][:, cols].bitcast(FP8X4),
+                    rhs_scale=moving[1][row:P, cols],
                     start=(first and t == 0),
                     stop=(final and t == 3),
                 )
 
         for q in range(Q):
             for a in range(A):
-                out_passes(q, w4_wd[:, a, :], w4_sd, 4 * a, v2_w[a], v2_s, a == 0, False)
+                out_passes(q, (w4_wd[:, a, :], w4_sd), (v2_w[a], v2_s), 4 * a, first=(a == 0))
         for q in range(Q):
-            out_passes(q, w3q[0][0], w3q[0][1], 0, zq[0][0], zq[0][1], False, False)
+            out_passes(q, w3q[0], z0)
 
-        z_c = held([P, M], U32, "z_c2")
-        z_s = held([P, M], U8, "z_s2")
-        zb2 = [held([P, 2 * M], BF16, "zb2%d" % i, "h%d" % i) for i in range(2)]
+        z2 = mx_tiles("z2")
+        zb2 = [held([P, 2 * M], BF16, "zb20", "tab_w"), held([P, 2 * M], BF16, "zb21", "h1")]
         for q in range(Q):
-            cols = slice(P * q, P * (q + 1))
             zb = zb2[q // 2][:, PASS * (q % 2) : PASS * (q % 2 + 1)]
-            multiply(zb, last, q, b_banks[q][:])
-            nc.vector.quantize_mx(out=z_c[:, cols].bitcast(FP8X4), scales=z_s[:, cols], in_=zb)
-            out_passes(q, w3q[1][0], w3q[1][1], 0, zq[1][0], zq[1][1], False, False)
-            out_passes(q, w3q[last][0], w3q[last][1], 0, z_c, z_s, False, True)
+            multiply(zb, 2, q, b_banks[q])
+            quantise(z2, slice(P * q, P * (q + 1)), zb)
+            out_passes(q, w3q[1], z1)
+            out_passes(q, w3q[2], z2, final=True)
 
         y_c = held([P, M], U32, "y_c")
         y_s = held([P, M], U8, "y_s")

@@ -15,6 +15,7 @@ FP8X4 = mybir.dt.float8_e4m3fn_x4
 FP4X4 = mybir.dt.float4_e2m1fn_x4
 IDENT = mybir.ActivationFunctionType.Identity
 MULT = mybir.AluOpType.mult
+ADD = mybir.AluOpType.add
 
 P = 128
 PASS = 512
@@ -202,9 +203,9 @@ def tile_list_inlining_adviser_kernel(
             )
             return quantised("w2_%d%d" % (g, a), rounded)
 
-        def round_w3_half(copy, g, half, rounded):
+        def round_w3_half(g, half, rounded):
             source = w3_raw[g][:].rearrange("p j (m t) -> p m j t", t=4)
-            copy(
+            nc.scalar.copy(
                 out=rounded.rearrange("p (t m j) -> p m j t", t=2, j=4),
                 in_=source[:, :, :, 2 * half : 2 * half + 2],
             )
@@ -212,7 +213,7 @@ def tile_list_inlining_adviser_kernel(
         def prepare_w3(g, on):
             rounded = held([P, 4 * N], BF16, "w3_bf%d" % g, on)
             for half in range(2):
-                round_w3_half(nc.scalar.copy, g, half, rounded[:, 2 * N * half : 2 * N * (half + 1)])
+                round_w3_half(g, half, rounded[:, 2 * N * half : 2 * N * (half + 1)])
             return quantised("w3_%d" % g, rounded)
 
         def half_columns(half):
@@ -261,6 +262,12 @@ def tile_list_inlining_adviser_kernel(
         scope_slice(2, 1, "w2_raw01")
         scope_slice(2, 2)
         scope_slice(2, 3)
+        w3_bf01 = held([P, 2 * N], BF16, "w3_bf01", "h10")
+        dealt = w3_bf01[:].rearrange("p (t m j) -> p m t j", t=2, j=4)
+        source = w3_raw[0][:].rearrange("p j (m t) -> p m t j", t=4)
+        for c in range(2):
+            part = slice(P // 2 * c, P // 2 * (c + 1))
+            nc.gpsimd.tensor_scalar(dealt[:, part], source[:, part, 2:4], 1.0, 0.0, MULT, ADD)
         zb0 = held([P, 4 * M], BF16, "zb0", "h11")
         for q in range(Q):
             multiply(zb0[:, PASS * q : PASS * (q + 1)], 0, q, call_projection(w2q, q))
@@ -281,11 +288,11 @@ def tile_list_inlining_adviser_kernel(
         zb1.append(half_products_1(1, "h5"))
 
         z1 = mx_tiles("z1")
-        w3q = [mx_tiles("w3_0")]
-        for half, copy, on in ((1, nc.vector.tensor_copy, "h3"), (0, nc.scalar.copy, "w2_raw21")):
-            rounded = held([P, 2 * N], BF16, "w3_bf0%d" % half, on)
-            round_w3_half(copy, 0, half, rounded[:])
-            quantise(w3q[0], half_columns(half), rounded[:])
+        w3q = [mx_tiles("w3_0", "h3")]
+        quantise(w3q[0], half_columns(1), w3_bf01[:])
+        w3_bf00 = held([P, 2 * N], BF16, "w3_bf00", "w2_raw21")
+        round_w3_half(0, 0, w3_bf00[:])
+        quantise(w3q[0], half_columns(0), w3_bf00[:])
         w3q.append(prepare_w3(1, "tab_w"))
         for half in range(2):
             quantise(z1, half_columns(half), zb1[half][:])

@@ -21,6 +21,8 @@ P = 128
 PASS = 512
 G = H // PASS
 A = K2 // PASS
+SHARE = 96
+SLICES = [(0, 0), (0, 1), (1, 0), (1, 1), (2, 0), (2, 1), (0, 2), (0, 3), (1, 2), (1, 3), (2, 2), (2, 3)]
 Q = M // P
 
 
@@ -84,9 +86,14 @@ def tile_list_inlining_adviser_kernel(
             load_bias1(s)
         nc.sync.dma_start(offs2_sb[:], offs2)
         load_scale_rows(tab2_s, tab2_scales)
-        nc.sync.dma_start(out=tab2_w[0][:], in_=words_view(tab2_words[0]))
         nc.sync.dma_start(pos_sb[:], pos1)
-        nc.sync.dma_start(out=tab2_w[1][:], in_=words_view(tab2_words[1]))
+        for a in range(A):
+            nc.sync.dma_start(out=tab2_w[a][:], in_=words_view(tab2_words[a]))
+
+        warm_in = held([P, 1], F32, "warm_in")
+        warm_out = held([P, 1], F32, "warm_out")
+        nc.vector.memset(warm_in[:], 0.0)
+        nc.scalar.activation(warm_out[:], warm_in[:], IDENT)
 
         def load_w2(g, a):
             raw = held([P, 4, PASS], F32, "w2_raw%d%d" % (g, a))
@@ -101,28 +108,27 @@ def tile_list_inlining_adviser_kernel(
                 nc.sync.dma_start(out=raw[:, j, :], in_=rows[j])
             return raw
 
-        w2_raw = [[load_w2(0, a) for a in range(A)]]
+        w2_raw = [[load_w2(g, a) for a in range(A)] for g in range(2)]
+        w3_raw = {0: load_w3(0, None)}
         load_scale_rows(w4_s, w4_scales)
         nc.sync.dma_start(out=w4_w[:], in_=w4_words.rearrange("a p c i -> p a (c i)").bitcast(I32))
         nc.sync.dma_start(out=gy_sb[:], in_=gy.rearrange("(p t) -> p t", t=4))
         nc.sync.dma_start(out=by_sb[:], in_=by.rearrange("(p t) -> p t", t=4))
-        w2_raw.append([load_w2(1, a) for a in range(A)])
-        w3_raw = [load_w3(0, None)]
         w2_raw.append([load_w2(2, a) for a in range(A)])
 
-        w1_wd = held([P, H // 2], I32, "w1_wd")
-        w1_sd = held([P, H], U8, "w1_sd")
-        nc.vector.tensor_copy(
-            out=w1_wd[:].rearrange("p (g t u i) -> p t g u i", g=G, t=4, i=2),
-            in_=w1_w[:].rearrange("p (g u t i) -> p t g u i", g=G, t=4, i=2),
-        )
         v_s = held([P, S], U8, "v_s")
         v_w = [held([P, PASS], U32, "v_w0")]
         nc.vector.tensor_copy(v_s[:], tab_s[:].indirect(offs_sb[:]))
         nc.vector.tensor_copy(v_w[0][:], tab_w[:].bitcast(U32).indirect(offs_sb[:, 0:32]))
+        w1_wd = held([P, H // 2], I32, "w1_wd")
+        w1_sd = held([P, H], U8, "w1_sd")
         nc.vector.tensor_copy(
             out=w1_sd[:].bitcast(I32).rearrange("p (g t c i) -> p c g t i", g=G, t=4, i=4),
             in_=w1_s[:].bitcast(I32).rearrange("p (g c i t) -> p c g t i", g=G, t=4, i=4),
+        )
+        nc.vector.tensor_copy(
+            out=w1_wd[:].rearrange("p (g t u i) -> p t g u i", g=G, t=4, i=2),
+            in_=w1_w[:].rearrange("p (g u t i) -> p t g u i", g=G, t=4, i=2),
         )
         v_w.append(held([P, PASS], U32, "v_w1", "w1_s"))
         nc.vector.tensor_copy(v_w[1][:], tab_w[:].bitcast(U32).indirect(offs_sb[:, 32:64]))
@@ -131,12 +137,10 @@ def tile_list_inlining_adviser_kernel(
         nc.vector.tensor_copy(v2_s[:], tab2_s[:].indirect(offs2_sb[:]))
 
 
-        def scope_tile(g, t, on=None):
-            return held([P, S], F32, "h%d" % (4 * g + t), on)
-
-        def scope_half(h, g, t, c):
+        def scope_half(h, n, c):
+            g, t = SLICES[n]
             i = 4 * g + t
-            bank = psum_bank([P, PASS], 2 * t + c)
+            bank = psum_bank([P, PASS], (2 * (n % 4) if n < 6 else Q + 2 * (n % 2)) + c)
             nc.tensor.matmul_mx(
                 out=bank[:],
                 lhsT=w1_wd[:, 64 * i : 64 * (i + 1)].bitcast(U8).bitcast(FP4X4),
@@ -153,33 +157,31 @@ def tile_list_inlining_adviser_kernel(
 
         picked = [held([P, 4, M], F32, "picked%d" % g) for g in range(G)]
 
-        def pick_scope(h, g, t):
-            nc.vector.tensor_copy(picked[g][:, t, :], h[:].indirect(pos_sb[:]))
+        def pick_scope(h, n):
+            g, t = SLICES[n]
+            nc.vector.tensor_copy(picked[g][:, t, :], h.indirect(pos_sb[:]))
 
-        def scope_slice(g, t, on=None):
-            h = scope_tile(g, t, on)
+        def scope_slice(n, h=None):
+            if h is None:
+                h = held([P, S], F32, "h%d" % n)[:]
             for c in range(2):
-                scope_half(h, g, t, c)
-            pick_scope(h, g, t)
+                scope_half(h, n, c)
+            pick_scope(h, n)
 
-        def gather_calls(a, on):
-            words = held([P, M], U32, "v2_w%d" % a, on)
+        def gather_calls(a):
+            words = held([P, M], U32, "v2_w%d" % a)
             nc.vector.tensor_copy(words[:], tab2_w[a][:].bitcast(U32).indirect(offs2_sb[:]))
             return words
 
-        first_two = [scope_tile(0, t) for t in range(2)]
+        first_two = [held([P, S], F32, "h%d" % n)[:] for n in range(2)]
         for c in range(2):
             for t in range(2):
-                scope_half(first_two[t], 0, t, c)
-        pick_scope(first_two[0], 0, 0)
-        v2_w = [gather_calls(0, "h0")]
-        pick_scope(first_two[1], 0, 1)
-        scope_slice(0, 2)
-        v2_w.append(gather_calls(1, "h2"))
-        scope_slice(0, 3)
-        w3_raw.extend([load_w3(1 + a, "tab2_w%d" % a) for a in range(A)])
-        for t in range(4):
-            scope_slice(1, t)
+                scope_half(first_two[t], t, c)
+        for t in range(2):
+            pick_scope(first_two[t], t)
+        v2_w = [gather_calls(a) for a in range(A)]
+        w3_raw[2] = load_w3(2, "tab2_w0")
+        w3_raw[1] = load_w3(1, "tab2_w1")
 
         def mx_tiles(name, on=None):
             return held([P, PASS], U32, name + "_c", on), held([P, PASS], U8, name + "_s")
@@ -195,32 +197,39 @@ def tile_list_inlining_adviser_kernel(
             quantise(operand, slice(0, PASS), rounded[:])
             return operand
 
-        def prepare_w2(g, a, on):
+        def round_w2(g, a, on):
             rounded = held([P, 4 * PASS], BF16, "w2_bf%d%d" % (g, a), on)
             nc.scalar.copy(
                 out=rounded[:].rearrange("p (t u s j) -> p t u j s", t=4, s=4, j=4),
                 in_=w2_raw[g][a][:].rearrange("p j (u t s) -> p t u j s", t=4, s=4),
             )
-            return quantised("w2_%d%d" % (g, a), rounded)
+            return rounded
 
-        def round_w3_half(g, half, rounded):
+        def prepare_w2(g, a, on):
+            return quantised("w2_%d%d" % (g, a), round_w2(g, a, on))
+
+        def round_w3(g, rounded, columns):
             source = w3_raw[g][:].rearrange("p j (m t) -> p m j t", t=4)
-            nc.scalar.copy(
-                out=rounded.rearrange("p (t m j) -> p m j t", t=2, j=4),
-                in_=source[:, :, :, 2 * half : 2 * half + 2],
-            )
-
-        def prepare_w3(g, on):
-            rounded = held([P, 4 * N], BF16, "w3_bf%d" % g, on)
+            dealt = rounded[:].rearrange("p (t m j) -> p m j t", t=4, j=4)
             for half in range(2):
-                round_w3_half(g, half, rounded[:, 2 * N * half : 2 * N * (half + 1)])
-            return quantised("w3_%d" % g, rounded)
+                pair = slice(2 * half, 2 * half + 2)
+                nc.scalar.copy(out=dealt[:, columns, :, pair], in_=source[:, columns, :, pair])
 
-        def half_columns(half):
-            return slice(PASS // 2 * half, PASS // 2 * (half + 1))
+        def round_w3_beside_products(g, on):
+            rounded = held([P, 4 * N], BF16, "w3_bf%d" % g, on)
+            dealt = rounded[:].rearrange("p (t m j) -> p m t j", t=4, j=4)
+            source = w3_raw[g][:].rearrange("p j (m t) -> p m t j", t=4)
+            part = slice(0, SHARE)
+            nc.gpsimd.tensor_scalar(dealt[:, part], source[:, part], 1.0, 0.0, MULT, ADD)
+            return rounded
+
+        def last_two_slices(g):
+            pair = held([P, 2, S], F32, "h_pair%d" % g, "w2_raw%d1" % g)
+            for i in range(2):
+                scope_slice(6 + 2 * g + i, pair[:, i, :])
 
         def call_projection(w2_pass, q):
-            bank = psum_bank([P, 4, P], q)
+            bank = psum_bank([P, 4, P], Q + q)
             cols = slice(P * q, P * (q + 1))
             for t in range(4):
                 for a in range(A):
@@ -244,62 +253,21 @@ def tile_list_inlining_adviser_kernel(
                 MULT,
             )
 
-        w4_wd = held([P, A, N], I32, "w4_wd")
-        w4_sd = held([P, N], U8, "w4_sd")
-        nc.vector.tensor_copy(
-            out=w4_wd[:].rearrange("p a (t c i) -> p a c t i", t=4, i=4),
-            in_=w4_w[:].rearrange("p a (c i t) -> p a c t i", t=4, i=4),
-        )
-        nc.vector.tensor_copy(
-            out=w4_sd[:].rearrange("p (t c i) -> p c t i", t=4, i=16),
-            in_=w4_s[:].rearrange("p (c i t) -> p c t i", t=4, i=16),
-        )
-
-        nc.vector.tensor_tensor(gby[:], gy_sb[:], by_sb[:], MULT)
-
-        w2q = [prepare_w2(0, 0, "tab_w"), prepare_w2(0, 1, "h1")]
-        scope_slice(2, 0, "w2_raw00")
-        scope_slice(2, 1, "w2_raw01")
-        scope_slice(2, 2)
-        scope_slice(2, 3)
-        w3_bf01 = held([P, 2 * N], BF16, "w3_bf01", "h10")
-        dealt = w3_bf01[:].rearrange("p (t m j) -> p m t j", t=2, j=4)
-        source = w3_raw[0][:].rearrange("p j (m t) -> p m t j", t=4)
-        for c in range(2):
-            part = slice(P // 2 * c, P // 2 * (c + 1))
-            nc.gpsimd.tensor_scalar(dealt[:, part], source[:, part, 2:4], 1.0, 0.0, MULT, ADD)
-        zb0 = held([P, 4 * M], BF16, "zb0", "h11")
-        for q in range(Q):
-            multiply(zb0[:, PASS * q : PASS * (q + 1)], 0, q, call_projection(w2q, q))
-
-        w2q = [prepare_w2(1, 0, "h7"), prepare_w2(1, 1, "h3")]
-        w2q_last = [prepare_w2(2, 0, "h4")]
-        z0 = quantised("z0", zb0, "w2_raw20")
-
-        def half_products_1(half, on):
-            zb = held([P, 2 * M], BF16, "zb1%d" % half, on)
-            for i in range(2):
-                q = 2 * half + i
-                multiply(zb[:, PASS * i : PASS * (i + 1)], 1, q, call_projection(w2q, q))
+        def products(g, w2_pass, on):
+            zb = held([P, 4 * M], BF16, "zb%d" % g, on)
+            for q in range(Q):
+                multiply(zb[:, PASS * q : PASS * (q + 1)], g, q, call_projection(w2_pass, q))
             return zb
 
-        zb1 = [half_products_1(0, "h4")]
-        w2q_last.append(prepare_w2(2, 1, "h5"))
-        zb1.append(half_products_1(1, "h5"))
+        for n in range(2, 6):
+            scope_slice(n)
+        w2q = [prepare_w2(0, 0, "tab_w"), prepare_w2(0, 1, "h0")]
 
-        z1 = mx_tiles("z1")
-        w3q = [mx_tiles("w3_0", "h3")]
-        quantise(w3q[0], half_columns(1), w3_bf01[:])
-        w3_bf00 = held([P, 2 * N], BF16, "w3_bf00", "w2_raw21")
-        round_w3_half(0, 0, w3_bf00[:])
-        quantise(w3q[0], half_columns(0), w3_bf00[:])
-        w3q.append(prepare_w3(1, "tab_w"))
-        for half in range(2):
-            quantise(z1, half_columns(half), zb1[half][:])
-        w3q.append(prepare_w3(2, "h1"))
-        b_banks = [call_projection(w2q_last, q) for q in range(Q)]
+        last_two_slices(0)
+        w3_bf0 = round_w3_beside_products(0, "w2_raw01")
+        zb0 = products(0, w2q, "h3")
 
-        banks = [psum_bank([P, 4, P], Q + q) for q in range(Q)]
+        banks = [psum_bank([P, 4, P], q) for q in range(Q)]
 
         def out_passes(q, weight, moving, row=0, first=False, final=False):
             cols = slice(P * q, P * (q + 1))
@@ -314,20 +282,59 @@ def tile_list_inlining_adviser_kernel(
                     stop=(final and t == 3),
                 )
 
+        w2q = [prepare_w2(1, 0, "h1")]
+        z0 = quantised("z0", zb0, "w2_raw10")
+        w2q.append(prepare_w2(1, 1, "h2"))
+        last_two_slices(1)
+        w3_bf2 = round_w3_beside_products(2, "w2_raw11")
+        zb1 = products(1, w2q, "h4")
+        w4_wd = held([P, A, N], I32, "w4_wd")
+        w4_sd = held([P, N], U8, "w4_sd")
+        nc.vector.tensor_copy(
+            out=w4_wd[:].rearrange("p a (t c i) -> p a c t i", t=4, i=4),
+            in_=w4_w[:].rearrange("p a (c i t) -> p a c t i", t=4, i=4),
+        )
+        nc.vector.tensor_copy(
+            out=w4_sd[:].rearrange("p (t c i) -> p c t i", t=4, i=16),
+            in_=w4_s[:].rearrange("p (c i t) -> p c t i", t=4, i=16),
+        )
+
+        nc.vector.tensor_tensor(gby[:], gy_sb[:], by_sb[:], MULT)
+
         for q in range(Q):
             for a in range(A):
                 out_passes(q, (w4_wd[:, a, :], w4_sd), (v2_w[a], v2_s), 4 * a, first=(a == 0))
+        round_w3(0, w3_bf0, slice(SHARE, P))
+
+        w2_bf20 = round_w2(2, 0, "h5")
+        both = held([P, 2, PASS], U32, "w3_0_z1_c", "w2_raw20")
+        w3q0 = (both[:, 0, :], held([P, PASS], U8, "w3_0_s"))
+        quantise(w3q0, slice(0, PASS), w3_bf0[:])
         for q in range(Q):
-            out_passes(q, w3q[0], z0)
+            out_passes(q, w3q0, z0)
+        w2q = [quantised("w2_20", w2_bf20)]
+        z1 = (both[:, 1, :], held([P, PASS], U8, "z1_s"))
+        quantise(z1, slice(0, PASS), zb1[:])
+        w2q.append(prepare_w2(2, 1, "h0"))
+        last_two_slices(2)
+        b_banks = [call_projection(w2q, q) for q in range(Q)]
+        round_w3(2, w3_bf2, slice(SHARE, P))
+        w3q2 = quantised("w3_2", w3_bf2)
+        w3_bf1 = held([P, 4 * N], BF16, "w3_bf1", "h1")
+        round_w3(1, w3_bf1, slice(0, P))
+
+        w3q1 = quantised("w3_1", w3_bf1)
+        for q in range(Q):
+            out_passes(q, w3q1, z1)
 
         z2 = mx_tiles("z2")
-        zb2 = [held([P, 2 * M], BF16, "zb20", "tab_w"), held([P, 2 * M], BF16, "zb21", "h1")]
-        for q in range(Q):
-            zb = zb2[q // 2][:, PASS * (q % 2) : PASS * (q % 2 + 1)]
-            multiply(zb, 2, q, b_banks[q])
-            quantise(z2, slice(P * q, P * (q + 1)), zb)
-            out_passes(q, w3q[1], z1)
-            out_passes(q, w3q[2], z2, final=True)
+        zb2 = held([P, 4 * M], BF16, "zb2", "tab2_w1")
+        for q in range(Q + 1):
+            if q < Q:
+                multiply(zb2[:, PASS * q : PASS * (q + 1)], 2, q, b_banks[q])
+            if q > 0:
+                quantise(z2, slice(P * (q - 1), P * q), zb2[:, PASS * (q - 1) : PASS * q])
+                out_passes(q - 1, w3q2, z2, final=True)
 
         y_c = held([P, M], U32, "y_c")
         y_s = held([P, M], U8, "y_s")

@@ -21,8 +21,8 @@ P = 128
 PASS = 512
 G = H // PASS
 A = K2 // PASS
-SHARE = 96
-SLICES = [(0, 0), (0, 1), (1, 0), (1, 1), (2, 0), (2, 1), (0, 2), (0, 3), (1, 2), (1, 3), (2, 2), (2, 3)]
+SHARE = 80
+SLICES = [(2, 0), (2, 1), (2, 2), (2, 3), (0, 0), (0, 1), (1, 0), (1, 1), (0, 2), (0, 3), (1, 2), (1, 3)]
 Q = M // P
 
 
@@ -140,7 +140,7 @@ def tile_list_inlining_adviser_kernel(
         def scope_half(h, n, c):
             g, t = SLICES[n]
             i = 4 * g + t
-            bank = psum_bank([P, PASS], (2 * (n % 4) if n < 6 else Q + 2 * (n % 2)) + c)
+            bank = psum_bank([P, PASS], 2 * (n % 4) + c)
             nc.tensor.matmul_mx(
                 out=bank[:],
                 lhsT=w1_wd[:, 64 * i : 64 * (i + 1)].bitcast(U8).bitcast(FP4X4),
@@ -219,14 +219,17 @@ def tile_list_inlining_adviser_kernel(
             rounded = held([P, 4 * N], BF16, "w3_bf%d" % g, on)
             dealt = rounded[:].rearrange("p (t m j) -> p m t j", t=4, j=4)
             source = w3_raw[g][:].rearrange("p j (m t) -> p m t j", t=4)
-            part = slice(0, SHARE)
-            nc.gpsimd.tensor_scalar(dealt[:, part], source[:, part], 1.0, 0.0, MULT, ADD)
+            for half in range(2):
+                pair = slice(2 * half, 2 * half + 2)
+                nc.gpsimd.tensor_scalar(
+                    dealt[:, 0:SHARE, pair], source[:, 0:SHARE, pair], 1.0, 0.0, MULT, ADD
+                )
             return rounded
 
         def last_two_slices(g):
             pair = held([P, 2, S], F32, "h_pair%d" % g, "w2_raw%d1" % g)
             for i in range(2):
-                scope_slice(6 + 2 * g + i, pair[:, i, :])
+                scope_slice(8 + 2 * g + i, pair[:, i, :])
 
         def call_projection(w2_pass, q):
             bank = psum_bank([P, 4, P], Q + q)
@@ -259,7 +262,7 @@ def tile_list_inlining_adviser_kernel(
                 multiply(zb[:, PASS * q : PASS * (q + 1)], g, q, call_projection(w2_pass, q))
             return zb
 
-        for n in range(2, 6):
+        for n in range(2, 8):
             scope_slice(n)
         w2q = [prepare_w2(0, 0, "tab_w"), prepare_w2(0, 1, "h0")]
 
@@ -316,7 +319,6 @@ def tile_list_inlining_adviser_kernel(
         z1 = (both[:, 1, :], held([P, PASS], U8, "z1_s"))
         quantise(z1, slice(0, PASS), zb1[:])
         w2q.append(prepare_w2(2, 1, "h0"))
-        last_two_slices(2)
         b_banks = [call_projection(w2q, q) for q in range(Q)]
         round_w3(2, w3_bf2, slice(SHARE, P))
         w3q2 = quantised("w3_2", w3_bf2)
@@ -324,8 +326,6 @@ def tile_list_inlining_adviser_kernel(
         round_w3(1, w3_bf1, slice(0, P))
 
         w3q1 = quantised("w3_1", w3_bf1)
-        for q in range(Q):
-            out_passes(q, w3q1, z1)
 
         z2 = mx_tiles("z2")
         zb2 = held([P, 4 * M], BF16, "zb2", "tab2_w1")
@@ -334,6 +334,7 @@ def tile_list_inlining_adviser_kernel(
                 multiply(zb2[:, PASS * q : PASS * (q + 1)], 2, q, b_banks[q])
             if q > 0:
                 quantise(z2, slice(P * (q - 1), P * q), zb2[:, PASS * (q - 1) : PASS * q])
+                out_passes(q - 1, w3q1, z1)
                 out_passes(q - 1, w3q2, z2, final=True)
 
         y_c = held([P, M], U32, "y_c")
@@ -354,7 +355,11 @@ def tile_list_inlining_adviser_kernel(
                 in_=y[:].rearrange("p t (c i) -> p c t i", i=2),
             )
             nc.vector.quantize_mx(out=y_c[:, cols].bitcast(FP8X4), scales=y_s[:, cols], in_=yb[:])
-            nc.sync.dma_start(out=words_view(out_1[0])[:, cols], in_=y_c[:, cols].bitcast(I32))
+            if q % 2:
+                cols = slice(P * (q - 1), P * (q + 1))
+                nc.sync.dma_start(
+                    out=words_view(out_1[0])[:, cols], in_=y_c[:, cols].bitcast(I32)
+                )
         for quad in range(4):
             queue = nc.scalar if quad % 2 else nc.sync
             queue.dma_start(

@@ -63,8 +63,10 @@ def tile_list_inlining_adviser_kernel(
         tab2_w = [held([P, T2], I32, "tab2_w%d" % a) for a in range(A)]
         w4_w = held([P, A, N], I32, "w4_w")
         w4_s = held([P, N], U8, "w4_s")
-        for scale_tile in (tab_s, w1_s, tab2_s, w4_s):
+        for scale_tile in (tab_s, w1_s):
             nc.gpsimd.memset(scale_tile[:].bitcast(I32), 0)
+        for scale_tile in (tab2_s, w4_s):
+            nc.vector.memset(scale_tile[:].bitcast(I32), 0)
 
         bias1 = held([P, G, 16], F32, "bias1")
         by_sb = held([P, 4], F32, "by_sb")
@@ -73,22 +75,23 @@ def tile_list_inlining_adviser_kernel(
 
         b1_view = b1.rearrange("(g u k) -> u g k", g=G, k=16)
 
-        def load_bias1(s):
-            nc.sync.dma_start(out=bias1[s:P:4, :, 0:13], in_=b1_view[:, :, s : s + 13])
+        def load_bias1(s, queue):
+            queue.dma_start(out=bias1[s:P:4, :, 0:13], in_=b1_view[:, :, s : s + 13])
 
         nc.sync.dma_start(offs_sb[:], offs)
         nc.sync.dma_start(out=w1_w[:], in_=w1_words[0].bitcast(I32))
-        load_bias1(0)
+        load_bias1(0, nc.sync)
         load_scale_rows(tab_s, tab_scales)
         nc.sync.dma_start(out=tab_w[:], in_=words_view(tab_words[0]))
         load_scale_rows(w1_s, w1_scales)
-        for s in range(1, 4):
-            load_bias1(s)
+        load_bias1(1, nc.sync)
+        for s in range(2, 4):
+            load_bias1(s, nc.gpsimd)
         nc.sync.dma_start(offs2_sb[:], offs2)
-        load_scale_rows(tab2_s, tab2_scales)
+        nc.sync.dma_start(out=tab2_w[0][:], in_=words_view(tab2_words[0]))
         nc.sync.dma_start(pos_sb[:], pos1)
-        for a in range(A):
-            nc.sync.dma_start(out=tab2_w[a][:], in_=words_view(tab2_words[a]))
+        load_scale_rows(tab2_s, tab2_scales)
+        nc.sync.dma_start(out=tab2_w[1][:], in_=words_view(tab2_words[1]))
 
         warm_in = held([P, 1], F32, "warm_in")
         warm_out = held([P, 1], F32, "warm_out")

@@ -21,7 +21,7 @@ P = 128
 PASS = 512
 G = H // PASS
 A = K2 // PASS
-SHARE = 80
+SHARE = 64
 SLICES = [(2, 0), (2, 1), (2, 2), (2, 3), (0, 0), (0, 1), (1, 0), (1, 1), (0, 2), (0, 3), (1, 2), (1, 3)]
 Q = M // P
 
@@ -162,7 +162,11 @@ def tile_list_inlining_adviser_kernel(
 
         def pick_scope(h, n):
             g, t = SLICES[n]
-            nc.vector.tensor_copy(picked[g][:, t, :], h.indirect(pos_sb[:]))
+            parts = 2 if n in (9, 11) else 1
+            for i in range(parts):
+                entries = slice(M // parts * i, M // parts * (i + 1))
+                columns = slice(entries.start // 16, entries.stop // 16)
+                nc.vector.tensor_copy(picked[g][:, t, entries], h.indirect(pos_sb[:, columns]))
 
         def scope_slice(n, h=None):
             if h is None:
@@ -328,38 +332,48 @@ def tile_list_inlining_adviser_kernel(
         w3_bf1 = held([P, 4 * N], BF16, "w3_bf1", "h1")
         round_w3(1, w3_bf1, slice(0, P))
 
-        w3q1 = quantised("w3_1", w3_bf1)
-
         z2 = mx_tiles("z2")
-        zb2 = held([P, 4 * M], BF16, "zb2", "tab2_w1")
-        for q in range(Q + 1):
-            if q < Q:
-                multiply(zb2[:, PASS * q : PASS * (q + 1)], 2, q, b_banks[q])
-            if q > 0:
-                quantise(z2, slice(P * (q - 1), P * q), zb2[:, PASS * (q - 1) : PASS * q])
-                out_passes(q - 1, w3q1, z1)
-                out_passes(q - 1, w3q2, z2, final=True)
+
+        def half_of_pass_2(half, on):
+            zb = held([P, 2 * M], BF16, "zb2%d" % half, on)
+            for i in range(2):
+                multiply(zb[:, PASS * i : PASS * (i + 1)], 2, 2 * half + i, b_banks[2 * half + i])
+            for i in range(2):
+                q = 2 * half + i
+                quantise(z2, slice(P * q, P * (q + 1)), zb[:, PASS * i : PASS * (i + 1)])
+
+        half_of_pass_2(0, "tab2_w0")
+        for q in range(2):
+            out_passes(q, w3q2, z2)
+        w3q1 = quantised("w3_1", w3_bf1)
+        for q in range(Q):
+            out_passes(q, w3q1, z1, final=(q < 2))
+        half_of_pass_2(1, "tab2_w1")
+        for q in range(2, Q):
+            out_passes(q, w3q2, z2, final=True)
 
         y_c = held([P, M], U32, "y_c")
         y_s = held([P, M], U8, "y_s")
         y_rows = out_0.rearrange("(p t) m -> p t m", t=4)
-        for q in range(Q):
-            cols = slice(P * q, P * (q + 1))
-            y = held([P, 4, P], F32, "y%d" % q)
-            for t in range(4):
-                nc.scalar.activation(
-                    y[:, t, :], banks[q][:, t, :], IDENT,
-                    bias=gby[:, t : t + 1], scale=gy_sb[:, t : t + 1],
+        yb = []
+        for q in range(Q + 1):
+            if q < Q:
+                y = held([P, 4, P], F32, "y%d" % q)
+                for t in range(4):
+                    nc.scalar.activation(
+                        y[:, t, :], banks[q][:, t, :], IDENT,
+                        bias=gby[:, t : t + 1], scale=gy_sb[:, t : t + 1],
+                    )
+                nc.sync.dma_start(out=y_rows[:, :, P * q : P * (q + 1)], in_=y[:])
+                yb.append(held([P, PASS], BF16, "yb%d" % q))
+                nc.vector.tensor_copy(
+                    out=yb[q][:].rearrange("p (c i t) -> p c t i", i=2, t=4),
+                    in_=y[:].rearrange("p t (c i) -> p c t i", i=2),
                 )
-            nc.sync.dma_start(out=y_rows[:, :, cols], in_=y[:])
-            yb = held([P, PASS], BF16, "yb%d" % q)
-            nc.vector.tensor_copy(
-                out=yb[:].rearrange("p (c i t) -> p c t i", i=2, t=4),
-                in_=y[:].rearrange("p t (c i) -> p c t i", i=2),
-            )
-            nc.vector.quantize_mx(out=y_c[:, cols].bitcast(FP8X4), scales=y_s[:, cols], in_=yb[:])
-            if q % 2:
-                cols = slice(P * (q - 1), P * (q + 1))
+            if q > 0:
+                quantise((y_c, y_s), slice(P * (q - 1), P * q), yb[q - 1][:])
+            if q in (2, 4):
+                cols = slice(P * (q - 2), P * q)
                 nc.sync.dma_start(
                     out=words_view(out_1[0])[:, cols], in_=y_c[:, cols].bitcast(I32)
                 )

@@ -21,7 +21,7 @@ P = 128
 PASS = 512
 G = H // PASS
 A = K2 // PASS
-SHARE = 64
+SHARE = 56
 SLICES = [(2, 0), (2, 1), (2, 2), (2, 3), (0, 0), (0, 1), (1, 0), (1, 1), (0, 2), (0, 3), (1, 2), (1, 3)]
 Q = M // P
 
@@ -63,13 +63,13 @@ def tile_list_inlining_adviser_kernel(
         tab2_w = [held([P, T2], I32, "tab2_w%d" % a) for a in range(A)]
         w4_w = held([P, A, N], I32, "w4_w")
         w4_s = held([P, N], U8, "w4_s")
-        for scale_tile in (tab_s, w1_s):
-            nc.gpsimd.memset(scale_tile[:].bitcast(I32), 0)
-        for scale_tile in (tab2_s, w4_s):
+        by_sb = held([P, 4], F32, "by_sb")
+        nc.gpsimd.memset(tab_s[:].bitcast(I32), 0)
+        nc.gpsimd.dma_start(out=by_sb[:], in_=by.rearrange("(p t) -> p t", t=4))
+        for scale_tile in (w1_s, tab2_s, w4_s):
             nc.vector.memset(scale_tile[:].bitcast(I32), 0)
 
         bias1 = held([P, G, 16], F32, "bias1")
-        by_sb = held([P, 4], F32, "by_sb")
         gy_sb = held([P, 4], F32, "gy_sb")
         gby = held([P, 4], F32, "gby")
 
@@ -80,23 +80,22 @@ def tile_list_inlining_adviser_kernel(
 
         nc.sync.dma_start(offs_sb[:], offs)
         nc.sync.dma_start(out=w1_w[:], in_=w1_words[0].bitcast(I32))
-        load_bias1(0, nc.sync)
+        nc.sync.dma_start(out=gy_sb[:], in_=gy.rearrange("(p t) -> p t", t=4))
         load_scale_rows(tab_s, tab_scales)
         nc.sync.dma_start(out=tab_w[:], in_=words_view(tab_words[0]))
         load_scale_rows(w1_s, w1_scales)
-        load_bias1(1, nc.sync)
-        for s in range(2, 4):
-            load_bias1(s, nc.gpsimd)
-        nc.sync.dma_start(offs2_sb[:], offs2)
+        for s in range(4):
+            load_bias1(s, nc.sync if s < 2 else nc.gpsimd)
         nc.sync.dma_start(out=tab2_w[0][:], in_=words_view(tab2_words[0]))
+        nc.sync.dma_start(offs2_sb[:], offs2)
         nc.sync.dma_start(pos_sb[:], pos1)
         load_scale_rows(tab2_s, tab2_scales)
         nc.sync.dma_start(out=tab2_w[1][:], in_=words_view(tab2_words[1]))
 
-        warm_in = held([P, 1], F32, "warm_in")
-        warm_out = held([P, 1], F32, "warm_out")
-        nc.vector.memset(warm_in[:], 0.0)
-        nc.scalar.activation(warm_out[:], warm_in[:], IDENT)
+        for t in range(4):
+            nc.scalar.activation(
+                gby[:, t : t + 1], by_sb[:, t : t + 1], IDENT, scale=gy_sb[:, t : t + 1]
+            )
 
         def load_w2(g, a):
             raw = held([P, 4, PASS], F32, "w2_raw%d%d" % (g, a))
@@ -115,8 +114,6 @@ def tile_list_inlining_adviser_kernel(
         w3_raw = {0: load_w3(0, None)}
         load_scale_rows(w4_s, w4_scales)
         nc.sync.dma_start(out=w4_w[:], in_=w4_words.rearrange("a p c i -> p a (c i)").bitcast(I32))
-        nc.sync.dma_start(out=gy_sb[:], in_=gy.rearrange("(p t) -> p t", t=4))
-        nc.sync.dma_start(out=by_sb[:], in_=by.rearrange("(p t) -> p t", t=4))
         w2_raw.append([load_w2(2, a) for a in range(A)])
 
         v_s = held([P, S], U8, "v_s")
@@ -308,8 +305,6 @@ def tile_list_inlining_adviser_kernel(
             out=w4_sd[:].rearrange("p (t c i) -> p c t i", t=4, i=16),
             in_=w4_s[:].rearrange("p (c i t) -> p c t i", t=4, i=16),
         )
-
-        nc.vector.tensor_tensor(gby[:], gy_sb[:], by_sb[:], MULT)
 
         for q in range(Q):
             for a in range(A):

@@ -21,9 +21,10 @@ P = 128
 PASS = 512
 G = H // PASS
 A = K2 // PASS
-SHARE = 56
-SLICES = [(2, 0), (2, 1), (2, 2), (2, 3), (0, 0), (0, 1), (1, 0), (1, 1), (0, 2), (0, 3), (1, 2), (1, 3)]
 Q = M // P
+UNITS = PASS // 16
+EARLY = [(2, t) for t in range(4)] + [(g, t) for g in range(2) for t in range(2)]
+HELD_BACK = [[(g, t) for t in range(2, 4)] for g in range(2)]
 
 
 def tile_list_inlining_adviser_kernel(
@@ -78,19 +79,28 @@ def tile_list_inlining_adviser_kernel(
         def load_bias1(s, queue):
             queue.dma_start(out=bias1[s:P:4, :, 0:13], in_=b1_view[:, :, s : s + 13])
 
-        nc.sync.dma_start(offs_sb[:], offs)
+        def load_w2_columns(name, a, first, count):
+            raw = held([P, 4, count], F32, name)
+            rows = w2[PASS * a : PASS * (a + 1), first : first + count]
+            nc.sync.dma_start(out=raw[:], in_=rows.rearrange("(p j) c -> p j c", j=4))
+            return raw
+
         nc.sync.dma_start(out=w1_w[:], in_=w1_words[0].bitcast(I32))
+        nc.sync.dma_start(offs_sb[:], offs)
         nc.sync.dma_start(out=gy_sb[:], in_=gy.rearrange("(p t) -> p t", t=4))
         load_scale_rows(tab_s, tab_scales)
         nc.sync.dma_start(out=tab_w[:], in_=words_view(tab_words[0]))
         load_scale_rows(w1_s, w1_scales)
-        for s in range(4):
-            load_bias1(s, nc.sync if s < 2 else nc.gpsimd)
-        nc.sync.dma_start(out=tab2_w[0][:], in_=words_view(tab2_words[0]))
+        first_piece = [load_w2_columns("w2_half0", 0, 0, PASS // 2)]
+        load_bias1(0, nc.sync)
+        first_piece.append(load_w2_columns("w2_half1", 0, PASS // 2, PASS // 2))
+        for s in range(1, 4):
+            load_bias1(s, nc.gpsimd)
         nc.sync.dma_start(offs2_sb[:], offs2)
-        nc.sync.dma_start(pos_sb[:], pos1)
         load_scale_rows(tab2_s, tab2_scales)
-        nc.sync.dma_start(out=tab2_w[1][:], in_=words_view(tab2_words[1]))
+        nc.sync.dma_start(pos_sb[:], pos1)
+        for a in range(A):
+            nc.sync.dma_start(out=tab2_w[a][:], in_=words_view(tab2_words[a]))
 
         for t in range(4):
             nc.scalar.activation(
@@ -98,10 +108,7 @@ def tile_list_inlining_adviser_kernel(
             )
 
         def load_w2(g, a):
-            raw = held([P, 4, PASS], F32, "w2_raw%d%d" % (g, a))
-            rows = w2[PASS * a : PASS * (a + 1), PASS * g : PASS * (g + 1)]
-            nc.sync.dma_start(out=raw[:], in_=rows.rearrange("(p j) c -> p j c", j=4))
-            return raw
+            return load_w2_columns("w2_raw%d%d" % (g, a), a, PASS * g, PASS)
 
         def load_w3(g, on):
             raw = held([P, 4, N], F32, "w3_raw%d" % g, on)
@@ -110,11 +117,14 @@ def tile_list_inlining_adviser_kernel(
                 nc.sync.dma_start(out=raw[:, j, :], in_=rows[j])
             return raw
 
-        w2_raw = [[load_w2(g, a) for a in range(A)] for g in range(2)]
-        w3_raw = {0: load_w3(0, None)}
+        w2_raw = {(0, 1): load_w2(0, 1)}
         load_scale_rows(w4_s, w4_scales)
         nc.sync.dma_start(out=w4_w[:], in_=w4_words.rearrange("a p c i -> p a (c i)").bitcast(I32))
-        w2_raw.append([load_w2(2, a) for a in range(A)])
+        for a in range(A):
+            w2_raw[(1, a)] = load_w2(1, a)
+        w3_raw = {0: load_w3(0, None)}
+        for a in range(A):
+            w2_raw[(2, a)] = load_w2(2, a)
 
         v_s = held([P, S], U8, "v_s")
         v_w = [held([P, PASS], U32, "v_w0")]
@@ -136,53 +146,49 @@ def tile_list_inlining_adviser_kernel(
         v2_s = held([P, M], U8, "v2_s")
         nc.vector.tensor_copy(v2_s[:], tab2_s[:].indirect(offs2_sb[:]))
 
-
-        def scope_half(h, n, c):
-            g, t = SLICES[n]
-            i = 4 * g + t
-            bank = psum_bank([P, PASS], 2 * (n % 4) + c)
-            nc.tensor.matmul_mx(
-                out=bank[:],
-                lhsT=w1_wd[:, 64 * i : 64 * (i + 1)].bitcast(U8).bitcast(FP4X4),
-                lhsT_scale=w1_sd[:, P * i : P * (i + 1)],
-                rhs=v_w[c][:].bitcast(FP8X4),
-                rhs_scale=v_s[:, PASS * c : PASS * (c + 1)],
-                start=True,
-                stop=True,
-            )
-            nc.scalar.activation(
-                h[:, PASS * c : PASS * (c + 1)], bank[:], IDENT,
-                bias=bias1[:, g, 4 * t : 4 * t + 1],
-            )
-
         picked = [held([P, 4, M], F32, "picked%d" % g) for g in range(G)]
 
-        def pick_scope(h, n):
-            g, t = SLICES[n]
-            parts = 2 if n in (9, 11) else 1
-            for i in range(parts):
-                entries = slice(M // parts * i, M // parts * (i + 1))
+        def scope_slice(g, t, h, first_bank, parts=1):
+            i = 4 * g + t
+            for c in range(2):
+                bank = psum_bank([P, PASS], first_bank + c)
+                nc.tensor.matmul_mx(
+                    out=bank[:],
+                    lhsT=w1_wd[:, 64 * i : 64 * (i + 1)].bitcast(U8).bitcast(FP4X4),
+                    lhsT_scale=w1_sd[:, P * i : P * (i + 1)],
+                    rhs=v_w[c][:].bitcast(FP8X4),
+                    rhs_scale=v_s[:, PASS * c : PASS * (c + 1)],
+                    start=True,
+                    stop=True,
+                )
+                nc.scalar.activation(
+                    h[:, PASS * c : PASS * (c + 1)], bank[:], IDENT,
+                    bias=bias1[:, g, 4 * t : 4 * t + 1],
+                )
+            for part in range(parts):
+                entries = slice(M // parts * part, M // parts * (part + 1))
                 columns = slice(entries.start // 16, entries.stop // 16)
                 nc.vector.tensor_copy(picked[g][:, t, entries], h.indirect(pos_sb[:, columns]))
-
-        def scope_slice(n, h=None):
-            if h is None:
-                h = held([P, S], F32, "h%d" % n)[:]
-            for c in range(2):
-                scope_half(h, n, c)
-            pick_scope(h, n)
 
         def gather_calls(a):
             words = held([P, M], U32, "v2_w%d" % a)
             nc.vector.tensor_copy(words[:], tab2_w[a][:].bitcast(U32).indirect(offs2_sb[:]))
             return words
 
-        first_two = [held([P, S], F32, "h%d" % n)[:] for n in range(2)]
-        for c in range(2):
-            for t in range(2):
-                scope_half(first_two[t], t, c)
-        for t in range(2):
-            pick_scope(first_two[t], t)
+        def round_w2_columns(raw, rounded, units):
+            nc.scalar.copy(
+                out=rounded[:].rearrange("p (t u s j) -> p t u j s", t=4, s=4, j=4)[:, :, units],
+                in_=raw[:].rearrange("p j (u t s) -> p t u j s", t=4, s=4),
+            )
+
+        w2_bf00 = held([P, 4 * PASS], BF16, "w2_bf00")
+        for half in range(2):
+            units = slice(UNITS // 2 * half, UNITS // 2 * (half + 1))
+            round_w2_columns(first_piece[half], w2_bf00, units)
+
+        first_two = held([P, 2, S], F32, "h01", "w2_half1")
+        for n in range(2):
+            scope_slice(*EARLY[n], first_two[:, n, :], 2 * n)
         v2_w = [gather_calls(a) for a in range(A)]
         w3_raw[2] = load_w3(2, "tab2_w0")
         w3_raw[1] = load_w3(1, "tab2_w1")
@@ -201,54 +207,54 @@ def tile_list_inlining_adviser_kernel(
             quantise(operand, slice(0, PASS), rounded[:])
             return operand
 
-        def round_w2(g, a, on):
+        def prepare_w2(g, a, on):
             rounded = held([P, 4 * PASS], BF16, "w2_bf%d%d" % (g, a), on)
+            round_w2_columns(w2_raw[(g, a)], rounded, slice(0, UNITS))
+            return quantised("w2_%d%d" % (g, a), rounded)
+
+        def round_w3_pair(g, pair, rounded):
+            source = w3_raw[g][:].rearrange("p j (m t) -> p m j t", t=4)
             nc.scalar.copy(
-                out=rounded[:].rearrange("p (t u s j) -> p t u j s", t=4, s=4, j=4),
-                in_=w2_raw[g][a][:].rearrange("p j (u t s) -> p t u j s", t=4, s=4),
+                out=rounded.rearrange("p (t m j) -> p m j t", t=2, j=4),
+                in_=source[:, :, :, 2 * pair : 2 * pair + 2],
             )
             return rounded
 
-        def prepare_w2(g, a, on):
-            return quantised("w2_%d%d" % (g, a), round_w2(g, a, on))
-
-        def round_w3(g, rounded, columns):
-            source = w3_raw[g][:].rearrange("p j (m t) -> p m j t", t=4)
-            dealt = rounded[:].rearrange("p (t m j) -> p m j t", t=4, j=4)
-            for half in range(2):
-                pair = slice(2 * half, 2 * half + 2)
-                nc.scalar.copy(out=dealt[:, columns, :, pair], in_=source[:, columns, :, pair])
-
         def round_w3_beside_products(g, on):
-            rounded = held([P, 4 * N], BF16, "w3_bf%d" % g, on)
-            dealt = rounded[:].rearrange("p (t m j) -> p m t j", t=4, j=4)
+            rounded = held([P, 2 * N], BF16, "w3_bf%d1" % g, on)
             source = w3_raw[g][:].rearrange("p j (m t) -> p m t j", t=4)
-            for half in range(2):
-                pair = slice(2 * half, 2 * half + 2)
-                nc.gpsimd.tensor_scalar(
-                    dealt[:, 0:SHARE, pair], source[:, 0:SHARE, pair], 1.0, 0.0, MULT, ADD
-                )
-            return rounded
+            nc.gpsimd.tensor_scalar(
+                rounded[:].rearrange("p (t m j) -> p m t j", t=2, j=4),
+                source[:, :, 2:4], 1.0, 0.0, MULT, ADD,
+            )
+            return rounded[:]
 
-        def last_two_slices(g):
-            pair = held([P, 2, S], F32, "h_pair%d" % g, "w2_raw%d1" % g)
-            for i in range(2):
-                scope_slice(8 + 2 * g + i, pair[:, i, :])
+        def quantise_pairs(operand, pairs):
+            for pair in (1, 0):
+                quantise(operand, slice(2 * P * pair, 2 * P * (pair + 1)), pairs[pair])
+
+        def half_columns(half):
+            return slice(M // 2 * half, M // 2 * (half + 1))
+
+        def held_back_slices(g, last_parts):
+            both = held([P, 2, S], F32, "h_held%d" % g, "w2_raw%d1" % g)
+            for n in range(2):
+                scope_slice(*HELD_BACK[g][n], both[:, n, :], Q + 2 * n, last_parts if n else 1)
 
         def call_projection(w2_pass, q):
             bank = psum_bank([P, 4, P], Q + q)
             cols = slice(P * q, P * (q + 1))
-            for t in range(4):
-                for a in range(A):
-                    codes, scales = w2_pass[a]
+            for a in range(A):
+                codes, scales = w2_pass[a]
+                for t in range(4):
                     nc.tensor.matmul_mx(
                         out=bank[:, t, :],
                         lhsT=codes[:, P * t : P * (t + 1)].bitcast(FP8X4),
                         lhsT_scale=scales[:, P * t : P * (t + 1)],
                         rhs=v2_w[a][:, cols].bitcast(FP8X4),
                         rhs_scale=v2_s[4 * a : P, cols],
-                        start=(a == 0),
-                        stop=(a == A - 1),
+                        start=(a == 0 and t == 0),
+                        stop=(a == A - 1 and t == 3),
                     )
             return bank
 
@@ -266,13 +272,34 @@ def tile_list_inlining_adviser_kernel(
                 multiply(zb[:, PASS * q : PASS * (q + 1)], g, q, call_projection(w2_pass, q))
             return zb
 
-        for n in range(2, 8):
-            scope_slice(n)
-        w2q = [prepare_w2(0, 0, "tab_w"), prepare_w2(0, 1, "h0")]
+        for n in range(2, len(EARLY)):
+            scope_slice(*EARLY[n], held([P, S], F32, "h%d" % n)[:], 2 * (n % 2))
+        w2q = [quantised("w2_00", w2_bf00), prepare_w2(0, 1, "w2_half1")]
 
-        last_two_slices(0)
-        w3_bf0 = round_w3_beside_products(0, "w2_raw01")
+        w4_wd = held([P, A, N], I32, "w4_wd")
+        w4_sd = held([P, N], U8, "w4_sd")
+        nc.vector.tensor_copy(
+            out=w4_wd[:].rearrange("p a (t c i) -> p a c t i", t=4, i=4),
+            in_=w4_w[:].rearrange("p a (c i t) -> p a c t i", t=4, i=4),
+        )
+        nc.vector.tensor_copy(
+            out=w4_sd[:].rearrange("p (t c i) -> p c t i", t=4, i=16),
+            in_=w4_s[:].rearrange("p (c i t) -> p c t i", t=4, i=16),
+        )
+
+        held_back_slices(0, 2)
+        w3_bf01 = round_w3_beside_products(0, "w2_raw01")
         zb0 = products(0, w2q, "h3")
+
+        w2q = [prepare_w2(1, 0, "tab_w")]
+        z0 = quantised("z0", zb0, "w2_raw10")
+        w2q.append(prepare_w2(1, 1, "h2"))
+        held_back_slices(1, 1)
+        w3q0 = mx_tiles("w3_0", "w2_raw11")
+        w3_bf00 = round_w3_pair(0, 0, held([P, 2 * N], BF16, "w3_bf00", "h4")[:])
+        quantise_pairs(w3q0, (w3_bf00, w3_bf01))
+        w3_bf21 = round_w3_beside_products(2, "h4")
+        zb1 = products(1, w2q, "w2_raw01")
 
         banks = [psum_bank([P, 4, P], q) for q in range(Q)]
 
@@ -289,43 +316,22 @@ def tile_list_inlining_adviser_kernel(
                     stop=(final and t == 3),
                 )
 
-        w2q = [prepare_w2(1, 0, "h1")]
-        z0 = quantised("z0", zb0, "w2_raw10")
-        w2q.append(prepare_w2(1, 1, "h2"))
-        last_two_slices(1)
-        w3_bf2 = round_w3_beside_products(2, "w2_raw11")
-        zb1 = products(1, w2q, "h4")
-        w4_wd = held([P, A, N], I32, "w4_wd")
-        w4_sd = held([P, N], U8, "w4_sd")
-        nc.vector.tensor_copy(
-            out=w4_wd[:].rearrange("p a (t c i) -> p a c t i", t=4, i=4),
-            in_=w4_w[:].rearrange("p a (c i t) -> p a c t i", t=4, i=4),
-        )
-        nc.vector.tensor_copy(
-            out=w4_sd[:].rearrange("p (t c i) -> p c t i", t=4, i=16),
-            in_=w4_s[:].rearrange("p (c i t) -> p c t i", t=4, i=16),
-        )
-
         for q in range(Q):
             for a in range(A):
                 out_passes(q, (w4_wd[:, a, :], w4_sd), (v2_w[a], v2_s), 4 * a, first=(a == 0))
-        round_w3(0, w3_bf0, slice(SHARE, P))
-
-        w2_bf20 = round_w2(2, 0, "h5")
-        both = held([P, 2, PASS], U32, "w3_0_z1_c", "w2_raw20")
-        w3q0 = (both[:, 0, :], held([P, PASS], U8, "w3_0_s"))
-        quantise(w3q0, slice(0, PASS), w3_bf0[:])
-        for q in range(Q):
             out_passes(q, w3q0, z0)
-        w2q = [quantised("w2_20", w2_bf20)]
-        z1 = (both[:, 1, :], held([P, PASS], U8, "z1_s"))
-        quantise(z1, slice(0, PASS), zb1[:])
-        w2q.append(prepare_w2(2, 1, "h0"))
+
+        w2q = [prepare_w2(2, 0, "h5"), prepare_w2(2, 1, "w2_half1")]
         b_banks = [call_projection(w2q, q) for q in range(Q)]
-        round_w3(2, w3_bf2, slice(SHARE, P))
-        w3q2 = quantised("w3_2", w3_bf2)
-        w3_bf1 = held([P, 4 * N], BF16, "w3_bf1", "h1")
-        round_w3(1, w3_bf1, slice(0, P))
+        late_codes = held([P, 2, PASS], U32, "z1_w3_2_c", "w2_raw21")
+        z1 = (late_codes[:, 0, :], held([P, PASS], U8, "z1_s"))
+        quantise(z1, slice(0, PASS), zb1[:])
+        w3q2 = (late_codes[:, 1, :], held([P, PASS], U8, "w3_2_s"))
+        w3_bf20 = round_w3_pair(2, 0, held([P, 2 * N], BF16, "w3_bf20", "h6")[:])
+        quantise_pairs(w3q2, (w3_bf20, w3_bf21))
+        w3_bf1 = held([P, 4 * N], BF16, "w3_bf1", "tab_w")
+        for pair in range(2):
+            round_w3_pair(1, pair, w3_bf1[:, 2 * N * pair : 2 * N * (pair + 1)])
 
         z2 = mx_tiles("z2")
 
@@ -347,31 +353,41 @@ def tile_list_inlining_adviser_kernel(
         for q in range(2, Q):
             out_passes(q, w3q2, z2, final=True)
 
-        y_c = held([P, M], U32, "y_c")
         y_s = held([P, M], U8, "y_s")
         y_rows = out_0.rearrange("(p t) m -> p t m", t=4)
-        yb = []
-        for q in range(Q + 1):
-            if q < Q:
-                y = held([P, 4, P], F32, "y%d" % q)
-                for t in range(4):
-                    nc.scalar.activation(
-                        y[:, t, :], banks[q][:, t, :], IDENT,
-                        bias=gby[:, t : t + 1], scale=gy_sb[:, t : t + 1],
-                    )
-                nc.sync.dma_start(out=y_rows[:, :, P * q : P * (q + 1)], in_=y[:])
-                yb.append(held([P, PASS], BF16, "yb%d" % q))
-                nc.vector.tensor_copy(
-                    out=yb[q][:].rearrange("p (c i t) -> p c t i", i=2, t=4),
-                    in_=y[:].rearrange("p t (c i) -> p c t i", i=2),
+
+        def empty_bank(q):
+            y = held([P, 4, P], F32, "y%d" % q)
+            for t in range(4):
+                nc.scalar.activation(
+                    y[:, t, :], banks[q][:, t, :], IDENT,
+                    bias=gby[:, t : t + 1], scale=gy_sb[:, t : t + 1],
                 )
-            if q > 0:
-                quantise((y_c, y_s), slice(P * (q - 1), P * q), yb[q - 1][:])
-            if q in (2, 4):
-                cols = slice(P * (q - 2), P * q)
-                nc.sync.dma_start(
-                    out=words_view(out_1[0])[:, cols], in_=y_c[:, cols].bitcast(I32)
+            nc.sync.dma_start(out=y_rows[:, :, P * q : P * (q + 1)], in_=y[:])
+            return y
+
+        def round_y(q, y):
+            yb = held([P, PASS], BF16, "yb%d" % q)
+            nc.vector.tensor_copy(
+                out=yb[:].rearrange("p (c i t) -> p c t i", i=2, t=4),
+                in_=y[:].rearrange("p t (c i) -> p c t i", i=2),
+            )
+            return yb
+
+        for half in range(2):
+            quarters = (2 * half, 2 * half + 1)
+            y = [empty_bank(q) for q in quarters]
+            yb = [round_y(quarters[i], y[i]) for i in range(2)]
+            y_c = held([P, M // 2], U32, "y_c%d" % half, "gby" if half else None)
+            for i in range(2):
+                nc.vector.quantize_mx(
+                    out=y_c[:, P * i : P * (i + 1)].bitcast(FP8X4),
+                    scales=y_s[:, P * quarters[i] : P * (quarters[i] + 1)],
+                    in_=yb[i][:],
                 )
+            nc.sync.dma_start(
+                out=words_view(out_1[0])[:, half_columns(half)], in_=y_c[:].bitcast(I32)
+            )
         for quad in range(4):
             queue = nc.scalar if quad % 2 else nc.sync
             queue.dma_start(

@@ -42,10 +42,10 @@ def tile_list_inlining_adviser_kernel(
         def held(shape, dtype, name, on=None):
             return keep.tile(shape, dtype, name=name, tag=on or name, align_bytes=64)
 
-        def load_scale_rows(scale_tile, scales):
+        def load_scale_rows(scale_tile, scales, queue=nc.sync):
             passes = scales.shape[0]
             for quad in range(4):
-                nc.sync.dma_start(
+                queue.dma_start(
                     out=scale_tile[32 * quad : 32 * quad + 4 * passes, :].bitcast(I32),
                     in_=scales[:, 4 * quad : 4 * quad + 4, :].bitcast(I32),
                 )
@@ -66,7 +66,6 @@ def tile_list_inlining_adviser_kernel(
         w4_s = held([P, N], U8, "w4_s")
         by_sb = held([P, 4], F32, "by_sb")
         nc.gpsimd.memset(tab_s[:].bitcast(I32), 0)
-        nc.gpsimd.dma_start(out=by_sb[:], in_=by.rearrange("(p t) -> p t", t=4))
         for scale_tile in (w1_s, tab2_s, w4_s):
             nc.vector.memset(scale_tile[:].bitcast(I32), 0)
 
@@ -87,25 +86,19 @@ def tile_list_inlining_adviser_kernel(
 
         nc.sync.dma_start(out=w1_w[:], in_=w1_words[0].bitcast(I32))
         nc.sync.dma_start(offs_sb[:], offs)
-        nc.sync.dma_start(out=gy_sb[:], in_=gy.rearrange("(p t) -> p t", t=4))
+        nc.sync.dma_start(offs2_sb[:], offs2)
         load_scale_rows(tab_s, tab_scales)
         nc.sync.dma_start(out=tab_w[:], in_=words_view(tab_words[0]))
         load_scale_rows(w1_s, w1_scales)
         first_piece = [load_w2_columns("w2_half0", 0, 0, PASS // 2)]
         load_bias1(0, nc.sync)
-        first_piece.append(load_w2_columns("w2_half1", 0, PASS // 2, PASS // 2))
         for s in range(1, 4):
             load_bias1(s, nc.gpsimd)
-        nc.sync.dma_start(offs2_sb[:], offs2)
         load_scale_rows(tab2_s, tab2_scales)
         nc.sync.dma_start(pos_sb[:], pos1)
-        for a in range(A):
-            nc.sync.dma_start(out=tab2_w[a][:], in_=words_view(tab2_words[a]))
-
-        for t in range(4):
-            nc.scalar.activation(
-                gby[:, t : t + 1], by_sb[:, t : t + 1], IDENT, scale=gy_sb[:, t : t + 1]
-            )
+        nc.sync.dma_start(out=tab2_w[0][:], in_=words_view(tab2_words[0]))
+        nc.sync.dma_start(out=tab2_w[1][:], in_=words_view(tab2_words[1]))
+        first_piece.append(load_w2_columns("w2_half1", 0, PASS // 2, PASS // 2))
 
         def load_w2(g, a):
             return load_w2_columns("w2_raw%d%d" % (g, a), a, PASS * g, PASS)
@@ -123,6 +116,9 @@ def tile_list_inlining_adviser_kernel(
         for a in range(A):
             w2_raw[(1, a)] = load_w2(1, a)
         w3_raw = {0: load_w3(0, None)}
+        nc.sync.dma_start(out=gy_sb[:], in_=gy.rearrange("(p t) -> p t", t=4))
+        nc.sync.dma_start(out=by_sb[:], in_=by.rearrange("(p t) -> p t", t=4))
+        nc.gpsimd.tensor_tensor(gby[:], by_sb[:], gy_sb[:], MULT)
         for a in range(A):
             w2_raw[(2, a)] = load_w2(2, a)
 
@@ -132,15 +128,15 @@ def tile_list_inlining_adviser_kernel(
         nc.vector.tensor_copy(v_w[0][:], tab_w[:].bitcast(U32).indirect(offs_sb[:, 0:32]))
         w1_wd = held([P, H // 2], I32, "w1_wd")
         w1_sd = held([P, H], U8, "w1_sd")
-        nc.vector.tensor_copy(
-            out=w1_sd[:].bitcast(I32).rearrange("p (g t c i) -> p c g t i", g=G, t=4, i=4),
-            in_=w1_s[:].bitcast(I32).rearrange("p (g c i t) -> p c g t i", g=G, t=4, i=4),
+        nc.scalar.copy(
+            out=w1_wd[:].bitcast(U32).rearrange("p (g t u i) -> p t g u i", g=G, t=4, i=2),
+            in_=w1_w[:].bitcast(U32).rearrange("p (g u t i) -> p t g u i", g=G, t=4, i=2),
         )
-        nc.vector.tensor_copy(
-            out=w1_wd[:].rearrange("p (g t u i) -> p t g u i", g=G, t=4, i=2),
-            in_=w1_w[:].rearrange("p (g u t i) -> p t g u i", g=G, t=4, i=2),
+        nc.scalar.copy(
+            out=w1_sd[:].bitcast(U32).rearrange("p (g t c i) -> p c g t i", g=G, t=4, i=4),
+            in_=w1_s[:].bitcast(U32).rearrange("p (g c i t) -> p c g t i", g=G, t=4, i=4),
         )
-        v_w.append(held([P, PASS], U32, "v_w1", "w1_s"))
+        v_w.append(held([P, PASS], U32, "v_w1"))
         nc.vector.tensor_copy(v_w[1][:], tab_w[:].bitcast(U32).indirect(offs_sb[:, 32:64]))
 
         v2_s = held([P, M], U8, "v2_s")
@@ -186,7 +182,7 @@ def tile_list_inlining_adviser_kernel(
             units = slice(UNITS // 2 * half, UNITS // 2 * (half + 1))
             round_w2_columns(first_piece[half], w2_bf00, units)
 
-        first_two = held([P, 2, S], F32, "h01", "w2_half1")
+        first_two = held([P, 2, S], F32, "h01")
         for n in range(2):
             scope_slice(*EARLY[n], first_two[:, n, :], 2 * n)
         v2_w = [gather_calls(a) for a in range(A)]
@@ -273,8 +269,8 @@ def tile_list_inlining_adviser_kernel(
             return zb
 
         for n in range(2, len(EARLY)):
-            scope_slice(*EARLY[n], held([P, S], F32, "h%d" % n)[:], 2 * (n % 2))
-        w2q = [quantised("w2_00", w2_bf00), prepare_w2(0, 1, "w2_half1")]
+            scope_slice(*EARLY[n], held([P, S], F32, "h%d" % n)[:], 2 * (n % 4))
+        w2q = [quantised("w2_00", w2_bf00), prepare_w2(0, 1, "h01")]
 
         w4_wd = held([P, A, N], I32, "w4_wd")
         w4_sd = held([P, N], U8, "w4_sd")
@@ -321,7 +317,7 @@ def tile_list_inlining_adviser_kernel(
                 out_passes(q, (w4_wd[:, a, :], w4_sd), (v2_w[a], v2_s), 4 * a, first=(a == 0))
             out_passes(q, w3q0, z0)
 
-        w2q = [prepare_w2(2, 0, "h5"), prepare_w2(2, 1, "w2_half1")]
+        w2q = [prepare_w2(2, 0, "h5"), prepare_w2(2, 1, "h01")]
         b_banks = [call_projection(w2q, q) for q in range(Q)]
         late_codes = held([P, 2, PASS], U32, "z1_w3_2_c", "w2_raw21")
         z1 = (late_codes[:, 0, :], held([P, PASS], U8, "z1_s"))

@@ -97,8 +97,8 @@ def tile_list_inlining_adviser_kernel(
         load_scale_rows(tab2_s, tab2_scales)
         nc.sync.dma_start(pos_sb[:], pos1)
         nc.sync.dma_start(out=tab2_w[0][:], in_=words_view(tab2_words[0]))
-        nc.sync.dma_start(out=tab2_w[1][:], in_=words_view(tab2_words[1]))
         first_piece.append(load_w2_columns("w2_half1", 0, PASS // 2, PASS // 2))
+        nc.sync.dma_start(out=tab2_w[1][:], in_=words_view(tab2_words[1]))
 
         def load_w2(g, a):
             return load_w2_columns("w2_raw%d%d" % (g, a), a, PASS * g, PASS)
@@ -113,9 +113,9 @@ def tile_list_inlining_adviser_kernel(
         w2_raw = {(0, 1): load_w2(0, 1)}
         load_scale_rows(w4_s, w4_scales)
         nc.sync.dma_start(out=w4_w[:], in_=w4_words.rearrange("a p c i -> p a (c i)").bitcast(I32))
-        for a in range(A):
-            w2_raw[(1, a)] = load_w2(1, a)
+        w2_raw[(1, 0)] = load_w2(1, 0)
         w3_raw = {0: load_w3(0, None)}
+        w2_raw[(1, 1)] = load_w2(1, 1)
         nc.sync.dma_start(out=gy_sb[:], in_=gy.rearrange("(p t) -> p t", t=4))
         nc.sync.dma_start(out=by_sb[:], in_=by.rearrange("(p t) -> p t", t=4))
         nc.gpsimd.tensor_tensor(gby[:], by_sb[:], gy_sb[:], MULT)
@@ -144,35 +144,41 @@ def tile_list_inlining_adviser_kernel(
 
         picked = [held([P, 4, M], F32, "picked%d" % g) for g in range(G)]
 
-        def scope_slice(g, t, h, first_bank, parts=1):
+        def scope_half(g, t, h, c, bank_index):
             i = 4 * g + t
-            for c in range(2):
-                bank = psum_bank([P, PASS], first_bank + c)
-                nc.tensor.matmul_mx(
-                    out=bank[:],
-                    lhsT=w1_wd[:, 64 * i : 64 * (i + 1)].bitcast(U8).bitcast(FP4X4),
-                    lhsT_scale=w1_sd[:, P * i : P * (i + 1)],
-                    rhs=v_w[c][:].bitcast(FP8X4),
-                    rhs_scale=v_s[:, PASS * c : PASS * (c + 1)],
-                    start=True,
-                    stop=True,
-                )
-                nc.scalar.activation(
-                    h[:, PASS * c : PASS * (c + 1)], bank[:], IDENT,
-                    bias=bias1[:, g, 4 * t : 4 * t + 1],
-                )
+            bank = psum_bank([P, PASS], bank_index)
+            nc.tensor.matmul_mx(
+                out=bank[:],
+                lhsT=w1_wd[:, 64 * i : 64 * (i + 1)].bitcast(U8).bitcast(FP4X4),
+                lhsT_scale=w1_sd[:, P * i : P * (i + 1)],
+                rhs=v_w[c][:].bitcast(FP8X4),
+                rhs_scale=v_s[:, PASS * c : PASS * (c + 1)],
+                start=True,
+                stop=True,
+            )
+            nc.scalar.activation(
+                h[:, PASS * c : PASS * (c + 1)], bank[:], IDENT,
+                bias=bias1[:, g, 4 * t : 4 * t + 1],
+            )
+
+        def pick(g, t, h, parts=1):
             for part in range(parts):
                 entries = slice(M // parts * part, M // parts * (part + 1))
                 columns = slice(entries.start // 16, entries.stop // 16)
                 nc.vector.tensor_copy(picked[g][:, t, entries], h.indirect(pos_sb[:, columns]))
+
+        def scope_slice(g, t, h, first_bank, parts=1):
+            for c in range(2):
+                scope_half(g, t, h, c, first_bank + c)
+            pick(g, t, h, parts)
 
         def gather_calls(a):
             words = held([P, M], U32, "v2_w%d" % a)
             nc.vector.tensor_copy(words[:], tab2_w[a][:].bitcast(U32).indirect(offs2_sb[:]))
             return words
 
-        def round_w2_columns(raw, rounded, units):
-            nc.scalar.copy(
+        def round_w2_columns(raw, rounded, units, copy=nc.scalar.copy):
+            copy(
                 out=rounded[:].rearrange("p (t u s j) -> p t u j s", t=4, s=4, j=4)[:, :, units],
                 in_=raw[:].rearrange("p j (u t s) -> p t u j s", t=4, s=4),
             )
@@ -180,11 +186,15 @@ def tile_list_inlining_adviser_kernel(
         w2_bf00 = held([P, 4 * PASS], BF16, "w2_bf00")
         for half in range(2):
             units = slice(UNITS // 2 * half, UNITS // 2 * (half + 1))
-            round_w2_columns(first_piece[half], w2_bf00, units)
+            copy = nc.vector.tensor_copy if half else nc.scalar.copy
+            round_w2_columns(first_piece[half], w2_bf00, units, copy)
 
         first_two = held([P, 2, S], F32, "h01")
+        for c in range(2):
+            for n in range(2):
+                scope_half(*EARLY[n], first_two[:, n, :], c, 2 * n + c)
         for n in range(2):
-            scope_slice(*EARLY[n], first_two[:, n, :], 2 * n)
+            pick(*EARLY[n], first_two[:, n, :])
         v2_w = [gather_calls(a) for a in range(A)]
         w3_raw[2] = load_w3(2, "tab2_w0")
         w3_raw[1] = load_w3(1, "tab2_w1")
@@ -290,9 +300,9 @@ def tile_list_inlining_adviser_kernel(
         w2q = [prepare_w2(1, 0, "tab_w")]
         z0 = quantised("z0", zb0, "w2_raw10")
         w2q.append(prepare_w2(1, 1, "h2"))
+        w3_bf00 = round_w3_pair(0, 0, held([P, 2 * N], BF16, "w3_bf00", "h4")[:])
         held_back_slices(1, 1)
         w3q0 = mx_tiles("w3_0", "w2_raw11")
-        w3_bf00 = round_w3_pair(0, 0, held([P, 2 * N], BF16, "w3_bf00", "h4")[:])
         quantise_pairs(w3q0, (w3_bf00, w3_bf01))
         w3_bf21 = round_w3_beside_products(2, "h4")
         zb1 = products(1, w2q, "w2_raw01")

@@ -34,12 +34,15 @@ def tile_list_inlining_adviser_kernel(
     nc = tc.nc
     with ExitStack() as ctx:
         keep = ctx.enter_context(tc.tile_pool(name="keep", bufs=1))
+        stage = ctx.enter_context(tc.tile_pool(name="stage", bufs=1))
         psum = ctx.enter_context(tc.psum_pool(name="psum", bufs=1))
 
         def psum_bank(shape, index):
             return psum.tile(shape, F32, name="bank%d" % index)
 
         def held(shape, dtype, name, on=None):
+            if isinstance(on, int):
+                return stage.tile(shape, dtype, name=name, align_bytes=64, offset=on)
             return keep.tile(shape, dtype, name=name, tag=on or name, align_bytes=64)
 
         def load_scale_rows(scale_tile, scales, queue=nc.sync):
@@ -78,8 +81,8 @@ def tile_list_inlining_adviser_kernel(
         def load_bias1(s, queue):
             queue.dma_start(out=bias1[s:P:4, :, 0:13], in_=b1_view[:, :, s : s + 13])
 
-        def load_w2_columns(name, a, first, count):
-            raw = held([P, 4, count], F32, name)
+        def load_w2_columns(name, a, first, count, on=None):
+            raw = held([P, 4, count], F32, name, on)
             rows = w2[PASS * a : PASS * (a + 1), first : first + count]
             nc.sync.dma_start(out=raw[:], in_=rows.rearrange("(p j) c -> p j c", j=4))
             return raw
@@ -110,12 +113,12 @@ def tile_list_inlining_adviser_kernel(
                 nc.sync.dma_start(out=raw[:, j, :], in_=rows[j])
             return raw
 
-        w2_raw = {(0, 1): load_w2(0, 1)}
+        w2_raw = {(0, 1): load_w2_columns("w2_raw01", 1, 0, PASS, 0)}
         load_scale_rows(w4_s, w4_scales)
         nc.sync.dma_start(out=w4_w[:], in_=w4_words.rearrange("a p c i -> p a (c i)").bitcast(I32))
         w2_raw[(1, 0)] = load_w2(1, 0)
         w3_raw = {0: load_w3(0, None)}
-        w2_raw[(1, 1)] = load_w2(1, 1)
+        w2_raw[(1, 1)] = load_w2_columns("w2_raw11", 1, PASS, PASS, 8 * S)
         nc.sync.dma_start(out=gy_sb[:], in_=gy.rearrange("(p t) -> p t", t=4))
         nc.sync.dma_start(out=by_sb[:], in_=by.rearrange("(p t) -> p t", t=4))
         nc.gpsimd.tensor_tensor(gby[:], by_sb[:], gy_sb[:], MULT)
@@ -161,7 +164,20 @@ def tile_list_inlining_adviser_kernel(
                 bias=bias1[:, g, 4 * t : 4 * t + 1],
             )
 
+        def pick_by_quarters(g, t, h, runs):
+            by_quarter = picked[g][:].rearrange("p t m -> p (t m)").rearrange(
+                "p (q t c) -> p q t c", q=Q, t=4
+            )
+            for first, last in runs:
+                nc.vector.tensor_copy(
+                    by_quarter[:, first:last, t, :], h.indirect(pos_sb[:, 8 * first : 8 * last])
+                )
+
         def pick(g, t, h, parts=1):
+            if g < 2:
+                runs = [(3, 4), (0, 3)] if t < 2 else [(0, 4)] if parts == 1 else [(0, 2), (2, 4)]
+                pick_by_quarters(g, t, h, runs)
+                return
             for part in range(parts):
                 entries = slice(M // parts * part, M // parts * (part + 1))
                 columns = slice(entries.start // 16, entries.stop // 16)
@@ -243,9 +259,9 @@ def tile_list_inlining_adviser_kernel(
             return slice(M // 2 * half, M // 2 * (half + 1))
 
         def held_back_slices(g, last_parts):
-            both = held([P, 2, S], F32, "h_held%d" % g, "w2_raw%d1" % g)
             for n in range(2):
-                scope_slice(*HELD_BACK[g][n], both[:, n, :], Q + 2 * n, last_parts if n else 1)
+                h = held([P, S], F32, "h_held%d%d" % (g, n), 4 * S * (2 * g + n))
+                scope_slice(*HELD_BACK[g][n], h[:], Q + 2 * n, last_parts if n else 1)
 
         def call_projection(w2_pass, q):
             bank = psum_bank([P, 4, P], Q + q)
@@ -265,9 +281,12 @@ def tile_list_inlining_adviser_kernel(
             return bank
 
         def multiply(z_rounded, g, q, bank):
+            scopes = picked[g][:, :, P * q : P * (q + 1)]
+            if g < 2:
+                scopes = picked[g][:, q, :].rearrange("p (t c) -> p t c", t=4)
             nc.vector.tensor_tensor(
                 z_rounded.rearrange("p (c i t) -> p c t i", i=2, t=4),
-                picked[g][:, :, P * q : P * (q + 1)].rearrange("p t (c i) -> p c t i", i=2),
+                scopes.rearrange("p t (c i) -> p c t i", i=2),
                 bank[:].rearrange("p t (c i) -> p c t i", i=2),
                 MULT,
             )
@@ -278,9 +297,27 @@ def tile_list_inlining_adviser_kernel(
                 multiply(zb[:, PASS * q : PASS * (q + 1)], g, q, call_projection(w2_pass, q))
             return zb
 
+        beside_picks = []
         for n in range(2, len(EARLY)):
             scope_slice(*EARLY[n], held([P, S], F32, "h%d" % n)[:], 2 * (n % 4))
-        w2q = [quantised("w2_00", w2_bf00), prepare_w2(0, 1, "h01")]
+            if n in (3, 4):
+                t = n - 1
+                rounded = held([P, PASS], BF16, "w2_bf01%d" % t, "h%d" % n)
+                source = w2_raw[(0, 1)][:].rearrange("p j (u t s) -> p t u s j", t=4, s=4)
+                nc.gpsimd.tensor_scalar(
+                    rounded[:].rearrange("p (u s j) -> p u s j", s=4, j=4),
+                    source[:, t], 1.0, 0.0, MULT, ADD,
+                )
+                beside_picks.append(rounded)
+        lower = held([P, 2 * PASS], BF16, "w2_bf01", "h01")
+        nc.scalar.copy(
+            out=lower[:].rearrange("p (t u s j) -> p t u j s", t=2, s=4, j=4),
+            in_=w2_raw[(0, 1)][:].rearrange("p j (u t s) -> p t u j s", t=4, s=4)[:, 0:2],
+        )
+        w2q = [quantised("w2_00", w2_bf00), mx_tiles("w2_01", "h5")]
+        for i in range(2):
+            quantise(w2q[1], slice(P * (2 + i), P * (3 + i)), beside_picks[i][:])
+        quantise(w2q[1], slice(0, 2 * P), lower[:])
 
         w4_wd = held([P, A, N], I32, "w4_wd")
         w4_sd = held([P, N], U8, "w4_sd")
@@ -294,7 +331,7 @@ def tile_list_inlining_adviser_kernel(
         )
 
         held_back_slices(0, 2)
-        w3_bf01 = round_w3_beside_products(0, "w2_raw01")
+        w3_bf01 = round_w3_beside_products(0, 4 * S)
         zb0 = products(0, w2q, "h3")
 
         w2q = [prepare_w2(1, 0, "tab_w")]
@@ -302,10 +339,10 @@ def tile_list_inlining_adviser_kernel(
         w2q.append(prepare_w2(1, 1, "h2"))
         w3_bf00 = round_w3_pair(0, 0, held([P, 2 * N], BF16, "w3_bf00", "h4")[:])
         held_back_slices(1, 1)
-        w3q0 = mx_tiles("w3_0", "w2_raw11")
+        w3q0 = mx_tiles("w3_0", 12 * S)
         quantise_pairs(w3q0, (w3_bf00, w3_bf01))
         w3_bf21 = round_w3_beside_products(2, "h4")
-        zb1 = products(1, w2q, "w2_raw01")
+        zb1 = products(1, w2q, 4 * S)
 
         banks = [psum_bank([P, 4, P], q) for q in range(Q)]
 

@@ -300,8 +300,8 @@ def tile_list_inlining_adviser_kernel(
         beside_picks = []
         for n in range(2, len(EARLY)):
             scope_slice(*EARLY[n], held([P, S], F32, "h%d" % n)[:], 2 * (n % 4))
-            if n in (3, 4):
-                t = n - 1
+            if n in (3, 4, 5, 6):
+                t = n - 3
                 rounded = held([P, PASS], BF16, "w2_bf01%d" % t, "h%d" % n)
                 source = w2_raw[(0, 1)][:].rearrange("p j (u t s) -> p t u s j", t=4, s=4)
                 nc.gpsimd.tensor_scalar(
@@ -309,15 +309,9 @@ def tile_list_inlining_adviser_kernel(
                     source[:, t], 1.0, 0.0, MULT, ADD,
                 )
                 beside_picks.append(rounded)
-        lower = held([P, 2 * PASS], BF16, "w2_bf01", "h01")
-        nc.scalar.copy(
-            out=lower[:].rearrange("p (t u s j) -> p t u j s", t=2, s=4, j=4),
-            in_=w2_raw[(0, 1)][:].rearrange("p j (u t s) -> p t u j s", t=4, s=4)[:, 0:2],
-        )
-        w2q = [quantised("w2_00", w2_bf00), mx_tiles("w2_01", "h5")]
-        for i in range(2):
-            quantise(w2q[1], slice(P * (2 + i), P * (3 + i)), beside_picks[i][:])
-        quantise(w2q[1], slice(0, 2 * P), lower[:])
+        w2q = [quantised("w2_00", w2_bf00), mx_tiles("w2_01", "h7")]
+        for t in range(4):
+            quantise(w2q[1], slice(P * t, P * (t + 1)), beside_picks[t][:])
 
         w4_wd = held([P, A, N], I32, "w4_wd")
         w4_sd = held([P, N], U8, "w4_sd")

@@ -23,8 +23,8 @@ G = H // PASS
 A = K2 // PASS
 Q = M // P
 UNITS = PASS // 16
-EARLY = [(2, t) for t in range(4)] + [(g, t) for g in range(2) for t in range(2)]
-HELD_BACK = [[(g, t) for t in range(2, 4)] for g in range(2)]
+EARLY = [(2, t) for t in range(4)] + [(0, 0), (0, 1), (1, 0), (1, 1), (0, 3)]
+HELD_BACK = [[(0, 2)], [(1, 2), (1, 3)]]
 
 
 def tile_list_inlining_adviser_kernel(
@@ -164,19 +164,31 @@ def tile_list_inlining_adviser_kernel(
                 bias=bias1[:, g, 4 * t : 4 * t + 1],
             )
 
-        def pick_by_quarters(g, t, h, runs):
-            by_quarter = picked[g][:].rearrange("p t m -> p (t m)").rearrange(
-                "p (q t c) -> p q t c", q=Q, t=4
-            )
-            for first, last in runs:
-                nc.vector.tensor_copy(
-                    by_quarter[:, first:last, t, :], h.indirect(pos_sb[:, 8 * first : 8 * last])
-                )
+        last_quarter = {}
+
+        def three_quarters(g):
+            flat = picked[g][:].rearrange("p t m -> p (t m)")
+            return flat.rearrange("p (q t c) -> p q t c", q=Q, t=4)[:, 0:3]
+
+        def pick_last_quarter(g, t, h):
+            if g not in last_quarter:
+                last_quarter[g] = held([P, 4, P], F32, "picked_last%d" % g, 4 * S + 2 * S * g)
+            nc.vector.tensor_copy(last_quarter[g][:, t, :], h.indirect(pos_sb[:, 24:32]))
+
+        waiting = []
 
         def pick(g, t, h, parts=1):
             if g < 2:
-                runs = [(3, 4), (0, 3)] if t < 2 else [(0, 4)] if parts == 1 else [(0, 2), (2, 4)]
-                pick_by_quarters(g, t, h, runs)
+                late = (g, t) in ((0, 2), (1, 2), (1, 3))
+                if late:
+                    for earlier in waiting:
+                        pick_last_quarter(*earlier)
+                    waiting.clear()
+                nc.vector.tensor_copy(three_quarters(g)[:, :, t, :], h.indirect(pos_sb[:, 0:24]))
+                if late:
+                    pick_last_quarter(g, t, h)
+                else:
+                    waiting.append((g, t, h))
                 return
             for part in range(parts):
                 entries = slice(M // parts * part, M // parts * (part + 1))
@@ -259,7 +271,7 @@ def tile_list_inlining_adviser_kernel(
             return slice(M // 2 * half, M // 2 * (half + 1))
 
         def held_back_slices(g, last_parts):
-            for n in range(2):
+            for n in range(len(HELD_BACK[g])):
                 h = held([P, S], F32, "h_held%d%d" % (g, n), 4 * S * (2 * g + n))
                 scope_slice(*HELD_BACK[g][n], h[:], Q + 2 * n, last_parts if n else 1)
 
@@ -283,7 +295,7 @@ def tile_list_inlining_adviser_kernel(
         def multiply(z_rounded, g, q, bank):
             scopes = picked[g][:, :, P * q : P * (q + 1)]
             if g < 2:
-                scopes = picked[g][:, q, :].rearrange("p (t c) -> p t c", t=4)
+                scopes = three_quarters(g)[:, q] if q < 3 else last_quarter[g][:]
             nc.vector.tensor_tensor(
                 z_rounded.rearrange("p (c i t) -> p c t i", i=2, t=4),
                 scopes.rearrange("p t (c i) -> p c t i", i=2),
@@ -297,21 +309,18 @@ def tile_list_inlining_adviser_kernel(
                 multiply(zb[:, PASS * q : PASS * (q + 1)], g, q, call_projection(w2_pass, q))
             return zb
 
-        beside_picks = []
         for n in range(2, len(EARLY)):
             scope_slice(*EARLY[n], held([P, S], F32, "h%d" % n)[:], 2 * (n % 4))
-            if n in (3, 4, 5, 6):
-                t = n - 3
-                rounded = held([P, PASS], BF16, "w2_bf01%d" % t, "h%d" % n)
+            if n == 3:
                 source = w2_raw[(0, 1)][:].rearrange("p j (u t s) -> p t u s j", t=4, s=4)
-                nc.gpsimd.tensor_scalar(
-                    rounded[:].rearrange("p (u s j) -> p u s j", s=4, j=4),
-                    source[:, t], 1.0, 0.0, MULT, ADD,
-                )
-                beside_picks.append(rounded)
-        w2q = [quantised("w2_00", w2_bf00), mx_tiles("w2_01", "h7")]
-        for t in range(4):
-            quantise(w2q[1], slice(P * t, P * (t + 1)), beside_picks[t][:])
+                rounded = held([P, 4, PASS], BF16, "w2_bf01", "h3")
+                for t in range(4):
+                    nc.gpsimd.tensor_scalar(
+                        rounded[:, t, :].rearrange("p (u s j) -> p u s j", s=4, j=4),
+                        source[:, t], 1.0, 0.0, MULT, ADD,
+                    )
+        w2q = [quantised("w2_00", w2_bf00), mx_tiles("w2_01")]
+        quantise(w2q[1], slice(0, PASS), rounded[:].rearrange("p t c -> p (t c)"))
 
         w4_wd = held([P, A, N], I32, "w4_wd")
         w4_sd = held([P, N], U8, "w4_sd")
@@ -325,7 +334,7 @@ def tile_list_inlining_adviser_kernel(
         )
 
         held_back_slices(0, 2)
-        w3_bf01 = round_w3_beside_products(0, 4 * S)
+        w3_bf01 = round_w3_beside_products(0, 0)
         zb0 = products(0, w2q, "h3")
 
         w2q = [prepare_w2(1, 0, "tab_w")]
@@ -336,7 +345,7 @@ def tile_list_inlining_adviser_kernel(
         w3q0 = mx_tiles("w3_0", 12 * S)
         quantise_pairs(w3q0, (w3_bf00, w3_bf01))
         w3_bf21 = round_w3_beside_products(2, "h4")
-        zb1 = products(1, w2q, 4 * S)
+        zb1 = products(1, w2q, 0)
 
         banks = [psum_bank([P, 4, P], q) for q in range(Q)]
 

@@ -23,8 +23,20 @@ G = H // PASS
 A = K2 // PASS
 Q = M // P
 UNITS = PASS // 16
-EARLY = [(2, t) for t in range(4)] + [(0, 0), (0, 1), (1, 0), (1, 1), (0, 3)]
-HELD_BACK = [[(0, 2)], [(1, 2), (1, 3)]]
+KIB = 1024
+REGIONS = (
+    [("w2_%d%d" % (g, a), 14 if (g, a) == (1, 1) else 8) for g in range(G) for a in range(A) if g or a]
+    + [("w3_%d" % g, 8) for g in range(G)]
+    + [("half%d" % i, 4) for i in range(2)]
+    + [("h%d" % n, 4) for n in range(4 * G)]
+    + [("picked0", 6), ("picked1", 6)]
+)
+ORDER = [2, 0, 1]
+
+
+def region_start(name):
+    names = [region for region, size in REGIONS]
+    return KIB * sum(size for region, size in REGIONS[: names.index(name)])
 
 
 def tile_list_inlining_adviser_kernel(
@@ -40,15 +52,16 @@ def tile_list_inlining_adviser_kernel(
         def psum_bank(shape, index):
             return psum.tile(shape, F32, name="bank%d" % index)
 
-        def held(shape, dtype, name, on=None):
-            if isinstance(on, int):
-                return stage.tile(shape, dtype, name=name, align_bytes=64, offset=on)
-            return keep.tile(shape, dtype, name=name, tag=on or name, align_bytes=64)
+        def held(shape, dtype, name, on=None, kib=0):
+            if on is None:
+                return keep.tile(shape, dtype, name=name, align_bytes=64)
+            offset = region_start(on) + KIB * kib
+            return stage.tile(shape, dtype, name=name, align_bytes=64, offset=offset)
 
-        def load_scale_rows(scale_tile, scales, queue=nc.sync):
+        def load_scale_rows(scale_tile, scales):
             passes = scales.shape[0]
             for quad in range(4):
-                queue.dma_start(
+                nc.sync.dma_start(
                     out=scale_tile[32 * quad : 32 * quad + 4 * passes, :].bitcast(I32),
                     in_=scales[:, 4 * quad : 4 * quad + 4, :].bitcast(I32),
                 )
@@ -68,23 +81,31 @@ def tile_list_inlining_adviser_kernel(
         w4_w = held([P, A, N], I32, "w4_w")
         w4_s = held([P, N], U8, "w4_s")
         by_sb = held([P, 4], F32, "by_sb")
+        gy_sb = held([P, 4], F32, "gy_sb")
+        bias1 = held([P, G, 16], F32, "bias1")
         nc.gpsimd.memset(tab_s[:].bitcast(I32), 0)
         for scale_tile in (w1_s, tab2_s, w4_s):
             nc.vector.memset(scale_tile[:].bitcast(I32), 0)
-
-        bias1 = held([P, G, 16], F32, "bias1")
-        gy_sb = held([P, 4], F32, "gy_sb")
-        gby = held([P, 4], F32, "gby")
 
         b1_view = b1.rearrange("(g u k) -> u g k", g=G, k=16)
 
         def load_bias1(s, queue):
             queue.dma_start(out=bias1[s:P:4, :, 0:13], in_=b1_view[:, :, s : s + 13])
 
-        def load_w2_columns(name, a, first, count, on=None):
-            raw = held([P, 4, count], F32, name, on)
+        def load_w2_columns(name, a, first, count):
+            raw = held([P, 4, count], F32, name + "_raw", name, 3 if name == "w2_11" else 0)
             rows = w2[PASS * a : PASS * (a + 1), first : first + count]
             nc.sync.dma_start(out=raw[:], in_=rows.rearrange("(p j) c -> p j c", j=4))
+            return raw
+
+        def load_w2(g, a):
+            return load_w2_columns("w2_%d%d" % (g, a), a, PASS * g, PASS)
+
+        def load_w3(g):
+            raw = held([P, 4, N], F32, "w3_raw%d" % g, "w3_%d" % g)
+            rows = w3[PASS * g : PASS * (g + 1), :].rearrange("(u j s) n -> j u s n", j=4, s=4)
+            for j in range(4):
+                nc.sync.dma_start(out=raw[:, j, :], in_=rows[j])
             return raw
 
         nc.sync.dma_start(out=w1_w[:], in_=w1_words[0].bitcast(I32))
@@ -93,40 +114,30 @@ def tile_list_inlining_adviser_kernel(
         load_scale_rows(tab_s, tab_scales)
         nc.sync.dma_start(out=tab_w[:], in_=words_view(tab_words[0]))
         load_scale_rows(w1_s, w1_scales)
-        first_piece = [load_w2_columns("w2_half0", 0, 0, PASS // 2)]
+        first_piece = [load_w2_columns("half0", 0, 0, PASS // 2)]
         load_bias1(0, nc.sync)
         for s in range(1, 4):
             load_bias1(s, nc.gpsimd)
         load_scale_rows(tab2_s, tab2_scales)
         nc.sync.dma_start(pos_sb[:], pos1)
         nc.sync.dma_start(out=tab2_w[0][:], in_=words_view(tab2_words[0]))
-        first_piece.append(load_w2_columns("w2_half1", 0, PASS // 2, PASS // 2))
+        first_piece.append(load_w2_columns("half1", 0, PASS // 2, PASS // 2))
         nc.sync.dma_start(out=tab2_w[1][:], in_=words_view(tab2_words[1]))
-
-        def load_w2(g, a):
-            return load_w2_columns("w2_raw%d%d" % (g, a), a, PASS * g, PASS)
-
-        def load_w3(g, on):
-            raw = held([P, 4, N], F32, "w3_raw%d" % g, on)
-            rows = w3[PASS * g : PASS * (g + 1), :].rearrange("(u j s) n -> j u s n", j=4, s=4)
-            for j in range(4):
-                nc.sync.dma_start(out=raw[:, j, :], in_=rows[j])
-            return raw
-
-        w2_raw = {(0, 1): load_w2_columns("w2_raw01", 1, 0, PASS, 0)}
+        w2_raw = {(0, 1): load_w2(0, 1)}
         load_scale_rows(w4_s, w4_scales)
-        nc.sync.dma_start(out=w4_w[:], in_=w4_words.rearrange("a p c i -> p a (c i)").bitcast(I32))
         w2_raw[(1, 0)] = load_w2(1, 0)
-        w3_raw = {0: load_w3(0, None)}
-        w2_raw[(1, 1)] = load_w2_columns("w2_raw11", 1, PASS, PASS, 8 * S)
+        w3_raw = {0: load_w3(0)}
+        w2_raw[(1, 1)] = load_w2(1, 1)
         nc.sync.dma_start(out=gy_sb[:], in_=gy.rearrange("(p t) -> p t", t=4))
         nc.sync.dma_start(out=by_sb[:], in_=by.rearrange("(p t) -> p t", t=4))
-        nc.gpsimd.tensor_tensor(gby[:], by_sb[:], gy_sb[:], MULT)
+        nc.sync.dma_start(out=w4_w[:], in_=w4_words.rearrange("a p c i -> p a (c i)").bitcast(I32))
         for a in range(A):
             w2_raw[(2, a)] = load_w2(2, a)
+        for g in (2, 1):
+            w3_raw[g] = load_w3(g)
 
         v_s = held([P, S], U8, "v_s")
-        v_w = [held([P, PASS], U32, "v_w0")]
+        v_w = [held([P, PASS], U32, "v_w%d" % c) for c in range(2)]
         nc.vector.tensor_copy(v_s[:], tab_s[:].indirect(offs_sb[:]))
         nc.vector.tensor_copy(v_w[0][:], tab_w[:].bitcast(U32).indirect(offs_sb[:, 0:32]))
         w1_wd = held([P, H // 2], I32, "w1_wd")
@@ -139,15 +150,15 @@ def tile_list_inlining_adviser_kernel(
             out=w1_sd[:].bitcast(U32).rearrange("p (g t c i) -> p c g t i", g=G, t=4, i=4),
             in_=w1_s[:].bitcast(U32).rearrange("p (g c i t) -> p c g t i", g=G, t=4, i=4),
         )
-        v_w.append(held([P, PASS], U32, "v_w1"))
         nc.vector.tensor_copy(v_w[1][:], tab_w[:].bitcast(U32).indirect(offs_sb[:, 32:64]))
-
         v2_s = held([P, M], U8, "v2_s")
         nc.vector.tensor_copy(v2_s[:], tab2_s[:].indirect(offs2_sb[:]))
 
-        picked = [held([P, 4, M], F32, "picked%d" % g) for g in range(G)]
+        places = {9: ("w2_10", 0), 10: ("w2_10", 4), 11: ("w2_11", 10)}
+        h = [held([P, S], F32, "h%d" % n, *places.get(n, ("h%d" % n, 0))) for n in range(4 * G)]
 
-        def scope_half(g, t, h, c, bank_index):
+        def scope_half(n, c, bank_index):
+            g, t = ORDER[n // 4], n % 4
             i = 4 * g + t
             bank = psum_bank([P, PASS], bank_index)
             nc.tensor.matmul_mx(
@@ -160,91 +171,51 @@ def tile_list_inlining_adviser_kernel(
                 stop=True,
             )
             nc.scalar.activation(
-                h[:, PASS * c : PASS * (c + 1)], bank[:], IDENT,
+                h[n][:, PASS * c : PASS * (c + 1)], bank[:], IDENT,
                 bias=bias1[:, g, 4 * t : 4 * t + 1],
             )
 
-        last_quarter = {}
-
-        def three_quarters(g):
-            flat = picked[g][:].rearrange("p t m -> p (t m)")
-            return flat.rearrange("p (q t c) -> p q t c", q=Q, t=4)[:, 0:3]
-
-        def pick_last_quarter(g, t, h):
-            if g not in last_quarter:
-                last_quarter[g] = held([P, 4, P], F32, "picked_last%d" % g, 4 * S + 2 * S * g)
-            nc.vector.tensor_copy(last_quarter[g][:, t, :], h.indirect(pos_sb[:, 24:32]))
-
-        waiting = []
-
-        def pick(g, t, h, parts=1):
-            if g < 2:
-                late = (g, t) in ((0, 2), (1, 2), (1, 3))
-                if late:
-                    for earlier in waiting:
-                        pick_last_quarter(*earlier)
-                    waiting.clear()
-                nc.vector.tensor_copy(three_quarters(g)[:, :, t, :], h.indirect(pos_sb[:, 0:24]))
-                if late:
-                    pick_last_quarter(g, t, h)
-                else:
-                    waiting.append((g, t, h))
-                return
-            for part in range(parts):
-                entries = slice(M // parts * part, M // parts * (part + 1))
-                columns = slice(entries.start // 16, entries.stop // 16)
-                nc.vector.tensor_copy(picked[g][:, t, entries], h.indirect(pos_sb[:, columns]))
-
-        def scope_slice(g, t, h, first_bank, parts=1):
+        def scope_slice(n, first_bank):
             for c in range(2):
-                scope_half(g, t, h, c, first_bank + c)
-            pick(g, t, h, parts)
+                scope_half(n, c, first_bank + c)
+
+        def pick_whole(n, picked):
+            nc.vector.tensor_copy(picked[:, n % 4, :], h[n][:].indirect(pos_sb[:]))
+
+        def pick_three_quarters(n, picked):
+            nc.vector.tensor_copy(picked[:, :, n % 4, :], h[n][:].indirect(pos_sb[:, 0:24]))
+
+        def pick_last_quarter(n, picked):
+            nc.vector.tensor_copy(picked[:, n % 4, :], h[n][:].indirect(pos_sb[:, 24:32]))
 
         def gather_calls(a):
             words = held([P, M], U32, "v2_w%d" % a)
             nc.vector.tensor_copy(words[:], tab2_w[a][:].bitcast(U32).indirect(offs2_sb[:]))
             return words
 
-        def round_w2_columns(raw, rounded, units, copy=nc.scalar.copy):
-            copy(
-                out=rounded[:].rearrange("p (t u s j) -> p t u j s", t=4, s=4, j=4)[:, :, units],
-                in_=raw[:].rearrange("p j (u t s) -> p t u j s", t=4, s=4),
+        def round_w2(raw, rounded, slices):
+            nc.scalar.copy(
+                out=rounded, in_=raw[:].rearrange("p j (u t s) -> p t u j s", t=4, s=4)[:, slices]
             )
 
-        w2_bf00 = held([P, 4 * PASS], BF16, "w2_bf00")
-        for half in range(2):
-            units = slice(UNITS // 2 * half, UNITS // 2 * (half + 1))
-            copy = nc.vector.tensor_copy if half else nc.scalar.copy
-            round_w2_columns(first_piece[half], w2_bf00, units, copy)
+        def dealt(tile_ap, slices):
+            return tile_ap.rearrange("p (t u s j) -> p t u j s", t=slices, s=4, j=4)
 
-        first_two = held([P, 2, S], F32, "h01")
-        for c in range(2):
-            for n in range(2):
-                scope_half(*EARLY[n], first_two[:, n, :], c, 2 * n + c)
-        for n in range(2):
-            pick(*EARLY[n], first_two[:, n, :])
-        v2_w = [gather_calls(a) for a in range(A)]
-        w3_raw[2] = load_w3(2, "tab2_w0")
-        w3_raw[1] = load_w3(1, "tab2_w1")
+        def round_w2_beside(raw, rounded, first):
+            source = raw[:].rearrange("p j (u t s) -> p t u s j", t=4, s=4)
+            for i in range(rounded.shape[1] // PASS):
+                nc.gpsimd.tensor_scalar(
+                    rounded[:, PASS * i : PASS * (i + 1)].rearrange("p (u s j) -> p u s j", s=4, j=4),
+                    source[:, first + i], 1.0, 0.0, MULT, ADD,
+                )
 
-        def mx_tiles(name, on=None):
-            return held([P, PASS], U32, name + "_c", on), held([P, PASS], U8, name + "_s")
-
-        def quantise(operand, cols, rounded):
-            codes, scales = operand
-            nc.vector.quantize_mx(
-                out=codes[:, cols].bitcast(FP8X4), scales=scales[:, cols], in_=rounded
+        def round_w3_beside(g, rounded, first):
+            slices = rounded.shape[1] // N
+            nc.gpsimd.tensor_scalar(
+                rounded[:].rearrange("p (t m j) -> p m t j", t=slices, j=4),
+                w3_raw[g][:].rearrange("p j (m t) -> p m t j", t=4)[:, :, first : first + slices],
+                1.0, 0.0, MULT, ADD,
             )
-
-        def quantised(name, rounded, on=None):
-            operand = mx_tiles(name, on)
-            quantise(operand, slice(0, PASS), rounded[:])
-            return operand
-
-        def prepare_w2(g, a, on):
-            rounded = held([P, 4 * PASS], BF16, "w2_bf%d%d" % (g, a), on)
-            round_w2_columns(w2_raw[(g, a)], rounded, slice(0, UNITS))
-            return quantised("w2_%d%d" % (g, a), rounded)
 
         def round_w3_pair(g, pair, rounded):
             source = w3_raw[g][:].rearrange("p j (m t) -> p m j t", t=4)
@@ -252,28 +223,31 @@ def tile_list_inlining_adviser_kernel(
                 out=rounded.rearrange("p (t m j) -> p m j t", t=2, j=4),
                 in_=source[:, :, :, 2 * pair : 2 * pair + 2],
             )
-            return rounded
 
-        def round_w3_beside_products(g, on):
-            rounded = held([P, 2 * N], BF16, "w3_bf%d1" % g, on)
-            source = w3_raw[g][:].rearrange("p j (m t) -> p m t j", t=4)
-            nc.gpsimd.tensor_scalar(
-                rounded[:].rearrange("p (t m j) -> p m t j", t=2, j=4),
-                source[:, :, 2:4], 1.0, 0.0, MULT, ADD,
+        def mx_tiles(name, on=None, kib=0):
+            return held([P, PASS], U32, name + "_c", on, kib), held([P, PASS], U8, name + "_s")
+
+        def quantise(operand, cols, rounded):
+            codes, scales = operand
+            nc.vector.quantize_mx(
+                out=codes[:, cols].bitcast(FP8X4), scales=scales[:, cols], in_=rounded
             )
-            return rounded[:]
 
-        def quantise_pairs(operand, pairs):
-            for pair in (1, 0):
-                quantise(operand, slice(2 * P * pair, 2 * P * (pair + 1)), pairs[pair])
+        def quantised(name, rounded, on=None, kib=0):
+            operand = mx_tiles(name, on, kib)
+            quantise(operand, slice(0, PASS), rounded[:])
+            return operand
 
-        def half_columns(half):
-            return slice(M // 2 * half, M // 2 * (half + 1))
+        def quantised_pairs(name, lower, upper, on=None, kib=0):
+            operand = mx_tiles(name, on, kib)
+            quantise(operand, slice(2 * P, 4 * P), upper[:])
+            quantise(operand, slice(0, 2 * P), lower[:])
+            return operand
 
-        def held_back_slices(g, last_parts):
-            for n in range(len(HELD_BACK[g])):
-                h = held([P, S], F32, "h_held%d%d" % (g, n), 4 * S * (2 * g + n))
-                scope_slice(*HELD_BACK[g][n], h[:], Q + 2 * n, last_parts if n else 1)
+        def prepare_w2(g, a, on, codes_on=None, codes_kib=0):
+            rounded = held([P, 4 * PASS], BF16, "w2_bf%d%d" % (g, a), on)
+            round_w2(w2_raw[(g, a)], dealt(rounded[:], 4), slice(0, 4))
+            return quantised("w2_%d%d" % (g, a), rounded, codes_on, codes_kib)
 
         def call_projection(w2_pass, q):
             bank = psum_bank([P, 4, P], Q + q)
@@ -292,10 +266,7 @@ def tile_list_inlining_adviser_kernel(
                     )
             return bank
 
-        def multiply(z_rounded, g, q, bank):
-            scopes = picked[g][:, :, P * q : P * (q + 1)]
-            if g < 2:
-                scopes = three_quarters(g)[:, q] if q < 3 else last_quarter[g][:]
+        def multiply(z_rounded, scopes, bank):
             nc.vector.tensor_tensor(
                 z_rounded.rearrange("p (c i t) -> p c t i", i=2, t=4),
                 scopes.rearrange("p t (c i) -> p c t i", i=2),
@@ -303,49 +274,95 @@ def tile_list_inlining_adviser_kernel(
                 MULT,
             )
 
-        def products(g, w2_pass, on):
-            zb = held([P, 4 * M], BF16, "zb%d" % g, on)
-            for q in range(Q):
-                multiply(zb[:, PASS * q : PASS * (q + 1)], g, q, call_projection(w2_pass, q))
-            return zb
+        def shared_w2(g, a, beside, first, on, kib, codes_on=None, codes_kib=0):
+            rounded = held([P, first * PASS], BF16, "w2_bf%d%d" % (g, a), on, kib)
+            round_w2(w2_raw[(g, a)], dealt(rounded[:], first), slice(0, first))
+            operand = mx_tiles("w2_%d%d" % (g, a), codes_on, codes_kib)
+            quantise(operand, slice(first * P, 4 * P), beside[:])
+            quantise(operand, slice(0, first * P), rounded[:])
+            return operand
 
-        for n in range(2, len(EARLY)):
-            scope_slice(*EARLY[n], held([P, S], F32, "h%d" % n)[:], 2 * (n % 4))
-            if n == 3:
-                source = w2_raw[(0, 1)][:].rearrange("p j (u t s) -> p t u s j", t=4, s=4)
-                rounded = held([P, 4, PASS], BF16, "w2_bf01", "h3")
-                for t in range(4):
-                    nc.gpsimd.tensor_scalar(
-                        rounded[:, t, :].rearrange("p (u s j) -> p u s j", s=4, j=4),
-                        source[:, t], 1.0, 0.0, MULT, ADD,
-                    )
-        w2q = [quantised("w2_00", w2_bf00), mx_tiles("w2_01")]
-        quantise(w2q[1], slice(0, PASS), rounded[:].rearrange("p t c -> p (t c)"))
+        def products(zb, first_three, last, b_banks, quarters):
+            for q in quarters:
+                scopes = first_three[:, q] if q < 3 else last[:]
+                multiply(zb[:, PASS * q : PASS * (q + 1)], scopes, b_banks[q])
 
-        w4_wd = held([P, A, N], I32, "w4_wd")
-        w4_sd = held([P, N], U8, "w4_sd")
-        nc.vector.tensor_copy(
-            out=w4_wd[:].rearrange("p a (t c i) -> p a c t i", t=4, i=4),
-            in_=w4_w[:].rearrange("p a (c i t) -> p a c t i", t=4, i=4),
-        )
+        w2_bf00 = held([P, 4 * PASS], BF16, "w2_bf00")
+        first_units = [slice(0, UNITS // 2), slice(UNITS // 2, UNITS)]
+        round_w2(first_piece[0], dealt(w2_bf00[:], 4)[:, :, first_units[0]], slice(0, 4))
+        picked2 = held([P, 4, M], F32, "picked2")
+        for c in range(2):
+            for n in range(2):
+                scope_half(n, c, 2 * n + c)
+        for n in range(2):
+            pick_whole(n, picked2)
+        v2_w = [gather_calls(a) for a in range(A)]
+        round_w2(first_piece[1], dealt(w2_bf00[:], 4)[:, :, first_units[1]], slice(0, 4))
+        w2q = [quantised("w2_00", w2_bf00)]
+        for n in range(2, 4):
+            scope_slice(n, 2 * n)
+            pick_whole(n, picked2)
+
+        w2_bf01 = held([P, 4 * PASS], BF16, "w2_bf01", "h3")
+        round_w2_beside(w2_raw[(0, 1)], w2_bf01, 0)
+        picked0 = held([P, 3, 4, P], F32, "picked0", "picked0")
+        picked1 = held([P, 3, 4, P], F32, "picked1", "picked1")
+        for n in range(4, 9):
+            scope_slice(n, 2 * (n % 2))
+            pick_three_quarters(n, picked0 if n < 8 else picked1)
+        w2q.append(quantised("w2_01", w2_bf01))
+        w4_sd = held([P, N], U8, "w4_sd", "w2_01", 2)
         nc.vector.tensor_copy(
             out=w4_sd[:].rearrange("p (t c i) -> p c t i", t=4, i=16),
             in_=w4_s[:].rearrange("p (c i t) -> p c t i", t=4, i=16),
         )
+        last0 = held([P, 4, P], F32, "last0", "w2_01")
+        for n in range(4, 8):
+            pick_last_quarter(n, last0)
+        b_banks = [call_projection(w2q, q) for q in range(Q)]
+        w3_pairs = [held([P, 2 * N], BF16, "w3_bf0%d" % i, "h7", 2 * i) for i in range(2)]
+        for i in range(2):
+            round_w3_beside(0, w3_pairs[i], 2 * i)
+        zb0 = held([P, 4 * M], BF16, "zb0", "h4")
+        products(zb0, picked0, last0, b_banks, range(Q))
 
-        held_back_slices(0, 2)
-        w3_bf01 = round_w3_beside_products(0, 0)
-        zb0 = products(0, w2q, "h3")
+        w2_bf10 = held([P, 4 * PASS], BF16, "w2_bf10", "half0")
+        round_w2(w2_raw[(1, 0)], dealt(w2_bf10[:], 4), slice(0, 4))
+        for n in range(9, 11):
+            scope_slice(n, 2 * (n % 2))
+            pick_three_quarters(n, picked1)
+        w2_bf11 = held([P, 4 * PASS], BF16, "w2_bf11", "h1")
+        round_w2(w2_raw[(1, 1)], dealt(w2_bf11[:], 4), slice(0, 4))
+        w2q = [quantised("w2_10", w2_bf10, "w2_11", 4)]
+        z = [quantised("z0", zb0, "w2_11", 6)]
+        w2q.append(quantised("w2_11", w2_bf11))
+        w3q = {0: quantised_pairs("w3_0", w3_pairs[0], w3_pairs[1], "w2_11", 8)}
+        scope_slice(11, 2)
+        last1 = held([P, 4, P], F32, "last1", "h1")
+        for n in range(8, 12):
+            pick_last_quarter(n, last1)
+        pick_three_quarters(11, picked1)
+        b_banks = {q: call_projection(w2q, q) for q in (3, 0, 1, 2)}
+        w3_bf2_upper = held([P, 2 * N], BF16, "w3_bf2u", "w2_10", 4)
+        round_w3_beside(2, w3_bf2_upper, 2)
+        beside = held([P, PASS], BF16, "w2_beside21", "w2_10", 6)
+        round_w2_beside(w2_raw[(2, 1)], beside, 3)
+        gby = held([P, 4], F32, "gby", "w2_10", 7)
+        nc.gpsimd.tensor_tensor(gby[:], by_sb[:], gy_sb[:], MULT)
+        zb1 = held([P, 4 * M], BF16, "zb1", "h8")
+        products(zb1, picked1, last1, b_banks, (3, 0, 1, 2))
 
-        w2q = [prepare_w2(1, 0, "tab_w")]
-        z0 = quantised("z0", zb0, "w2_raw10")
-        w2q.append(prepare_w2(1, 1, "h2"))
-        w3_bf00 = round_w3_pair(0, 0, held([P, 2 * N], BF16, "w3_bf00", "h4")[:])
-        held_back_slices(1, 1)
-        w3q0 = mx_tiles("w3_0", 12 * S)
-        quantise_pairs(w3q0, (w3_bf00, w3_bf01))
-        w3_bf21 = round_w3_beside_products(2, "h4")
-        zb1 = products(1, w2q, 0)
+        w4_wd = held([P, A, N], I32, "w4_wd", "w2_11")
+        nc.scalar.copy(
+            out=w4_wd[:].bitcast(U32).rearrange("p a (t c i) -> p a c t i", t=4, i=4),
+            in_=w4_w[:].bitcast(U32).rearrange("p a (c i t) -> p a c t i", t=4, i=4),
+        )
+        w2q = [prepare_w2(2, 0, "h2", "picked1"), shared_w2(2, 1, beside, 3, "w2_20", 0, "picked1", 2)]
+        b_banks = [call_projection(w2q, q) for q in range(Q)]
+        z.append(quantised("z1", zb1))
+        w3_bf2_lower = held([P, 2 * N], BF16, "w3_bf2l", "w2_21")
+        round_w3_pair(2, 0, w3_bf2_lower[:])
+        w3q[2] = quantised_pairs("w3_2", w3_bf2_lower, w3_bf2_upper, "picked1", 4)
 
         banks = [psum_bank([P, 4, P], q) for q in range(Q)]
 
@@ -365,39 +382,32 @@ def tile_list_inlining_adviser_kernel(
         for q in range(Q):
             for a in range(A):
                 out_passes(q, (w4_wd[:, a, :], w4_sd), (v2_w[a], v2_s), 4 * a, first=(a == 0))
-            out_passes(q, w3q0, z0)
+            out_passes(q, w3q[0], z[0])
 
-        w2q = [prepare_w2(2, 0, "h5"), prepare_w2(2, 1, "h01")]
-        b_banks = [call_projection(w2q, q) for q in range(Q)]
-        late_codes = held([P, 2, PASS], U32, "z1_w3_2_c", "w2_raw21")
-        z1 = (late_codes[:, 0, :], held([P, PASS], U8, "z1_s"))
-        quantise(z1, slice(0, PASS), zb1[:])
-        w3q2 = (late_codes[:, 1, :], held([P, PASS], U8, "w3_2_s"))
-        w3_bf20 = round_w3_pair(2, 0, held([P, 2 * N], BF16, "w3_bf20", "h6")[:])
-        quantise_pairs(w3q2, (w3_bf20, w3_bf21))
-        w3_bf1 = held([P, 4 * N], BF16, "w3_bf1", "tab_w")
-        for pair in range(2):
-            round_w3_pair(1, pair, w3_bf1[:, 2 * N * pair : 2 * N * (pair + 1)])
-
-        z2 = mx_tiles("z2")
+        z.append(mx_tiles("z2"))
 
         def half_of_pass_2(half, on):
-            zb = held([P, 2 * M], BF16, "zb2%d" % half, on)
-            for i in range(2):
-                multiply(zb[:, PASS * i : PASS * (i + 1)], 2, 2 * half + i, b_banks[2 * half + i])
+            zb_half = held([P, 2 * M], BF16, "zb2%d" % half, on)
             for i in range(2):
                 q = 2 * half + i
-                quantise(z2, slice(P * q, P * (q + 1)), zb[:, PASS * i : PASS * (i + 1)])
+                scopes = picked2[:, :, P * q : P * (q + 1)]
+                multiply(zb_half[:, PASS * i : PASS * (i + 1)], scopes, b_banks[q])
+            for i in range(2):
+                q = 2 * half + i
+                quantise(z[2], slice(P * q, P * (q + 1)), zb_half[:, PASS * i : PASS * (i + 1)])
 
-        half_of_pass_2(0, "tab2_w0")
+        w3_bf1 = held([P, 4 * N], BF16, "w3_bf1", "w2_20", 4)
+        for pair in range(2):
+            round_w3_pair(1, pair, w3_bf1[:, 2 * N * pair : 2 * N * (pair + 1)])
+        half_of_pass_2(0, "w3_2")
         for q in range(2):
-            out_passes(q, w3q2, z2)
-        w3q1 = quantised("w3_1", w3_bf1)
+            out_passes(q, w3q[2], z[2])
+        w3q[1] = quantised("w3_1", w3_bf1)
         for q in range(Q):
-            out_passes(q, w3q1, z1, final=(q < 2))
-        half_of_pass_2(1, "tab2_w1")
+            out_passes(q, w3q[1], z[1], final=(q < 2))
+        half_of_pass_2(1, "w3_1")
         for q in range(2, Q):
-            out_passes(q, w3q2, z2, final=True)
+            out_passes(q, w3q[2], z[2], final=True)
 
         y_s = held([P, M], U8, "y_s")
         y_rows = out_0.rearrange("(p t) m -> p t m", t=4)
@@ -424,7 +434,7 @@ def tile_list_inlining_adviser_kernel(
             quarters = (2 * half, 2 * half + 1)
             y = [empty_bank(q) for q in quarters]
             yb = [round_y(quarters[i], y[i]) for i in range(2)]
-            y_c = held([P, M // 2], U32, "y_c%d" % half, "gby" if half else None)
+            y_c = held([P, M // 2], U32, "y_c%d" % half, "w2_10" if half else None, 7)
             for i in range(2):
                 nc.vector.quantize_mx(
                     out=y_c[:, P * i : P * (i + 1)].bitcast(FP8X4),
@@ -432,7 +442,8 @@ def tile_list_inlining_adviser_kernel(
                     in_=yb[i][:],
                 )
             nc.sync.dma_start(
-                out=words_view(out_1[0])[:, half_columns(half)], in_=y_c[:].bitcast(I32)
+                out=words_view(out_1[0])[:, M // 2 * half : M // 2 * (half + 1)],
+                in_=y_c[:].bitcast(I32),
             )
         for quad in range(4):
             queue = nc.scalar if quad % 2 else nc.sync

@@ -320,7 +320,7 @@ def tile_list_inlining_adviser_kernel(
         for n in range(4, 8):
             pick_last_quarter(n, last0)
         b_banks = [call_projection(w2q, q) for q in range(Q)]
-        w3_pairs = [held([P, 2 * N], BF16, "w3_bf0%d" % i, "h7", 2 * i) for i in range(2)]
+        w3_pairs = [held([P, 2 * N], BF16, "w3_bf0%d" % i, "h6", 2 * i) for i in range(2)]
         for i in range(2):
             round_w3_beside(0, w3_pairs[i], 2 * i)
         zb0 = held([P, 4 * M], BF16, "zb0", "h4")
@@ -343,12 +343,10 @@ def tile_list_inlining_adviser_kernel(
             pick_last_quarter(n, last1)
         pick_three_quarters(11, picked1)
         b_banks = {q: call_projection(w2q, q) for q in (3, 0, 1, 2)}
-        w3_bf2_upper = held([P, 2 * N], BF16, "w3_bf2u", "w2_10", 4)
-        round_w3_beside(2, w3_bf2_upper, 2)
         beside = held([P, PASS], BF16, "w2_beside21", "w2_10", 6)
         round_w2_beside(w2_raw[(2, 1)], beside, 3)
-        gby = held([P, 4], F32, "gby", "w2_10", 7)
-        nc.gpsimd.tensor_tensor(gby[:], by_sb[:], gy_sb[:], MULT)
+        w3_bf2_upper = held([P, 2 * N], BF16, "w3_bf2u", "w2_10", 4)
+        round_w3_beside(2, w3_bf2_upper, 2)
         zb1 = held([P, 4 * M], BF16, "zb1", "h8")
         products(zb1, picked1, last1, b_banks, (3, 0, 1, 2))
 
@@ -360,6 +358,8 @@ def tile_list_inlining_adviser_kernel(
         w2q = [prepare_w2(2, 0, "h2", "picked1"), shared_w2(2, 1, beside, 3, "w2_20", 0, "picked1", 2)]
         b_banks = [call_projection(w2q, q) for q in range(Q)]
         z.append(quantised("z1", zb1))
+        gby = held([P, 4], F32, "gby", "h8")
+        nc.vector.tensor_tensor(gby[:], by_sb[:], gy_sb[:], MULT)
         w3_bf2_lower = held([P, 2 * N], BF16, "w3_bf2l", "w2_21")
         round_w3_pair(2, 0, w3_bf2_lower[:])
         w3q[2] = quantised_pairs("w3_2", w3_bf2_lower, w3_bf2_upper, "picked1", 4)
@@ -434,7 +434,7 @@ def tile_list_inlining_adviser_kernel(
             quarters = (2 * half, 2 * half + 1)
             y = [empty_bank(q) for q in quarters]
             yb = [round_y(quarters[i], y[i]) for i in range(2)]
-            y_c = held([P, M // 2], U32, "y_c%d" % half, "w2_10" if half else None, 7)
+            y_c = held([P, M // 2], U32, "y_c%d" % half, "h8" if half else None)
             for i in range(2):
                 nc.vector.quantize_mx(
                     out=y_c[:, P * i : P * (i + 1)].bitcast(FP8X4),

from contextlib import ExitStack

import concourse.mybir as mybir

K, T, S, K2, T2, M, H, N = 512, 2048, 1024, 1024, 2048, 512, 1536, 512
FLOPS = 2 * (K * H * S + K2 * H * M + H * N * M + K2 * N * M)

F32 = mybir.dt.float32
BF16 = mybir.dt.bfloat16
I32 = mybir.dt.int32
U32 = mybir.dt.uint32
U16 = mybir.dt.uint16
U8 = mybir.dt.uint8
FP8X4 = mybir.dt.float8_e4m3fn_x4
FP4X4 = mybir.dt.float4_e2m1fn_x4
IDENT = mybir.ActivationFunctionType.Identity
MULT = mybir.AluOpType.mult
ADD = mybir.AluOpType.add

P = 128
PASS = 512
G = H // PASS
A = K2 // PASS
Q = M // P
UNITS = PASS // 16
KIB = 1024
REGIONS = (
    [("w2_%d%d" % (g, a), 14 if (g, a) == (1, 1) else 8) for g in range(G) for a in range(A) if g or a]
    + [("w3_%d" % g, 8) for g in range(G)]
    + [("half%d" % i, 4) for i in range(2)]
    + [("h%d" % n, 4) for n in range(4 * G)]
    + [("picked0", 6), ("picked1", 6)]
)
ORDER = [2, 0, 1]


def region_start(name):
    names = [region for region, size in REGIONS]
    return KIB * sum(size for region, size in REGIONS[: names.index(name)])


def tile_list_inlining_adviser_kernel(
    tc, tab_words, tab_scales, offs, pos1, tab2_words, tab2_scales, offs2, w1_words, w1_scales,
    b1, w2, w3, w4_words, w4_scales, by, gy, out_0, out_1, out_2,
):
    nc = tc.nc
    with ExitStack() as ctx:
        keep = ctx.enter_context(tc.tile_pool(name="keep", bufs=1))
        stage = ctx.enter_context(tc.tile_pool(name="stage", bufs=1))
        psum = ctx.enter_context(tc.psum_pool(name="psum", bufs=1))

        def psum_bank(shape, index):
            return psum.tile(shape, F32, name="bank%d" % index)

        def held(shape, dtype, name, on=None, kib=0):
            if on is None:
                return keep.tile(shape, dtype, name=name, align_bytes=64)
            offset = region_start(on) + KIB * kib
            return stage.tile(shape, dtype, name=name, align_bytes=64, offset=offset)

        def load_scale_rows(scale_tile, scales):
            passes = scales.shape[0]
            for quad in range(4):
                nc.sync.dma_start(
                    out=scale_tile[32 * quad : 32 * quad + 4 * passes, :].bitcast(I32),
                    in_=scales[:, 4 * quad : 4 * quad + 4, :].bitcast(I32),
                )

        def words_view(words_pass):
            return words_pass.rearrange("p t i -> p (t i)").bitcast(I32)

        offs_sb = held([P, S // 16], U16, "offs_sb")
        offs2_sb = held([P, M // 16], U16, "offs2_sb")
        pos_sb = held([P, M // 16], U16, "pos_sb")
        w1_w = held([P, H // 2], I32, "w1_w")
        w1_s = held([P, H], U8, "w1_s")
        tab_w = held([P, T], I32, "tab_w")
        tab_s = held([P, T], U8, "tab_s")
        tab2_s = held([P, T2], U8, "tab2_s")
        tab2_w = [held([P, T2], I32, "tab2_w%d" % a) for a in range(A)]
        w4_w = held([P, A, N], I32, "w4_w")
        w4_s = held([P, N], U8, "w4_s")
        by_sb = held([P, 4], F32, "by_sb")
        gy_sb = held([P, 4], F32, "gy_sb")
        bias1 = held([P, G, 16], F32, "bias1")
        nc.gpsimd.memset(tab_s[:].bitcast(I32), 0)
        for scale_tile in (w1_s, tab2_s, w4_s):
            nc.vector.memset(scale_tile[:].bitcast(I32), 0)

        b1_view = b1.rearrange("(g u k) -> u g k", g=G, k=16)

        def load_bias1(s, queue):
            queue.dma_start(out=bias1[s:P:4, :, 0:13], in_=b1_view[:, :, s : s + 13])

        def load_w2_columns(name, a, first, count):
            raw = held([P, 4, count], F32, name + "_raw", name, 3 if name == "w2_11" else 0)
            rows = w2[PASS * a : PASS * (a + 1), first : first + count]
            nc.sync.dma_start(out=raw[:], in_=rows.rearrange("(p j) c -> p j c", j=4))
            return raw

        def load_w2(g, a):
            return load_w2_columns("w2_%d%d" % (g, a), a, PASS * g, PASS)

        def load_w3(g):
            raw = held([P, 4, N], F32, "w3_raw%d" % g, "w3_%d" % g)
            rows = w3[PASS * g : PASS * (g + 1), :].rearrange("(u j s) n -> j u s n", j=4, s=4)
            for j in range(4):
                nc.sync.dma_start(out=raw[:, j, :], in_=rows[j])
            return raw

        nc.sync.dma_start(out=w1_w[:], in_=w1_words[0].bitcast(I32))
        nc.sync.dma_start(offs_sb[:], offs)
        nc.sync.dma_start(offs2_sb[:], offs2)
        load_scale_rows(tab_s, tab_scales)
        nc.sync.dma_start(out=tab_w[:], in_=words_view(tab_words[0]))
        load_scale_rows(w1_s, w1_scales)
        first_piece = [load_w2_columns("half0", 0, 0, PASS // 2)]
        load_bias1(0, nc.sync)
        for s in range(1, 4):
            load_bias1(s, nc.gpsimd)
        load_scale_rows(tab2_s, tab2_scales)
        nc.sync.dma_start(pos_sb[:], pos1)
        nc.sync.dma_start(out=tab2_w[0][:], in_=words_view(tab2_words[0]))
        first_piece.append(load_w2_columns("half1", 0, PASS // 2, PASS // 2))
        nc.sync.dma_start(out=tab2_w[1][:], in_=words_view(tab2_words[1]))
        w2_raw = {(0, 1): load_w2(0, 1)}
        load_scale_rows(w4_s, w4_scales)
        w2_raw[(1, 0)] = load_w2(1, 0)
        w3_raw = {0: load_w3(0)}
        w2_raw[(1, 1)] = load_w2(1, 1)
        nc.sync.dma_start(out=gy_sb[:], in_=gy.rearrange("(p t) -> p t", t=4))
        nc.sync.dma_start(out=by_sb[:], in_=by.rearrange("(p t) -> p t", t=4))
        nc.sync.dma_start(out=w4_w[:], in_=w4_words.rearrange("a p c i -> p a (c i)").bitcast(I32))
        for a in range(A):
            w2_raw[(2, a)] = load_w2(2, a)
        for g in (2, 1):
            w3_raw[g] = load_w3(g)

        v_s = held([P, S], U8, "v_s")
        v_w = [held([P, PASS], U32, "v_w%d" % c) for c in range(2)]
        nc.vector.tensor_copy(v_s[:], tab_s[:].indirect(offs_sb[:]))
        nc.vector.tensor_copy(v_w[0][:], tab_w[:].bitcast(U32).indirect(offs_sb[:, 0:32]))
        w1_wd = held([P, H // 2], I32, "w1_wd")
        w1_sd = held([P, H], U8, "w1_sd")
        nc.scalar.copy(
            out=w1_wd[:].bitcast(U32).rearrange("p (g t u i) -> p t g u i", g=G, t=4, i=2),
            in_=w1_w[:].bitcast(U32).rearrange("p (g u t i) -> p t g u i", g=G, t=4, i=2),
        )
        nc.scalar.copy(
            out=w1_sd[:].bitcast(U32).rearrange("p (g t c i) -> p c g t i", g=G, t=4, i=4),
            in_=w1_s[:].bitcast(U32).rearrange("p (g c i t) -> p c g t i", g=G, t=4, i=4),
        )
        nc.vector.tensor_copy(v_w[1][:], tab_w[:].bitcast(U32).indirect(offs_sb[:, 32:64]))
        v2_s = held([P, M], U8, "v2_s")
        nc.vector.tensor_copy(v2_s[:], tab2_s[:].indirect(offs2_sb[:]))

        places = {9: ("w2_10", 0), 10: ("w2_10", 4), 11: ("w2_11", 10)}
        h = [held([P, S], F32, "h%d" % n, *places.get(n, ("h%d" % n, 0))) for n in range(4 * G)]

        def scope_half(n, c, bank_index):
            g, t = ORDER[n // 4], n % 4
            i = 4 * g + t
            bank = psum_bank([P, PASS], bank_index)
            nc.tensor.matmul_mx(
                out=bank[:],
                lhsT=w1_wd[:, 64 * i : 64 * (i + 1)].bitcast(U8).bitcast(FP4X4),
                lhsT_scale=w1_sd[:, P * i : P * (i + 1)],
                rhs=v_w[c][:].bitcast(FP8X4),
                rhs_scale=v_s[:, PASS * c : PASS * (c + 1)],
                start=True,
                stop=True,
            )
            nc.scalar.activation(
                h[n][:, PASS * c : PASS * (c + 1)], bank[:], IDENT,
                bias=bias1[:, g, 4 * t : 4 * t + 1],
            )

        def scope_slice(n, first_bank):
            for c in range(2):
                scope_half(n, c, first_bank + c)

        def pick_whole(n, picked):
            nc.vector.tensor_copy(picked[:, n % 4, :], h[n][:].indirect(pos_sb[:]))

        def pick_three_quarters(n, picked):
            nc.vector.tensor_copy(picked[:, :, n % 4, :], h[n][:].indirect(pos_sb[:, 0:24]))

        def pick_last_quarter(n, picked):
            nc.vector.tensor_copy(picked[:, n % 4, :], h[n][:].indirect(pos_sb[:, 24:32]))

        def gather_calls(a):
            words = held([P, M], U32, "v2_w%d" % a)
            nc.vector.tensor_copy(words[:], tab2_w[a][:].bitcast(U32).indirect(offs2_sb[:]))
            return words

        def round_w2(raw, rounded, slices):
            nc.scalar.copy(
                out=rounded, in_=raw[:].rearrange("p j (u t s) -> p t u j s", t=4, s=4)[:, slices]
            )

        def dealt(tile_ap, slices):
            return tile_ap.rearrange("p (t u s j) -> p t u j s", t=slices, s=4, j=4)

        def round_w2_beside(raw, rounded, first):
            source = raw[:].rearrange("p j (u t s) -> p t u s j", t=4, s=4)
            for i in range(rounded.shape[1] // PASS):
                nc.gpsimd.tensor_scalar(
                    rounded[:, PASS * i : PASS * (i + 1)].rearrange("p (u s j) -> p u s j", s=4, j=4),
                    source[:, first + i], 1.0, 0.0, MULT, ADD,
                )

        def round_w3_beside(g, rounded, first):
            slices = rounded.shape[1] // N
            nc.gpsimd.tensor_scalar(
                rounded[:].rearrange("p (t m j) -> p m t j", t=slices, j=4),
                w3_raw[g][:].rearrange("p j (m t) -> p m t j", t=4)[:, :, first : first + slices],
                1.0, 0.0, MULT, ADD,
            )

        def round_w3_pair(g, pair, rounded):
            source = w3_raw[g][:].rearrange("p j (m t) -> p m j t", t=4)
            nc.scalar.copy(
                out=rounded.rearrange("p (t m j) -> p m j t", t=2, j=4),
                in_=source[:, :, :, 2 * pair : 2 * pair + 2],
            )

        def mx_tiles(name, on=None, kib=0):
            return held([P, PASS], U32, name + "_c", on, kib), held([P, PASS], U8, name + "_s")

        def quantise(operand, cols, rounded):
            codes, scales = operand
            nc.vector.quantize_mx(
                out=codes[:, cols].bitcast(FP8X4), scales=scales[:, cols], in_=rounded
            )

        def quantised(name, rounded, on=None, kib=0):
            operand = mx_tiles(name, on, kib)
            quantise(operand, slice(0, PASS), rounded[:])
            return operand

        def quantised_pairs(name, lower, upper, on=None, kib=0):
            operand = mx_tiles(name, on, kib)
            quantise(operand, slice(2 * P, 4 * P), upper[:])
            quantise(operand, slice(0, 2 * P), lower[:])
            return operand

        def prepare_w2(g, a, on, codes_on=None, codes_kib=0):
            rounded = held([P, 4 * PASS], BF16, "w2_bf%d%d" % (g, a), on)
            round_w2(w2_raw[(g, a)], dealt(rounded[:], 4), slice(0, 4))
            return quantised("w2_%d%d" % (g, a), rounded, codes_on, codes_kib)

        def call_projection(w2_pass, q):
            bank = psum_bank([P, 4, P], Q + q)
            cols = slice(P * q, P * (q + 1))
            for a in range(A):
                codes, scales = w2_pass[a]
                for t in range(4):
                    nc.tensor.matmul_mx(
                        out=bank[:, t, :],
                        lhsT=codes[:, P * t : P * (t + 1)].bitcast(FP8X4),
                        lhsT_scale=scales[:, P * t : P * (t + 1)],
                        rhs=v2_w[a][:, cols].bitcast(FP8X4),
                        rhs_scale=v2_s[4 * a : P, cols],
                        start=(a == 0 and t == 0),
                        stop=(a == A - 1 and t == 3),
                    )
            return bank

        def multiply(z_rounded, scopes, bank):
            nc.vector.tensor_tensor(
                z_rounded.rearrange("p (c i t) -> p c t i", i=2, t=4),
                scopes.rearrange("p t (c i) -> p c t i", i=2),
                bank[:].rearrange("p t (c i) -> p c t i", i=2),
                MULT,
            )

        def shared_w2(g, a, beside, first, on, kib, codes_on=None, codes_kib=0):
            rounded = held([P, first * PASS], BF16, "w2_bf%d%d" % (g, a), on, kib)
            round_w2(w2_raw[(g, a)], dealt(rounded[:], first), slice(0, first))
            operand = mx_tiles("w2_%d%d" % (g, a), codes_on, codes_kib)
            quantise(operand, slice(first * P, 4 * P), beside[:])
            quantise(operand, slice(0, first * P), rounded[:])
            return operand

        def products(zb, first_three, last, b_banks, quarters):
            for q in quarters:
                scopes = first_three[:, q] if q < 3 else last[:]
                multiply(zb[:, PASS * q : PASS * (q + 1)], scopes, b_banks[q])

        w2_bf00 = held([P, 4 * PASS], BF16, "w2_bf00")
        first_units = [slice(0, UNITS // 2), slice(UNITS // 2, UNITS)]
        round_w2(first_piece[0], dealt(w2_bf00[:], 4)[:, :, first_units[0]], slice(0, 4))
        picked2 = held([P, 4, M], F32, "picked2")
        for c in range(2):
            for n in range(2):
                scope_half(n, c, 2 * n + c)
        for n in range(2):
            pick_whole(n, picked2)
        v2_w = [gather_calls(a) for a in range(A)]
        round_w2(first_piece[1], dealt(w2_bf00[:], 4)[:, :, first_units[1]], slice(0, 4))
        w2q = [quantised("w2_00", w2_bf00)]
        for n in range(2, 4):
            scope_slice(n, 2 * n)
            pick_whole(n, picked2)

        w2_bf01 = held([P, 4 * PASS], BF16, "w2_bf01", "h3")
        round_w2_beside(w2_raw[(0, 1)], w2_bf01, 0)
        picked0 = held([P, 3, 4, P], F32, "picked0", "picked0")
        picked1 = held([P, 3, 4, P], F32, "picked1", "picked1")
        for n in range(4, 9):
            scope_slice(n, 2 * (n % 2))
            pick_three_quarters(n, picked0 if n < 8 else picked1)
        w2q.append(quantised("w2_01", w2_bf01))
        w4_sd = held([P, N], U8, "w4_sd", "w2_01", 2)
        nc.vector.tensor_copy(
            out=w4_sd[:].rearrange("p (t c i) -> p c t i", t=4, i=16),
            in_=w4_s[:].rearrange("p (c i t) -> p c t i", t=4, i=16),
        )
        last0 = held([P, 4, P], F32, "last0", "w2_01")
        for n in range(4, 8):
            pick_last_quarter(n, last0)
        b_banks = [call_projection(w2q, q) for q in range(Q)]
        w3_pairs = [held([P, 2 * N], BF16, "w3_bf0%d" % i, "h6", 2 * i) for i in range(2)]
        for i in range(2):
            round_w3_beside(0, w3_pairs[i], 2 * i)
        zb0 = held([P, 4 * M], BF16, "zb0", "h4")
        products(zb0, picked0, last0, b_banks, range(Q))

        w2_bf10 = held([P, 4 * PASS], BF16, "w2_bf10", "half0")
        round_w2(w2_raw[(1, 0)], dealt(w2_bf10[:], 4), slice(0, 4))
        for n in range(9, 11):
            scope_slice(n, 2 * (n % 2))
            pick_three_quarters(n, picked1)
        w2_bf11 = held([P, 4 * PASS], BF16, "w2_bf11", "h1")
        round_w2(w2_raw[(1, 1)], dealt(w2_bf11[:], 4), slice(0, 4))
        w2q = [quantised("w2_10", w2_bf10, "w2_11", 4)]
        z = [quantised("z0", zb0, "w2_11", 6)]
        w2q.append(quantised("w2_11", w2_bf11))
        w3q = {0: quantised_pairs("w3_0", w3_pairs[0], w3_pairs[1], "w2_11", 8)}
        scope_slice(11, 2)
        last1 = held([P, 4, P], F32, "last1", "h1")
        for n in range(8, 12):
            pick_last_quarter(n, last1)
        pick_three_quarters(11, picked1)
        b_banks = {q: call_projection(w2q, q) for q in (3, 0, 1, 2)}
        beside = held([P, PASS], BF16, "w2_beside21", "w2_10", 6)
        round_w2_beside(w2_raw[(2, 1)], beside, 3)
        w3_bf2_upper = held([P, 2 * N], BF16, "w3_bf2u", "w2_10", 4)
        round_w3_beside(2, w3_bf2_upper, 2)
        zb1 = held([P, 4 * M], BF16, "zb1", "h8")
        products(zb1, picked1, last1, b_banks, (3, 0, 1, 2))

        w4_wd = held([P, A, N], I32, "w4_wd", "w2_11")
        nc.scalar.copy(
            out=w4_wd[:].bitcast(U32).rearrange("p a (t c i) -> p a c t i", t=4, i=4),
            in_=w4_w[:].bitcast(U32).rearrange("p a (c i t) -> p a c t i", t=4, i=4),
        )
        w2q = [prepare_w2(2, 0, "h2", "picked1"), shared_w2(2, 1, beside, 3, "w2_20", 0, "picked1", 2)]
        b_banks = [call_projection(w2q, q) for q in range(Q)]
        z.append(quantised("z1", zb1))
        gby = held([P, 4], F32, "gby", "h8")
        nc.vector.tensor_tensor(gby[:], by_sb[:], gy_sb[:], MULT)
        w3_bf2_lower = held([P, 2 * N], BF16, "w3_bf2l", "w2_21")
        round_w3_pair(2, 0, w3_bf2_lower[:])
        w3q[2] = quantised_pairs("w3_2", w3_bf2_lower, w3_bf2_upper, "picked1", 4)

        banks = [psum_bank([P, 4, P], q) for q in range(Q)]

        def out_passes(q, weight, moving, row=0, first=False, final=False):
            cols = slice(P * q, P * (q + 1))
            for t in range(4):
                nc.tensor.matmul_mx(
                    out=banks[q][:, t, :],
                    lhsT=weight[0][:, P * t : P * (t + 1)].bitcast(FP8X4),
                    lhsT_scale=weight[1][row:P, P * t : P * (t + 1)],
                    rhs=moving[0][:, cols].bitcast(FP8X4),
                    rhs_scale=moving[1][row:P, cols],
                    start=(first and t == 0),
                    stop=(final and t == 3),
                )

        for q in range(Q):
            for a in range(A):
                out_passes(q, (w4_wd[:, a, :], w4_sd), (v2_w[a], v2_s), 4 * a, first=(a == 0))
            out_passes(q, w3q[0], z[0])

        z.append(mx_tiles("z2"))

        def half_of_pass_2(half, on):
            zb_half = held([P, 2 * M], BF16, "zb2%d" % half, on)
            for i in range(2):
                q = 2 * half + i
                scopes = picked2[:, :, P * q : P * (q + 1)]
                multiply(zb_half[:, PASS * i : PASS * (i + 1)], scopes, b_banks[q])
            for i in range(2):
                q = 2 * half + i
                quantise(z[2], slice(P * q, P * (q + 1)), zb_half[:, PASS * i : PASS * (i + 1)])

        w3_bf1 = held([P, 4 * N], BF16, "w3_bf1", "w2_20", 4)
        for pair in range(2):
            round_w3_pair(1, pair, w3_bf1[:, 2 * N * pair : 2 * N * (pair + 1)])
        half_of_pass_2(0, "w3_2")
        for q in range(2):
            out_passes(q, w3q[2], z[2])
        w3q[1] = quantised("w3_1", w3_bf1)
        for q in range(Q):
            out_passes(q, w3q[1], z[1], final=(q < 2))
        half_of_pass_2(1, "w3_1")
        for q in range(2, Q):
            out_passes(q, w3q[2], z[2], final=True)

        y_s = held([P, M], U8, "y_s")
        y_rows = out_0.rearrange("(p t) m -> p t m", t=4)

        def empty_bank(q):
            y = held([P, 4, P], F32, "y%d" % q)
            for t in range(4):
                nc.scalar.activation(
                    y[:, t, :], banks[q][:, t, :], IDENT,
                    bias=gby[:, t : t + 1], scale=gy_sb[:, t : t + 1],
                )
            nc.sync.dma_start(out=y_rows[:, :, P * q : P * (q + 1)], in_=y[:])
            return y

        def round_y(q, y):
            yb = held([P, PASS], BF16, "yb%d" % q)
            nc.vector.tensor_copy(
                out=yb[:].rearrange("p (c i t) -> p c t i", i=2, t=4),
                in_=y[:].rearrange("p t (c i) -> p c t i", i=2),
            )
            return yb

        for half in range(2):
            quarters = (2 * half, 2 * half + 1)
            y = [empty_bank(q) for q in quarters]
            yb = [round_y(quarters[i], y[i]) for i in range(2)]
            y_c = held([P, M // 2], U32, "y_c%d" % half, "h8" if half else None)
            for i in range(2):
                nc.vector.quantize_mx(
                    out=y_c[:, P * i : P * (i + 1)].bitcast(FP8X4),
                    scales=y_s[:, P * quarters[i] : P * (quarters[i] + 1)],
                    in_=yb[i][:],
                )
            nc.sync.dma_start(
                out=words_view(out_1[0])[:, M // 2 * half : M // 2 * (half + 1)],
                in_=y_c[:].bitcast(I32),
            )
        for quad in range(4):
            queue = nc.scalar if quad % 2 else nc.sync
            queue.dma_start(
                out=out_2[0, 4 * quad : 4 * quad + 4, :].bitcast(I32),
                in_=y_s[32 * quad : 32 * quad + 4, :].bitcast(I32),
            )
